import numpy as np, ml_dtypes
CORES = [2,6,10,14,18,22,26,30]
N = 8
BF = ml_dtypes.bfloat16
V, D, L, RO, HOP = 2048, 8, 256, 3, 3
def meet(rng, n, rest):
    p = np.argsort(rng.random((N, 8, n, V)), axis=-1); h = np.zeros_like(p)
    np.put_along_axis(h, p[..., 0::2], p[..., 1::2], 3); np.put_along_axis(h, p[..., 1::2], p[..., 0::2], 3)
    o = np.concatenate([h, rest], axis=2)
    return np.ascontiguousarray(np.take_along_axis(o, np.argsort(rng.random(o.shape), axis=2), 2))
def court(rng, lo, hi):
    c = rng.integers(0, V, (N, 8, V))
    for r in range(N):
        for g in range(8):
            h = int(rng.integers(3, 10)); chief = rng.permutation(V)[:h]; w = np.add.accumulate(np.exp2(-(0.1 + rng.random()) * np.arange(h)))
            j = np.minimum(np.searchsorted(w, rng.random(V) * w[-1], side="right"), h - 1)
            c[r, g] = np.where(rng.random(V) < lo + (hi - lo) * rng.random(), chief[j], c[r, g])
    return c
def hubs(rng, og, n):
    z = rng.permutation(V)[:RO * n]; vv = np.concatenate([D * rng.permutation(L)[:16 * n] + t for t in range(RO)]).reshape(RO * n, 16)
    og[rng.integers(0, 16, vv.shape), vv] = z[:, None]; og[:, z] = vv.T
    return z
def pack(o, x, c):
    return {"hol": np.ascontiguousarray(o.reshape(N, 128, V)).astype(np.int32), "sha": np.ascontiguousarray(x.reshape(N, 128, V)).astype(np.float32).astype(BF), "ctl": c.astype(np.int32)}
def setup_inputs(rng):
    o = meet(rng, 8, rng.integers(0, V, (N, 8, 8, V))); c = court(rng, 0.85, 0.95); x = rng.integers(0, 16, (N, 8, 16, V))
    for r in range(N):
        for g in range(8): hubs(rng, o[r, g], 2)
    return pack(o, x, c)
def setup_inputs_spread(rng):
    e = rng.integers(1, 7, (N, 8, 1, 1)); o = meet(rng, 8, np.minimum((V * rng.random((N, 8, 8, V)) ** e).astype(np.int64), V - 1))
    c = court(rng, 0.5, 1.0); q = np.minimum((V * rng.random((N, 8, V)) ** rng.integers(1, 9, (N, 8, 1))).astype(np.int64), V - 1)
    c = np.where(rng.random((N, 8, V)) < 0.15, q, c)
    x = np.minimum((rng.random((N, 8, 16, V)) * rng.choice(np.array([1, 2, 3, 6, 11, 16]), (N, 8, 1, V))).astype(np.int64), 15)
    return pack(o, x, c)
def setup_inputs_ends(rng):
    top = V - 1; p = rng.choice(np.array([0.15, 0.5, 0.85]), (N, 8, 1, V)); odd = np.arange(16) % 2
    o = meet(rng, 6, np.where(rng.random((N, 8, 10, V)) < p, top, 0)); c = top * rng.integers(0, 2, (N, 8, V)); kind = rng.random((N, 8, 1, V))
    x = 15 * np.where(kind < 0.45, 1, np.where(kind < 0.55, 0, rng.integers(0, 2, (N, 8, 16, V))))
    for r in range(N):
        for g in range(8):
            og, xg, cg = o[r, g], x[r, g], c[r, g]
            if g % 4 == 1: cg[0] = top; cg[top] = 0
            elif g % 4 != 3 or g == 7:
                cg[0] = 0; cg[top] = top; xg[:, 0] = 15; xg[:, top] = 15; og[:, 0] = top * odd
                for t in range(RO):
                    v = D * (L - 1) + t; og[:, v] = top; xg[:, v] = 15
                    v = D * (L - 2) + t; og[:, v] = top * odd; xg[:, v] = 15
                    v = D + t; og[:, v] = top * (1 - odd); xg[:, v] = 15
                    xg[:, 2 * D + t] = 0
                    v = D * (L - 3) + t; z = D * (L - 1 - 2 * t) + D - 2; og[:, v] = top; xg[:, v] = 15
                    for k, a in ((14, z), (15, z - D)): og[k, v] = a; og[15, a] = v; xg[:, a] = 0; cg[a] = 0
    return pack(o, x, c)
def setup_inputs_corners(rng):
    o = meet(rng, 8, rng.integers(0, V, (N, 8, 8, V))); c = court(rng, 0.8, 1.0); x = rng.integers(0, 16, (N, 8, 16, V)); own = np.arange(V)
    kind = rng.integers(0, 8, (N, 8, 1, V)); x = np.where(kind == 0, 0, np.where(kind == 1, 15, x))
    for r in range(N):
        mo, ho = rng.permutation(8), rng.permutation(8)
        for g in range(8):
            og = o[r, g]; m, h = int(mo[g]), int(ho[g])
            if m == 0: c[r, g] = own
            elif m == 1: c[r, g] = 0
            elif m == 2: c[r, g] = V - 1
            elif m == 3: c[r, g] = (own + 1) % V
            elif m == 4: c[r, g] = V - 1 - own
            elif m == 5: c[r, g] = np.choose(rng.integers(0, 3, V), [np.zeros_like(own), own, np.full_like(own, V - 1)])
            if h in (0, 4): og[rng.integers(0, 16, V), own] = own
            elif h == 1: one = rng.random(V) < 0.3; og[:, one] = og[:1, one]
            elif h == 2: og[:] = np.choose(rng.integers(0, 3, (16, V)), [np.zeros((16, V), np.int64), np.broadcast_to(own, (16, V)), np.full((16, V), V - 1)])
            elif h == 3: og[3] = (own + 1) % V; og[12] = (own - 1) % V
    return pack(o, x, c)
def setup_inputs_ties(rng):
    o = meet(rng, 8, rng.integers(0, V, (N, 8, 8, V))); x = rng.integers(14, 16, (N, 8, 16, V)); c = np.zeros((N, 8, V), np.int64); idle = np.flatnonzero(np.arange(V) % D >= RO)
    for g in range(8):
        f = rng.permutation(idle)[:3]; f = f[:2 + g % 2]
        for r in range(N):
            c[r, g] = f[rng.integers(0, 2, V)]
            if g % 2: c[r, g] = np.where(rng.random(V) < 0.1, f[2], c[r, g])
            c[r, g, f] = f
            if g % 4 == 1: x[r, g] = 15
            elif g % 4 == 2:
                n = 9 if g == 2 else int(rng.integers(8, 11)); x[r, g] = (rng.permutation(16) < n).astype(np.int64)[:, None] * rng.integers(1, 16, (16, 1))
            elif g % 4 == 3: x[r, g] -= 7
    return pack(o, x, c)
def setup_inputs_rush(rng):
    o = meet(rng, 8, rng.integers(0, V, (N, 8, 8, V))); x = rng.integers(6, 16, (N, 8, 16, V)); low = rng.integers(0, 4, (N, 8, 16, V)); c = np.zeros((N, 8, V), np.int64)
    act, idle = np.flatnonzero(np.arange(V) % D < RO), np.flatnonzero(np.arange(V) % D >= RO)
    for g in range(8):
        f = rng.permutation(idle)[:2]; tp = {5: 0, 7: RO - 1}.get(g, -1)
        if tp >= 0: f[0] = D * int(rng.integers(0, L)) + tp
        for r in range(N):
            og = o[r, g]; k = rng.integers(0, 16, V); c[r, g] = np.where(rng.random(V) < 0.8, f[0], f[1]); z = act
            if g % 4 == 0: z = hubs(rng, og, L // 16)
            elif g % 4 == 1:
                for t in range(RO):
                    q = D * rng.permutation(L) + t; a, b = q[0::2], q[1::2]; og[k[a], a] = b; og[k[b], b] = a
            elif g % 4 == 2:
                og[k[act], act] = act; h = act[rng.random(len(act)) < 0.5]; og[(k[h] + 5) % 16, h] = h
            else:
                n = min(len(act), len(idle)); a, z = rng.permutation(act)[:n], rng.permutation(idle)[:n]
                for j in range(5): og[(k[a] + j) % 16, a] = z; og[(k[z] + j) % 16, z] = a
            c[r, g, z] = f[1]; x[r, g][:, z] = low[r, g][:, z]
            c[r, g, f] = f; x[r, g][:, f[0]] = 15
            if tp >= 0:
                h, y = [int(e) for e in rng.permutation(idle[idle != f[1]])[:2]]; i1, i2 = [int(e) for e in rng.permutation(16)[:2]]
                v = D * ((int(f[0]) // D + 1 + int(rng.integers(0, L - 1))) % L) + tp
                og[:, v] = h; og[i1, v] = f[0]; og[i2, v] = y; og[int(rng.integers(0, 16)), y] = v
                og[:, f[0]] = h; og[int(rng.integers(0, 16)), f[0]] = v
                c[r, g, h] = f[0]; c[r, g, v] = f[1]; c[r, g, y] = f[1]; x[r, g][:, h] = 15; x[r, g][:, v] = rng.integers(1, 4, 16)
    return pack(o, x, c)
def check_inputs(d):
    bad = []
    for k, hi in (("hol", V - 1), ("sha", 15), ("ctl", V - 1)):
        v = np.asarray(d[k]).astype(np.float64)
        if not (np.min(v) >= 0 and np.max(v) <= hi): bad.append("range of " + k)
        elif np.any(v != np.floor(v)): bad.append("whole numbers of " + k)
    return bad
def reference(hol, sha, ctl):
    o = hol.astype(np.int64).reshape(N, 8, 16, V); x = sha.astype(np.float32).astype(np.int64).reshape(N, 8, 16, V); c = ctl.astype(np.int64)
    last = np.zeros(N, np.int64)
    for t in range(RO):
        d = 1 + t % (N - 1); vs = D * np.arange(L) + t
        no, nc, wins = [], [], []
        for r in range(N):
            a = o[r][:, :, vs]; af = a.reshape(8, 16 * L); cf = af
            for h in range(HOP): cf = np.take_along_axis(c[(r + h * d) % N], cf, 1)
            ck = cf.reshape(8, 16, L)
            xk = np.take_along_axis(x[r], af[:, None, :], 2).reshape(8, 16, 16, L); xv = x[r][:, :, vs]
            m = np.add.reduce(np.minimum(xk, xv[:, :, None, :]), axis=1)
            pool = np.add.reduce(np.where(ck[:, :, None, :] == ck[:, None, :, :], m[:, None, :, :], 0), axis=2)
            kb = np.argmax(pool, axis=1)
            b = np.take_along_axis(ck, kb[:, None, :], 1)[:, 0]
            mine = ck == b[:, None, :]
            part = np.add.reduce(np.where(mine[:, None, :, :], xk, 0), axis=2); full = np.add.reduce(xk, axis=2)
            win = np.add.reduce((2 * part > full).astype(np.int64), axis=1) >= 9 + (last[r] & 1)
            ok = np.take_along_axis(o[r], af[:, None, :], 2).reshape(8, 16, 16, L)
            stake = np.any(ok == vs, axis=1)
            xb = np.take_along_axis(x[r], b[:, None, :], 2)
            far = np.where(stake & ~mine, np.add.reduce(np.abs(xk - xb[:, :, None, :]), axis=1), -1)
            ks = np.argmax(far, axis=1); sells = win & (np.max(far, axis=1) >= 0)
            goal = np.take_along_axis(a, ks[:, None, :], 1)[:, 0]; cs = np.take_along_axis(ck, ks[:, None, :], 1)[:, 0]
            on = o[r] + 0; cn = c[r] + 0
            for g in range(8):
                ln = np.flatnonzero(sells[g]); tg, first = np.unique(goal[g, ln], return_index=True); w = ln[first]
                col = o[r, g][:, tg]; on[g][:, tg] = np.where(col == vs[w], cs[g, w], col)
                on[g, ks[g, ln], vs[ln]] = b[g, ln]
            cn[:, vs] = np.where(win, b, vs)
            no.append(on); nc.append(cn); wins.append(np.add.reduce(win.astype(np.int64).reshape(-1)))
        o = np.stack(no); c = np.stack(nc); last = np.array(wins, np.int64)
    return {"yo": o.reshape(N, 128, V).astype(np.float32), "yc": c.astype(np.float32)}

@@ -1,0 +1,713 @@
+import numpy as np
+from concourse.mybir import AluOpType as A, ActivationFunctionType as F, AxisListType
+from concourse.bass import DstId, RemoteDMATransfer
+
+V, D, L, RO, N = 2048, 8, 256, 3, 8
+DEL = (1, 2, 4, 3, 6)
+NEXT = {0: (2, 4, 3, 6), 1: (3, 6)}
+NV = {"min": 8, "win": 5, "far": 6, "d": 128, "sk": 2, "sk2": 0, "c0": 5, "c1": 0}
+NA = 1
+S_ = np.s_
+
+_bf, _f, _i, _u = "bfloat16", "float32", "int32", "uint16"
+_shapes = {
+    "O": ([2304], _f), "holI": ([2048], _i), "X": ([2048], _bf), "raw": ([128], _i), "rawd": ([128], _f),
+    "HL": ([256], _bf), "VV": ([4096], _f), "xk": ([4096], _bf), "sk": ([4096], _bf), "dR": ([4096], _bf),
+    "mR": ([4096], _bf), "pR": ([4096], _bf), "T1": ([2048], _bf), "DT": ([2048], _bf), "EK": ([2048], _bf),
+    "E3": ([16, 272], _bf), "ycS": ([2048], _f),
+    "EQ": ([128, 16], _bf), "PA": ([128, 16], _bf), "PB": ([80, 32], _bf),
+    "off0": ([128], _u), "off1": ([128], _u), "a16": ([256], _u), "bo": ([16], _u), "go": ([16], _u), "so": ([16], _u),
+    "gSu": ([256], _u), "aD": ([256], _f), "cd": ([16, 24], _f), "md": ([16, 24], _bf), "cS": ([256], _f),
+    "bU": ([256], _f), "keyS": ([256], _f), "mxS": ([256], _f), "keyK": ([256], _f), "mx16": ([128], _f), "ohc": ([256], _f),
+    "cK": ([256], _f), "mine": ([256], _bf), "w1": ([256], _bf), "w16": ([256], _bf), "bw": ([256], _f), "bws": ([256], _f),
+    "xb": ([256], _bf), "gt": ([256], _bf), "wl": ([256], _bf), "winG": ([256], _f), "st": ([256], _bf), "el": ([256], _f), "elw": ([256], _f),
+    "FK": ([256], _f), "FKk": ([256], _f), "fS": ([256], _f), "ga": ([256], _f), "ca": ([256], _f), "ns": ([256], _f),
+    "sb": ([256], _f), "gw": ([256], _f), "gws": ([256], _f), "OG": ([256], _f), "dw": ([256], _f), "dws": ([256], _f),
+    "t1": ([16], _f), "t2": ([16], _f), "eqv": ([256], _f), "dd": ([256], _f), "tt": ([256], _f), "oc": ([256], _f),
+    "hR": ([256], _bf), "hU": ([256], _f), "vR": ([256], _bf), "vW": ([256], _bf), "vU": ([256], _f),
+    "cnw": ([1], _f), "cni": ([1], _i), "cnp": ([1], _i), "Z": ([1], _f),
+    "IF": ([256], _f), "JG": ([256], _f), "JM": ([256], _f), "JM3": ([16, 16], _f), "pi": ([1], _i), "qi": ([1], _i),
+    "cols": ([16], _f), "I": ([128], _bf), "I16": ([128], _bf), "I256": ([128], _bf), "nI": ([128], _bf), "Iw": ([128], _bf),
+    "I32": ([128], _f), "Ip32": ([128], _f), "Blk": ([128], _bf), "Blk32": ([128], _f), "BlkC": ([128], _bf), "B4096": ([128], _bf), "BlkV": ([128], _bf),
+    "fm": ([16, 8], _bf), "Blk8": ([8], _bf), "Blk8c": ([8], _bf), "B8s": ([8], _bf), "B816": ([8], _bf), "B8n32": ([8], _bf),
+    "B8h": ([8], _bf), "B8nh": ([8], _bf), "KSc": ([144], _bf),
+    "km": ([16], _f), "maskW": ([256], _f), "rst": ([256], _f), "tri": ([16, 16], _bf), "E1": ([256], _f), "k15": ([16, 16], _bf),
+    "kc": ([256], _bf), "dumG": ([256], _f), "dumW": ([16], _f), "zer": ([256], _bf), "o16": ([128], _f),
+}
+SCRATCH = {n: ("sbuf", [128] + s, d) for n, (s, d) in _shapes.items()}
+PACK = {n: 256 * j for j, n in enumerate((
+    "aD cS keyS mxS keyK ohc cK bw bws el elw winG FK FKk fS ga ca bU sb gw gws OG dw dws eqv tt hU vU").split())}
+SHAPE = dict(SCRATCH)
+for _n in PACK:
+    del SCRATCH[_n]
+SCRATCH["lanes"] = ("sbuf", [128, 256 * len(PACK)], _f)
+for _d in (0,) + DEL:
+    SCRATCH["tab%d" % _d] = ("sbuf", [128, 2048], _bf)
+for _d in DEL:
+    SCRATCH["la%d" % _d] = ("sbuf", [128, 256], _bf)
+for _t in NEXT:
+    for _d in NEXT[_t]:
+        SCRATCH["lb%d%d" % (_t, _d)] = ("sbuf", [128, 256], _bf)
+for _t in range(RO):
+    SCRATCH["CN%d" % _t] = ("sbuf", [128, 256], _bf)
+    SCRATCH["vHL%d" % _t] = ("sbuf", [128, 256], _bf)
+    SCRATCH["vG%d" % _t] = ("sbuf", [128, 256], _f)
+for _k in range(8):
+    SCRATCH["k%d" % _k] = ("psum", [128, 512] if _k in (0, 7) else [128, 16, 32], _f)
+SHAPE.update(SCRATCH)
+SEMAPHORES = ["qv", "qs", "qp", "qg", "ls"] + ["d%d" % k for k in range(24)] + ["a%d" % d for d in DEL] + ["b%d%d" % (t, d) for t in NEXT for d in NEXT[t]]
+
+
+def b(n, *ix):
+    return (n, (slice(None),) + ix)
+
+
+def bp(n, p, *ix):
+    return (n, (p,) + ix)
+
+
+def ind(w, o):
+    return ("ind", w, o)
+
+
+def rank_program(g, core, T, topo):
+    rank = T.rank_of(core)
+    if rank is None:
+        return
+    eng = {"v": g.vector, "s": g.scalar, "p": g.tensor, "g": g, "y": g.sync}
+    cnt, clk, hist, W, R, cache = {}, {q: {} for q in eng}, {}, {}, {}, {}
+    ndma = [0]
+
+    def ap(x):
+        if x[0] == "ind":
+            return T[x[1][0]][x[1][1]].indirect(T[x[2][0]][x[2][1]])
+        if x[0] in PACK:
+            lo, hi, st = (x[1][1] if len(x[1]) > 1 else slice(None)).indices(256)
+            return T["lanes"][x[1][0], PACK[x[0]] + lo:PACK[x[0]] + hi:st]
+        return T[x[0]][x[1]]
+
+    def parts(xs):
+        out = []
+        for x in xs:
+            if isinstance(x, tuple):
+                out += [x[1], x[2]] if x[0] == "ind" else [x]
+        return out
+
+    def size(n):
+        return int(np.prod(SHAPE[n][1][1:]))
+
+    def cols(x):
+        key = repr(x)
+        if key not in cache:
+            ix = x[1][1:]
+            m = np.arange(size(x[0])).reshape(SHAPE[x[0]][1][1:])
+            cache[key] = m[ix].ravel() if ix else m.ravel()
+        return cache[key]
+
+    def need(q, rd, wr):
+        req = {}
+        own = "q" + q
+
+        def take(tab, x, skip):
+            ps = SHAPE[x[0]][0] == "psum"
+            for s, arr in tab.get(x[0], {}).items():
+                if s == own and skip:
+                    continue
+                n = int(arr.max() if ps and s != own else arr[cols(x)].max())
+                if n > req.get(s, 0):
+                    req[s] = n
+        for x in rd:
+            take(W, x, False)
+            if SHAPE[x[0]][0] == "psum":
+                take(R, x, True)
+        for x in wr:
+            take(W, x, True)
+            take(R, x, True)
+        return req
+
+    def waits(q, req):
+        for s, n in sorted(req.items(), key=lambda z: -len(hist.get(z, ()))):
+            if clk[q].get(s, 0) < n:
+                eng[q].wait_ge(T.sem[s], n)
+                clk[q][s] = n
+                for s2, n2 in hist.get((s, n), {}).items():
+                    clk[q][s2] = max(clk[q].get(s2, 0), n2)
+
+    def note(tab, x, s, n):
+        d = tab.setdefault(x[0], {})
+        if s not in d:
+            d[s] = np.zeros(size(x[0]), np.int64)
+        d[s][cols(x)] = n
+
+    def op(q, fn, rd, wr, sem=None, amt=1):
+        rd, wr = parts(rd), parts(wr)
+        waits(q, need(q, rd, wr))
+        s = sem or "q" + q
+        cnt[s] = cnt.get(s, 0) + amt
+        n = cnt[s]
+        fn().then_inc(T.sem[s], amt)
+        hist[(s, n)] = dict(clk[q])
+        if sem is None:
+            hist[(s, n)][s] = n
+        for x in rd:
+            note(R, x, s, n)
+        for x in wr:
+            note(W, x, s, n)
+
+    v, sc, te = g.vector, g.scalar, g.tensor
+
+    def vt(out, i0, i1, o):
+        op("v", lambda: v.tensor_tensor(ap(out), ap(i0), ap(i1), o), [i0, i1] + ([out[2]] if out[0] == "ind" else []), [out[1] if out[0] == "ind" else out])
+
+    def vs(out, i0, s1, o1, s2=None, o2=None):
+        a = [ap(x) if isinstance(x, tuple) else x for x in (s1, s2)]
+        if o2 is None:
+            op("v", lambda: v.tensor_scalar(ap(out), ap(i0), a[0], None, o1), [i0, s1], [out])
+        else:
+            op("v", lambda: v.tensor_scalar(ap(out), ap(i0), a[0], a[1], o1, o2), [i0, s1, s2], [out])
+
+    def vc(out, i):
+        op("v", lambda: v.tensor_copy(ap(out), ap(i)), [i], [out])
+
+    def ms(out, c):
+        op("v", lambda: v.memset(ap(out), c), [], [out])
+
+    def scan(out, d0, d1, o0, o1):
+        op("v", lambda: v.tensor_tensor_scan(ap(out), ap(d0), ap(d1), 0.0, o0, o1), [d0, d1], [out])
+
+    def act(out, i, f=F.Identity, bias=0.0, scale=1.0):
+        a = [ap(x) if isinstance(x, tuple) else x for x in (bias, scale)]
+        op("s", lambda: sc.activation(ap(out), ap(i), f, bias=a[0], scale=a[1]), [i, bias, scale], [out])
+
+    def mm(out, l, r, start, stop):
+        op("p", lambda: te.matmul(ap(out), ap(l), ap(r), bool(start), bool(stop)), [l, r], [out])
+
+    def iota(out, pat, base, cm):
+        kw = {} if SCRATCH[out[0]][2] == _i else {"allow_small_or_imprecise_dtypes": True}
+        op("g", lambda: g.iota(ap(out), pat, base, cm, **kw), [], [out])
+
+    def dma(out, i):
+        s = "d%d" % ndma[0]
+        ndma[0] += 1
+        o_, i_ = (ap(x) if x[0] in SCRATCH else T[x[0]][x[1]] for x in (out, i))
+        op("y", lambda: g.sync.dma_start(o_, i_), [i] if i[0] in SCRATCH else [], [out] if out[0] in SCRATCH else [], s, 16)
+
+    nls = [0]
+
+    def send(src, items, ne):
+        waits("g", need("g", [src], []))
+        tr, k = [], 0
+        for d, dst, sem in items:
+            to = T.cores[(rank - d) % N]
+            rid, pid = topo.addr(to)[:2]
+            es = topo.engines(core, to)[k:k + ne]
+            k += ne
+            tr.append(RemoteDMATransfer(dst_ids=[DstId(rid=rid, pnc=pid)], dma_engine_mask=sum(1 << e for e in es), remote_sem=T.sem[sem], src=ap(src), dst=T[dst][:], alu_op=0))
+            nls[0] += ne
+        g.remote_dma_fused(tr, local_sem=T.sem.ls)
+
+    def arrives(dst, sem, ne):
+        cnt[sem] = ne
+        note(W, b(dst), sem, ne)
+
+    fills = []
+
+    def fill(n=1):
+        for _ in range(n):
+            if fills:
+                fills.pop(0)()
+    full = S_[:]
+    NE = 4
+    dma(b("raw"), ("ctl", S_[:]))
+    dma(b("holI"), ("hol", S_[:]))
+    dma(b("X"), ("sha", S_[:]))
+    iota(b("pi"), [[0, 1]], 0, 1)
+    iota(b("IF"), [[1, 256]], 0, 0)
+    iota(b("JG"), [[1, 16], [0, 16]], 0, 0)
+    iota(b("JM"), [[0, 16], [1, 16]], 0, 0)
+    col = {n: b("cols", S_[j:j + 1]) for j, n in enumerate(("p", "q", "g", "g15", "is", "po", "w", "po2"))}
+    vs(b("qi"), b("pi"), 15, A.bitwise_and)
+    vc(col["p"], b("pi"))
+    vc(col["q"], b("qi"))
+    vt(col["g15"], b("pi"), b("qi"), A.subtract)
+    vs(b("cni"), b("qi"), 1, A.bitwise_and)
+    vs(col["g"], col["g15"], 1.0 / 16, A.mult)
+    vs(col["is"], col["q"], 2.0, A.is_lt)
+    vc(col["po"], b("cni"))
+    vs(col["g15"], col["g15"], 15.0, A.add)
+
+    def eye(n, c):
+        vs(b(n), b("IF", S_[0:128]), col["p"], A.is_equal, c, A.mult)
+
+    def blk(n, c):
+        vs(b(n), b("JG", S_[0:128]), col["g"], A.is_equal, c, A.mult)
+
+    def b8(n, c):
+        vs(b(n), b("IF", S_[0:8]), col["g"], A.is_equal, c, A.mult)
+    blk("Blk", 1.0)
+    vs(b("km"), b("IF", S_[0:16]), col["q"], A.is_equal)
+    for k in range(16):
+        act(b("EK", S_[128 * k:128 * k + 128]), b("Blk"), F.Copy, scale=b("km", S_[k:k + 1]))
+    eye("I", 1.0)
+    vs(b("HL", S_[0:128]), b("raw"), 2048.0, A.add)
+    vt(b("rawd"), b("raw"), b("HL", S_[0:128]), A.subtract)
+    vs(b("HL", S_[128:256]), b("rawd"), 2048.0, A.add)
+    ms(b("tab0"), 0.0)
+    send(b("HL"), [(1, "la1", "a1"), (2, "la2", "a2")], NE)
+    send(b("HL"), [(4, "la4", "a4"), (3, "la3", "a3")], NE)
+    send(b("HL"), [(6, "la6", "a6")], NE)
+    for d in DEL:
+        arrives("la%d" % d, "a%d" % d, NE)
+    for t in NEXT:
+        for d in NEXT[t]:
+            arrives("lb%d%d" % (t, d), "b%d%d" % (t, d), NE)
+
+    def expand(n, src):
+        o = [bp(n, S_[h:128:16], S_[:]) for h in (0, 1)]
+        waits("y", need("y", [b(src)], [o[0]]))
+        for h in (0, 1):
+            s = "d%d" % ndma[0]
+            ndma[0] += 1
+            cnt[s] = 16
+            g.sync.dma_start(ap(o[h]), ap(b(src, S_[128 * h:128 * h + 128]))).then_inc(T.sem[s], 16)
+            hist[(s, 16)] = dict(clk["y"])
+            note(R, b(src), s, 16)
+            note(W, o[h], s, 16)
+    expand("tab0", "HL")
+    vs(b("KSc", S_[0:143]), b("IF", S_[0:143]), col["g15"], A.is_equal, col["is"], A.mult)
+    for d in (1, 2):
+        ms(b("tab%d" % d), 0.0)
+    expand("tab1", "la1")
+    expand("tab2", "la2")
+    vs(col["w"], col["po"], -2.0, A.mult, 1.0, A.add)
+    vs(col["po2"], col["po"], 2048.0, A.mult)
+    for n, o, c in (("nI", "I", -1.0), ("I16", "I", 16.0), ("I256", "I", 256.0), ("I32", "I", 1.0), ("Iw", "I", col["w"]), ("Ip32", "I", col["po"]), ("Blk32", "Blk", 1.0),
+                    ("B4096", "Blk", 4096.0), ("BlkC", "Blk", col["is"])):
+        act(b(n), b(o), F.Copy, scale=c)
+    for n, c in (("Blk8", 1.0), ("Blk8c", col["is"]), ("B8h", 0.5), ("B8nh", -0.5)):
+        b8(n, c)
+
+    def hl_v(t):
+        act(b("vR"), b("vG%d" % t), bias=2048.0)
+        act(b("vU"), b("vG%d" % t), bias=2048.0)
+        mm(b("k4", S_[0:8]), b("Iw"), b("vR"), True, False)
+        mm(b("k4", S_[0:8]), b("Ip32"), b("vU"), False, True)
+        act(b("vHL%d" % t), b("k4", S_[0:8]))
+
+    def vals(t):
+        iota(b("VV"), [[8, 256], [0, 16]], t, 0)
+
+    def wrap(bank, src, lo, hi):
+        bk = b(bank, S_[lo // 32:hi // 32])
+        for q in range(16):
+            mm(bk, b("KSc", S_[15 - q:143 - q]), b(src, S_[16 * lo + q:16 * hi:16]), q == 0, q == 15)
+
+    def unwrap(bank, out, lo, hi):
+        vs(b(out, S_[lo:hi]), b(bank, S_[lo // 32:hi // 32]), -2048.0, A.add)
+
+    def gath(e, out, w, o):
+        if e == "s":
+            act(out, ind(w, o))
+        else:
+            vc(out, ind(w, o))
+
+    def c1(s, h, e):
+        gath(e, b("T1", S_[1024 * h:1024 * h + 1024]), b("tab%d" % s, S_[:]), b("off0", S_[64 * h:64 * h + 64]))
+
+    def c2(u, h, e):
+        gath(e, b("DT", S_[1024 * h:1024 * h + 1024]), b("tab%d" % u, S_[:]), b("off1", S_[64 * h:64 * h + 64]))
+
+    def gather_d(lo, hi, e):
+        gath(e, b("dR", S_[16 * lo:16 * hi]), b("DT", S_[:]), b("a16", S_[lo:hi]))
+
+    def gather_x(h):
+        gath("s", b("xk", S_[2048 * h:2048 * h + 2048]), b("X", S_[:]), b("a16", S_[128 * h:128 * h + 128]))
+
+    def sk_piece(t, j):
+        w = b("O", S_[0:2048]) if t else b("holI", S_[:])
+        vt(b("sk", S_[512 * j:512 * j + 512]), ind(w, b("a16", S_[32 * j:32 * j + 32])), b("VV", S_[512 * j:512 * j + 512]), A.is_equal)
+
+    def xv_mm(t):
+        for k in (0, 1):
+            mm(b("k0", S_[k::2]), b("I"), b("X", S_[t:2048:8]), True, True)
+
+    def min_v(p):
+        vt(b("mR", S_[512 * p:512 * p + 512]), b("xk", S_[p::8]), b("k0"), A.min)
+
+    def min_s(t, p):
+        bk = "k1" if p % 2 else "k2"
+        mm(b(bk), b("I"), b("xk", S_[p::8]), True, False)
+        for kk in (0, 1):
+            mm(b(bk, full, S_[kk::2]), b("nI"), b("X", S_[t:2048:8]), False, kk)
+        act(b("mR", S_[512 * p:512 * p + 512]), b(bk), F.Abs)
+
+    def m_mm(t, p):
+        for k in (p, p + 8):
+            for h in (0, 1):
+                l = b("mR", S_[512 * p + 256 * h + k // 8:512 * p + 256 * h + 256:2])
+                for o in ((k, k + 16) if k < 8 else (k,)):
+                    out = b("k5", S_[8 * h:8 * h + 8], o)
+                    if p < NV["min"]:
+                        mm(out, l, b("Blk8"), True, True)
+                    else:
+                        mm(out, b("xk", S_[2048 * h + k:2048 * h + 2048:16]), b("B8h"), True, False)
+                        mm(out, b("X", S_[1024 * h + t:1024 * h + 1024:8]), b("B8h"), False, False)
+                        mm(out, l, b("B8nh"), False, True)
+
+    def spread_max(src, least, mid=None):
+        mm(bp("k1", S_[0:16], S_[0:4]), b(src, S_[15::16]), b("I32"), True, True)
+        vs(bp("mx16", S_[0:16], S_[:]), bp("k1", S_[0:16], S_[0:4], full), least, A.max)
+        if mid:
+            mid()
+        for h in (0, 1):
+            mm(b("k2", S_[4 * h:4 * h + 4]), bp("E1", S_[0:16], S_[128 * h:128 * h + 128]), bp("mx16", S_[0:16], S_[:]), True, True)
+
+    rest = b("k7", S_[256:512])
+
+    def sellers(t):
+        vt(rest, b("O", S_[t:2048:8]), rest, A.mult)
+        vt(b("O", S_[t:2048:8]), b("sb"), rest, A.add)
+
+    ms(b("fm", full, S_[0:NV["far"]]), 16.0)
+    ms(b("fm", full, S_[NV["far"]:8]), 0.0)
+    ms(b("zer"), 0.0)
+    ms(b("o16"), 1.0 / 16)
+    ms(b("Z"), 9.0)
+    ms(b("O", S_[2048:2304]), 0.0)
+    vs(b("dumW"), b("IF", S_[0:16]), 16.0, A.mult, col["q"], A.add)
+    vt(b("BlkV"), b("Blk"), b("fm"), A.mult)
+    vs(b("dumW"), b("dumW"), 2048.0, A.add)
+    vc(b("a16"), b("holI", S_[0:2048:8]))
+    wrap("k3", "tab0", 0, 128)
+    gather_x(0)
+    unwrap("k3", "off0", 0, 128)
+    vals(0)
+    for t in range(RO):
+        iota(b("vG%d" % t), [[8, 256]], t, 0)
+    iota(b("JM3"), [[0, 16], [1, 16]], 0, 0)
+    iota(b("k15"), [[0, 16], [-1, 16]], 15, 0)
+    for n, c in (("B8s", 1.0 / 16), ("B816", 16.0), ("B8n32", -32.0)):
+        b8(n, c)
+    vs(b("rst"), b("JM"), 0.0, A.is_gt)
+    vs(b("maskW"), b("JM"), col["q"], A.is_equal)
+    vs(b("kc"), b("JM"), -1.0, A.mult, 31.0, A.add)
+    vs(b("E1"), b("JG"), col["p"], A.is_equal)
+    vs(b("dumG"), b("IF"), 2048.0, A.add)
+    c1(1, 0, "s")
+    c1(1, 1, "v")
+    for j in range(3):
+        vc(b("O", S_[512 * j:512 * j + 512]), b("holI", S_[512 * j:512 * j + 512]))
+    gather_x(1)
+    for h in (1, 0):
+        wrap("k3", "T1", 64 * h, 64 * h + 64)
+    xv_mm(0)
+    for h in (1, 0):
+        unwrap("k3", "off1", 64 * h, 64 * h + 64)
+        c2(2, h, "v")
+    gather_d(0, 128, "s")
+    gather_d(128, 256, "v")
+    vt(b("aD"), b("holI", S_[0:2048:8]), b("dumG"), A.subtract)
+    fills.append(lambda: vs(b("tri"), b("JM3"), col["q"], A.is_gt))
+    for j in range(3, 4):
+        fills.append(lambda j=j: vc(b("O", S_[512 * j:512 * j + 512]), b("holI", S_[512 * j:512 * j + 512])))
+    for d in (4, 3, 6):
+        dma(b("tab%d" % d), b("tab0"))
+        expand("tab%d" % d, "la%d" % d)
+
+    for t in range(RO):
+        if t:
+            gather_x(0)
+            gather_x(1)
+            gather_d(NV["d"], 256, "v")
+            sellers(t - 1)
+            gather_d(0, NV["d"], "s")
+            xv_mm(t)
+            vs(b("Z"), b("cnp"), 9.0, A.add)
+            for j in range(NV["sk"]):
+                sk_piece(t, j)
+            vt(b("aD"), b("O", S_[t:2048:8]), b("dumG"), A.subtract)
+        fills[0:0] = [lambda j=j, t=t: sk_piece(t, j) for j in range(NV["sk"] if t else 0, 8)]
+        for p in range(NV["min"]):
+            min_v(p)
+        if t:
+            fill(NV["sk2"])
+        for p in range(NV["min"], 8):
+            min_s(t, p)
+
+        def c_mm(h):
+            for k in range(16):
+                mm(b("k4", S_[8 * h:8 * h + 8], k), b("dR", S_[2048 * h + k:2048 * h + 2048:16]), b("Blk8c"), True, True)
+        for p in range(8):
+            if p == NV["c0"]:
+                c_mm(0)
+            if p == NV["c1"]:
+                c_mm(1)
+            m_mm(t, p)
+        act(b("md"), b("k5", full, S_[0:24]))
+        c4 = b("k4", full, S_[0:16])
+        vc(b("cd", full, S_[0:16]), c4)
+        vc(b("cd", full, S_[16:24]), b("k4", full, S_[0:8]))
+        pool = b("k6", full, S_[0:16])
+        mm(pool, b("I"), b("k15"), True, False)
+        mm(pool, b("I16"), b("md", full, S_[0:16]), False, False)
+        back = [(1, s) for s in range(1, 9 - NA)] + [x for s in range(9 - NA, 9) for x in ((1, s), (0, s)) if x != (1, 8)]
+        for s in range(1, 9):
+            eq = b("EQ", S_[16 * s - 16:16 * s], full)
+            vt(eq, b("cd", full, S_[s:s + 16]), c4, A.is_equal)
+            for j, (way, r) in enumerate(back):
+                if r != s:
+                    continue
+                bank = "k1" if j // 2 % 2 == 0 else "k2"
+                reg = b(bank, full, S_[16 * (j % 2):16 * (j % 2) + 16])
+                mm(reg, b("I256"), eq, True, False)
+                mm(reg, b("I"), b("md", full, S_[0:16] if way else S_[s:s + 16]), False, True)
+                if j % 2:
+                    act(b("PB", S_[8 * j - 8:8 * j + 8], full), b(bank, full, full), F.Relu, bias=-256.0)
+        act(b("cS"), c4)
+
+        def pool_b(j):
+            way, s = back[j]
+            z, o = S_[16 * (j // 2):16 * (j // 2) + 16], 16 * (j % 2)
+            if way:
+                mm(b("k6", full, S_[s:16]), b("I16"), b("PB", z, S_[o:o + 16 - s]), False, False)
+                mm(b("k6", full, S_[0:s]), b("I16"), b("PB", z, S_[o + 16 - s:o + 16]), False, False)
+            else:
+                mm(pool, b("I16"), b("PB", z, S_[o:o + 16]), False, j == len(back) - 1)
+        for s in range(1, 9 - NA):
+            eq = b("EQ", S_[16 * s - 16:16 * s], full)
+            vt(b("PA", S_[16 * s - 16:16 * s], full), eq, b("k5", full, S_[s:s + 16]), A.mult)
+            mm(pool, b("I16"), b("PA", S_[16 * s - 16:16 * s], full), False, False)
+            if s > 1:
+                pool_b(s - 2)
+        for j in range(7 - NA, len(back)):
+            pool_b(j)
+        fill(1)
+        for h in (0, 1):
+            mm(b("k3", S_[4 * h:4 * h + 4]), b("cS", S_[128 * h:128 * h + 128]), b("I32"), True, True)
+        act(b("cK"), b("k3", S_[0:8]), bias=-2048.0)
+        vc(b("keyS"), pool)
+        scan(b("mxS"), b("rst"), b("keyS"), A.mult, A.max)
+        for h in (0, 1):
+            mm(b("k3", S_[8 + 4 * h:12 + 4 * h]), b("keyS", S_[128 * h:128 * h + 128]), b("I32"), True, True)
+        act(b("keyK"), b("k3", S_[8:16]))
+        fl = b("k7", S_[0:256])
+        if t == 1:
+            for d in (3, 6):
+                act(b("tab%d" % d, S_[0:2048:8]), b("lb0%d" % d))
+        fl = b("k7", S_[0:256])
+
+        def far_const():
+            mm(fl, b("I"), b("kc"), True, False)
+            for p in range(NV["far"]):
+                for k in (p, p + 8):
+                    for h in (0, 1):
+                        mm(b("k7", S_[128 * h + k:128 * h + 128:16]), b("xk", S_[2048 * h + k:2048 * h + 2048:16]), b("B816"), False, False)
+        fill(1)
+        spread_max("mxS", 0.0, lambda: fill(1))
+        hl_v(t)
+
+        def stakes(h):
+            for k in range(16):
+                mm(b("k6", S_[8 + 4 * h:12 + 4 * h], S_[k::16]), b("sk", S_[2048 * h + k:2048 * h + 2048:16]), b("B8s"), True, True)
+        hot = b("k1", S_[8:16])
+        vt(hot, b("keyK"), b("k2", S_[0:8]), A.is_equal)
+        vt(b("ohc"), b("cK"), hot, A.mult)
+        bG = b("k0", S_[0:256])
+        mm(bG, b("Blk32"), b("ohc"), True, True)
+        far_const()
+        fill(1)
+        vt(b("mine"), b("cK"), bG, A.is_equal)
+        vs(b("w1"), b("mine"), 2.0, A.mult, -1.0, A.add)
+        act(b("w16"), b("mine"), scale=32.0, bias=-16.0)
+        vt(b("bw"), bG, b("maskW"), A.mult)
+        scan(b("bws"), b("rst"), b("bw"), A.mult, A.add)
+        vc(b("bo"), b("bws", S_[15::16]))
+        dps = b("k5", S_[0:8])
+        first = [True]
+        nv, ns_ = [0], [0]
+
+        def vbank():
+            nv[0] += 1
+            return "k1" if nv[0] % 2 else "k2"
+
+        def sbank():
+            ns_[0] += 1
+            return "k4" if ns_[0] % 2 else "k3"
+
+        def win_feed(p):
+            vec = p < NV["win"]
+            bk = vbank() if vec else sbank()
+            if not vec:
+                mm(b(bk), b("I"), b("xk", S_[p::8]), True, False)
+            for kk in (0, 1):
+                k = p + 8 * kk
+                mm(b(bk, full, S_[kk::2]), b("EK", S_[128 * k:128 * k + 128]), b("w1" if vec else "w16"), vec, vec or kk)
+            o = b("pR", S_[512 * p:512 * p + 512])
+            if vec:
+                vt(o, b("xk", S_[p::8]), b(bk), A.mult)
+            else:
+                act(o, b(bk), F.Abs)
+
+        def win_acc(p, last):
+            for kk in (0, 1):
+                mm(dps, b("I"), b("pR", S_[512 * p + kk:512 * p + 512:2]), first[0], last and kk)
+                first[0] = False
+
+        def mix(nv_):
+            vps, sps = list(range(nv_)), list(range(nv_, 8))
+            out = []
+            for j in range(8):
+                out += vps[j:j + 1] + sps[j:j + 1]
+            return out
+        order = mix(NV["win"])
+        for p in order[:2]:
+            win_feed(p)
+        fill(99)
+        for p in order[2:4]:
+            win_feed(p)
+        act(b("xb"), ind(b("X", S_[:]), b("bo")))
+        hd = b("k0", S_[256:512])
+        act(b("hR"), bG, bias=2048.0)
+        act(b("hU"), bG, bias=col["po2"], scale=col["po"])
+        act(b("bU"), bG)
+        stakes(0)
+        for j, p in enumerate(order):
+            if j == 2:
+                mm(hd, b("Iw"), b("hR"), True, False)
+                mm(hd, b("nI"), b("vHL%d" % t), False, True)
+            win_acc(p, j == 7)
+            if j + 4 < 8:
+                win_feed(order[j + 4])
+        for kk in (0, 1):
+            mm(b("k2", full, S_[kk::2]), b("I"), b("xb"), True, True)
+        for h in (0, 1):
+            mm(b("k7", S_[128 * h:128 * h + 128]), b("xb", S_[128 * h:128 * h + 128]), b("BlkV"), False, False)
+        forder = mix(NV["far"])
+
+        def far_feed(p):
+            o = b("mR", S_[512 * p:512 * p + 512])
+            if p < NV["far"]:
+                vt(o, b("xk", S_[p::8]), b("k2"), A.min)
+            else:
+                bk = sbank()
+                mm(b(bk), b("I"), b("xk", S_[p::8]), True, False)
+                for kk in (0, 1):
+                    mm(b(bk, full, S_[kk::2]), b("nI"), b("xb"), False, kk)
+                act(o, b(bk), F.Abs)
+
+        def far_acc(p, last):
+            for k in (p, p + 8):
+                for h in (0, 1):
+                    mm(b("k7", S_[128 * h + k:128 * h + 128:16]), b("mR", S_[512 * p + 256 * h + k // 8:512 * p + 256 * h + 256:2]),
+                       b("B8n32" if p < NV["far"] else "B816"), False, last and k > 7 and h)
+        vs(b("gt"), dps, 32.0 * (8 - NV["win"]), A.is_gt)
+        for p in forder[:2]:
+            far_feed(p)
+        for h in (0, 1):
+            mm(b("k1", S_[4 * h:4 * h + 4]), b("gt", S_[128 * h:128 * h + 128]), b("Blk"), True, True)
+        mm(b("k1", S_[8:16]), b("Blk"), b("gt"), True, True)
+        far_feed(forder[2])
+        stakes(1)
+        act(b("st"), b("k6", S_[8:16]), F.Sign)
+        mm(b("k6", S_[0:8]), b("zer", S_[0:128]), b("zer"), True, False)
+        for h in (0, 1):
+            mm(b("k6", S_[4 * h:4 * h + 4]), b("mine", S_[128 * h:128 * h + 128]), b("nI"), False, False)
+        vs(b("wl"), b("k1", S_[0:8]), b("Z"), A.is_ge)
+        mm(b("k6", S_[0:8]), b("I"), b("st"), False, False)
+        mm(b("k6", S_[0:8]), b("I"), b("wl"), False, True)
+        act(b("elw"), b("k6", S_[0:8]), F.Relu, bias=-1.0)
+        vt(hd, b("hU"), hd, A.add)
+        vs(b("winG"), b("k1", S_[8:16]), b("Z"), A.is_ge)
+        vt(hd, b("winG"), hd, A.mult)
+        CN = "CN%d" % t
+        vt(b(CN), b("vHL%d" % t), hd, A.add)
+        if t in NEXT:
+            ds = NEXT[t]
+            for j in range(0, len(ds), 2):
+                send(b(CN), [(d, "lb%d%d" % (t, d), "b%d%d" % (t, d)) for d in ds[j:j + 2]], NE)
+            vals(t + 1)
+        vc(b("tab0", S_[t:2048:8]), b(CN))
+        for p in forder[3:6]:
+            far_feed(p)
+        for p in forder[:3]:
+            far_acc(p, False)
+        nxt = t < RO - 1
+        goal = b("k5", full, S_[0:16])
+        if nxt:
+            wrap("k5", "tab0", 0, 128)
+        for p in forder[3:5]:
+            far_acc(p, False)
+        for j in (6, 7):
+            far_feed(forder[j])
+        for j in (5, 6, 7):
+            far_acc(forder[j], j == 7)
+        vt(b("FK"), b("elw"), fl, A.mult)
+        scan(b("fS"), b("rst"), b("FK"), A.mult, A.max)
+        for h in (0, 1):
+            mm(b("k4", S_[4 * h:4 * h + 4]), b("FK", S_[128 * h:128 * h + 128]), b("I32"), True, True)
+        act(b("FKk"), b("k4", S_[0:8]))
+        if nxt:
+            unwrap("k5", "off0", 0, 128)
+            op("v", lambda: v.tensor_reduce(ap(b("cnw")), ap(b("winG")), AxisListType.X, A.add), [b("winG")], [b("cnw")])
+        spread_max("fS", 1.0)
+        if nxt:
+            mm(b("k3", 15, S_[31:32]), b("o16"), b("cnw"), True, True)
+            vc(b("cni"), b("k3", 15, S_[31:32]))
+            vs(b("cnp"), b("cni"), 1, A.bitwise_and)
+            s_, u_ = NEXT[t][0] if t == 0 else 3, NEXT[t][1] if t == 0 else 6
+            for d in (s_, u_):
+                act(b("tab%d" % d, S_[t:2048:8]), b("lb%d%d" % (t, d)))
+        mm(goal, b("I32"), b("dumG"), True, False)
+        vt(hot, b("FKk"), b("k2", S_[0:8]), A.is_equal)
+        vt(b("ga"), b("aD"), hot, A.mult)
+        mm(goal, b("Blk32"), b("ga"), False, True)
+        vt(b("ca"), b("cK"), hot, A.mult)
+        csG = b("k6", S_[0:8])
+        mm(csG, b("Blk32"), b("ca"), True, True)
+        mm(hd, b("I32"), b("vG%d" % t), True, True)
+        vt(b("sb"), b("bU"), hot, A.mult)
+        if nxt:
+            for h in (0, 1):
+                c1(s_, h, "s")
+        vt(b("gw"), goal, b("maskW"), A.mult)
+        scan(b("gws"), b("rst"), b("gw"), A.mult, A.add)
+        vc(b("gSu"), goal)
+        vc(b("go"), b("gws", S_[15::16]))
+        act(b("OG"), ind(b("O", S_[:]), b("go")))
+        act(rest, hot, scale=-1.0, bias=1.0)
+        dup = b("k4", full, S_[0:16])
+        mm(dup, b("I"), b("zer"), True, False)
+        for c in range(16):
+            vs(b("E3", c, S_[0:256 - 16 * c]), b("gSu", S_[16 * c:256]), b("gws", S_[16 * c + 15:16 * c + 16]), A.is_equal)
+            if c < 15:
+                mm(b("k4", S_[c + 1:16], S_[0:16]), b("B4096"), b("E3", c, S_[16:256 - 16 * c]), False, False)
+            if nxt and c in (1, 6):
+                h = c // 6
+                wrap("k3", "T1", 64 * h, 64 * h + 64)
+            if nxt and c in (13, 15):
+                h = c // 15
+                unwrap("k3", "off1", 64 * h, 64 * h + 64)
+                c2(u_, h, "s")
+        vt(b("E3", full, S_[0:16]), b("E3", full, S_[0:16]), b("tri"), A.mult)
+        mm(dup, b("B4096"), b("E3", full, S_[0:16]), False, True)
+        vt(b("eqv"), b("OG"), hd, A.is_equal)
+        vt(csG, csG, b("OG"), A.subtract)
+        vt(b("tt"), b("eqv"), csG, A.mult)
+        vt(b("dw"), dup, b("maskW"), A.mult)
+        scan(b("dws"), b("rst"), b("dw"), A.mult, A.add)
+        vt(b("t1"), b("dws", S_[15::16]), b("dumW"), A.min)
+        vt(b("t2"), b("t1"), b("gws", S_[15::16]), A.max)
+        vc(b("so"), b("t2"))
+        vt(ind(b("O", S_[:]), b("so")), b("OG"), b("tt"), A.add)
+        if not nxt:
+            break
+        vc(b("a16"), b("O", S_[t + 1:2048:8]))
+    sellers(RO - 1)
+    for j, bk in enumerate(("k1", "k2", "k3", "k4")):
+        mm(b(bk), b("BlkC"), b("tab0", S_[512 * j:512 * j + 512]), True, True)
+        act(b("ycS", S_[512 * j:512 * j + 512]), b(bk), bias=-2048.0)
+    dma(("yo", S_[:]), b("O", S_[0:2048]))
+    dma(("yc", S_[:]), bp("ycS", S_[0:128:16], S_[:]))
+    for s, n in cnt.items():
+        g.wait_ge(T.sem[s], n)
+    g.wait_ge(T.sem.ls, nls[0])

@@ -4,58 +4,47 @@ from concourse.bass import DstId, RemoteDMATransfer
 
 V, D, L, RO, N = 2048, 8, 256, 3, 8
 DEL = (1, 2, 4, 3, 6)
+HOPS = ((1, 2), (2, 4), (3, 6))
 NEXT = {0: (2, 4, 3, 6), 1: (3, 6)}
-NV = {"min": 8, "win": 5, "far": 6, "d": 128, "sk": 2, "sk2": 0, "c0": 5, "c1": 0}
-NA = 1
+PAR = {"prod": 6, "win": 0, "gx": "svsv", "gd": "ssss", "c1": "ss", "c2": "ss", "gx0": "ssss", "gd0": "svsv", "c10": "sv", "c20": "sv",
+       "sk": 16, "look": 1.0, "gat": 1.56, "arr": 3.0, "arr0": 6.0}
 S_ = np.s_
+U = 8192.0
 
-_bf, _f, _i, _u = "bfloat16", "float32", "int32", "uint16"
+_bf, _f, _i, _u, _h = "bfloat16", "float32", "int32", "uint16", "float16"
 _shapes = {
-    "O": ([2304], _f), "holI": ([2048], _i), "X": ([2048], _bf), "raw": ([128], _i), "rawd": ([128], _f),
-    "HL": ([256], _bf), "VV": ([4096], _f), "xk": ([4096], _bf), "sk": ([4096], _bf), "dR": ([4096], _bf),
-    "mR": ([4096], _bf), "pR": ([4096], _bf), "T1": ([2048], _bf), "DT": ([2048], _bf), "EK": ([2048], _bf),
+    "O": ([2304], _f), "holI": ([2048], _i), "X": ([2048], _bf), "raw": ([128], _i), "rawf": ([128], _f), "rawh": ([128], _h),
+    "C8": ([16, 128], _h), "VV": ([4096], _f), "xk": ([4096], _bf), "sk": ([4096], _bf), "dR": ([4096], _h),
+    "mR": ([4096], _bf), "pR": ([4096], _bf), "T1": ([2048], _h), "DT": ([2048], _f), "EK": ([2048], _bf), "ID": ([2048], _f),
     "E3": ([16, 272], _bf), "ycS": ([2048], _f),
-    "EQ": ([128, 16], _bf), "PA": ([128, 16], _bf), "PB": ([80, 32], _bf),
+    "cS": ([256], _h), "cm": ([16, 32], _h), "EQ": ([128, 16], _bf), "PA": ([128, 16], _bf), "PB": ([128, 32], _bf),
     "off0": ([128], _u), "off1": ([128], _u), "a16": ([256], _u), "bo": ([16], _u), "go": ([16], _u), "so": ([16], _u),
-    "gSu": ([256], _u), "aD": ([256], _f), "cd": ([16, 24], _f), "md": ([16, 24], _bf), "cS": ([256], _f),
-    "bU": ([256], _f), "keyS": ([256], _f), "mxS": ([256], _f), "keyK": ([256], _f), "mx16": ([128], _f), "ohc": ([256], _f),
-    "cK": ([256], _f), "mine": ([256], _bf), "w1": ([256], _bf), "w16": ([256], _bf), "bw": ([256], _f), "bws": ([256], _f),
-    "xb": ([256], _bf), "gt": ([256], _bf), "wl": ([256], _bf), "winG": ([256], _f), "st": ([256], _bf), "el": ([256], _f), "elw": ([256], _f),
-    "FK": ([256], _f), "FKk": ([256], _f), "fS": ([256], _f), "ga": ([256], _f), "ca": ([256], _f), "ns": ([256], _f),
-    "sb": ([256], _f), "gw": ([256], _f), "gws": ([256], _f), "OG": ([256], _f), "dw": ([256], _f), "dws": ([256], _f),
-    "t1": ([16], _f), "t2": ([16], _f), "eqv": ([256], _f), "dd": ([256], _f), "tt": ([256], _f), "oc": ([256], _f),
-    "hR": ([256], _bf), "hU": ([256], _f), "vR": ([256], _bf), "vW": ([256], _bf), "vU": ([256], _f),
-    "cnw": ([1], _f), "cni": ([1], _i), "cnp": ([1], _i), "Z": ([1], _f),
-    "IF": ([256], _f), "JG": ([256], _f), "JM": ([256], _f), "JM3": ([16, 16], _f), "pi": ([1], _i), "qi": ([1], _i),
-    "cols": ([16], _f), "I": ([128], _bf), "I16": ([128], _bf), "I256": ([128], _bf), "nI": ([128], _bf), "Iw": ([128], _bf),
-    "I32": ([128], _f), "Ip32": ([128], _f), "Blk": ([128], _bf), "Blk32": ([128], _f), "BlkC": ([128], _bf), "B4096": ([128], _bf), "BlkV": ([128], _bf),
-    "fm": ([16, 8], _bf), "Blk8": ([8], _bf), "Blk8c": ([8], _bf), "B8s": ([8], _bf), "B816": ([8], _bf), "B8n32": ([8], _bf),
-    "B8h": ([8], _bf), "B8nh": ([8], _bf), "KSc": ([144], _bf),
-    "km": ([16], _f), "maskW": ([256], _f), "rst": ([256], _f), "tri": ([16, 16], _bf), "E1": ([256], _f), "k15": ([16, 16], _bf),
-    "kc": ([256], _bf), "dumG": ([256], _f), "dumW": ([16], _f), "zer": ([256], _bf), "o16": ([128], _f),
+    "run": ([256], _f), "mxB": ([256], _f), "hotL": ([256], _bf), "cK": ([256], _h), "ohc": ([256], _h), "mine": ([256], _bf), "w1": ([256], _bf),
+    "xb": ([256], _bf), "gt": ([256], _bf), "wl": ([256], _bf), "st": ([256], _bf), "aD": ([256], _h), "ga": ([256], _h), "ca": ([256], _h),
+    "hotS": ([256], _bf), "gS": ([256], _h), "gw": ([16], _f), "gwh": ([16], _h), "OG": ([256], _f), "eqv": ([256], _bf), "tt": ([256], _f),
+    "dupS": ([256], _bf), "t1": ([16], _f), "dbv": ([16], _f), "winW": ([16], _f), "tw": ([16], _f), "nw": ([16], _f),
+    "cnw": ([1], _f), "cni": ([1], _i), "cnp": ([1], _i), "thr": ([RO], _f),
+    "IF": ([144], _f), "JG": ([128], _f), "JM": ([16, 16], _f), "pi": ([1], _i), "qi": ([1], _i), "cols": ([8], _f),
+    "I": ([128], _bf), "I16": ([128], _bf), "I256": ([128], _bf), "I5": ([128], _bf), "nIU": ([128], _bf),
+    "I32": ([128], _f), "nI32": ([128], _f), "one32": ([128], _f), "Blk": ([128], _bf),
+    "Blk8": ([8], _bf), "Blk8c": ([8], _bf), "B816": ([8], _bf), "B8n32": ([8], _bf),
+    "KSa": ([144], _bf), "KS0": ([144], _bf), "KS8": ([144], _bf), "km": ([16], _f), "rst": ([128], _f), "k15": ([128], _bf),
+    "kc": ([128], _bf), "lift": ([128], _bf), "tri": ([16, 16], _bf), "dumW": ([16], _f), "vW": ([48], _f), "zer": ([256], _bf),
 }
 SCRATCH = {n: ("sbuf", [128] + s, d) for n, (s, d) in _shapes.items()}
-PACK = {n: 256 * j for j, n in enumerate((
-    "aD cS keyS mxS keyK ohc cK bw bws el elw winG FK FKk fS ga ca bU sb gw gws OG dw dws eqv tt hU vU").split())}
-SHAPE = dict(SCRATCH)
-for _n in PACK:
-    del SCRATCH[_n]
-SCRATCH["lanes"] = ("sbuf", [128, 256 * len(PACK)], _f)
-for _d in (0,) + DEL:
-    SCRATCH["tab%d" % _d] = ("sbuf", [128, 2048], _bf)
 for _d in DEL:
-    SCRATCH["la%d" % _d] = ("sbuf", [128, 256], _bf)
+    SCRATCH["tab%d" % _d] = ("sbuf", [128, 2048], _f)
+    SCRATCH["la%d" % _d] = ("sbuf", [128, 128], _f)
 for _t in NEXT:
     for _d in NEXT[_t]:
-        SCRATCH["lb%d%d" % (_t, _d)] = ("sbuf", [128, 256], _bf)
+        SCRATCH["lb%d%d" % (_t, _d)] = ("sbuf", [128, 16], _u)
 for _t in range(RO):
-    SCRATCH["CN%d" % _t] = ("sbuf", [128, 256], _bf)
-    SCRATCH["vHL%d" % _t] = ("sbuf", [128, 256], _bf)
+    SCRATCH["nW%d" % _t] = ("sbuf", [128, 16], _u)
     SCRATCH["vG%d" % _t] = ("sbuf", [128, 256], _f)
 for _k in range(8):
-    SCRATCH["k%d" % _k] = ("psum", [128, 512] if _k in (0, 7) else [128, 16, 32], _f)
-SHAPE.update(SCRATCH)
-SEMAPHORES = ["qv", "qs", "qp", "qg", "ls"] + ["d%d" % k for k in range(24)] + ["a%d" % d for d in DEL] + ["b%d%d" % (t, d) for t in NEXT for d in NEXT[t]]
+    SCRATCH["k%d" % _k] = ("psum", [128, 16, 32] if _k < 6 else [128, 512], _f)
+SEMAPHORES = ["qv", "qs", "qp", "qg", "ls"] + ["d%d" % k for k in range(16)] + ["a%d" % d for d in DEL] + ["b%d%d" % (t, d) for t in NEXT for d in NEXT[t]]
+_memo = {}
 
 
 def b(n, *ix):
@@ -70,20 +59,138 @@ def ind(w, o):
     return ("ind", w, o)
 
 
+def cols(x):
+    key = repr(x)
+    if key not in _memo:
+        ix = x[1][1:]
+        sh = SCRATCH[x[0]][1][1:]
+        m = np.arange(int(np.prod(sh))).reshape(sh)
+        c = m[ix].ravel() if ix else m.ravel()
+        bits = np.zeros(m.size, np.uint8)
+        bits[c] = 1
+        _memo[key] = (c, int.from_bytes(np.packbits(bits).tobytes(), "big"))
+    return _memo[key]
+
+
+def psum(x):
+    return SCRATCH[x[0]][0] == "psum"
+
+
+def two(x):
+    return SCRATCH[x[0]][2] in (_bf, _h, _u)
+
+
+def order(ops):
+    n = len(ops)
+    pre = [set() for _ in range(n)]
+    Wr, Rd, bar, single, union, members = {}, {}, {}, {}, {}, {}
+    for i, o in enumerate(ops):
+        if o["grp"] is not None:
+            union[o["grp"]] = union.get(o["grp"], 0) | cols(o["wr"][0])[1]
+            members.setdefault(o["grp"], []).append(i)
+
+    def write(name, m, who, i):
+        for tab in (Wr, Rd):
+            keep = []
+            for j, mj in tab.get(name, ()):
+                if mj & m:
+                    pre[i].add(j)
+                    mj &= ~m
+                if mj:
+                    keep.append((j, mj))
+            tab[name] = keep
+        Wr[name] += [(j, m) for j in who]
+    for i, o in enumerate(ops):
+        pre[i].update(o["after"])
+        for x in o["rd"]:
+            m = cols(x)[1]
+            pre[i].update(j for j, mj in Wr.get(x[0], ()) if mj & m)
+        gr = o["grp"]
+        if gr is not None:
+            bank, mem = o["wr"][0][0], members[gr]
+            if i == mem[0]:
+                pre[i].update(bar.get(bank, ()))
+                if len(mem) > 1:
+                    pre[i].update(single.pop(bank, ()))
+                    bar[bank] = mem
+                else:
+                    single.setdefault(bank, []).append(i)
+                write(bank, union[gr], mem, i)
+            else:
+                pre[i].add(mem[0])
+        else:
+            for x in o["wr"]:
+                write(x[0], cols(x)[1], [i], i)
+        for x in o["rd"]:
+            Rd.setdefault(x[0], []).append((i, cols(x)[1]))
+        pre[i].discard(i)
+    suc = [[] for _ in range(n)]
+    for i in range(n):
+        assert all(j < i for j in pre[i])
+        for j in pre[i]:
+            suc[j].append(i)
+
+    def gap(j, i):
+        return ops[j]["lat"] + (0.0 if ops[j]["q"] == ops[i]["q"] else 0.06)
+    way = [0.0] * n
+    for i in range(n - 1, -1, -1):
+        way[i] = ops[i]["cost"] + max([way[j] + gap(i, j) for j in suc[i]], default=ops[i]["lat"])
+    left = [len(p) for p in pre]
+    banks = [set(x[0] for x in o["rd"] + o["wr"] if psum(x)) for o in ops]
+    ready, end, at, free, used, out = {}, [0.0] * n, [0.0] * n, {}, {}, []
+    for i in range(n):
+        if not left[i]:
+            ready.setdefault(ops[i]["q"], []).append(i)
+
+    def start(i):
+        q = ops[i]["q"]
+        t = max(at[i], free.get(q, 0.0))
+        for k in banks[i]:
+            for q2, e in used.get(k, {}).items():
+                if q2 != q and e > t:
+                    t = e
+        return t
+    while len(out) < n:
+        best = None
+        for q, lst in ready.items():
+            if lst:
+                st = [(start(i), i) for i in lst]
+                t0 = min(st)[0]
+                if best is None or t0 < best[0]:
+                    best = (t0, q, st)
+        t0, q, st = best
+        x = max((i for s, i in st if s <= t0 + 1e-9), key=lambda i: (way[i], -i))
+        s0 = t0
+        for s, i in st:
+            if way[i] > way[x] and t0 < s and (s - t0) < PAR["look"] * (s0 + ops[x]["cost"] - s):
+                x, s0 = i, s
+        ready[q].remove(x)
+        out.append(x)
+        end[x] = s0 + ops[x]["cost"]
+        if q:
+            free[q] = end[x]
+        for k in banks[x]:
+            used.setdefault(k, {})[q] = end[x] + ops[x]["lat"] + 0.06
+        for j in suc[x]:
+            at[j] = max(at[j], end[x] + gap(x, j))
+            left[j] -= 1
+            if not left[j]:
+                ready.setdefault(ops[j]["q"], []).append(j)
+    return out
+
+
 def rank_program(g, core, T, topo):
     rank = T.rank_of(core)
     if rank is None:
         return
     eng = {"v": g.vector, "s": g.scalar, "p": g.tensor, "g": g, "y": g.sync}
-    cnt, clk, hist, W, R, cache = {}, {q: {} for q in eng}, {}, {}, {}, {}
-    ndma = [0]
+    v, sc, te = g.vector, g.scalar, g.tensor
+    ops = []
+    CY = 0.83e-3
 
     def ap(x):
         if x[0] == "ind":
             return T[x[1][0]][x[1][1]].indirect(T[x[2][0]][x[2][1]])
-        if x[0] in PACK:
-            lo, hi, st = (x[1][1] if len(x[1]) > 1 else slice(None)).indices(256)
-            return T["lanes"][x[1][0], PACK[x[0]] + lo:PACK[x[0]] + hi:st]
         return T[x[0]][x[1]]
 
     def parts(xs):
@@ -91,219 +198,94 @@ def rank_program(g, core, T, topo):
         for x in xs:
             if isinstance(x, tuple):
                 out += [x[1], x[2]] if x[0] == "ind" else [x]
-        return out
+        return [x for x in out if x[0] in SCRATCH]
 
-    def size(n):
-        return int(np.prod(SHAPE[n][1][1:]))
+    def op(q, fn, rd, wr, cost, lat=0.0, sem=None, amt=1, grp=None, after=()):
+        ops.append({"q": q, "fn": fn, "rd": parts(rd), "wr": parts(wr), "cost": cost, "lat": lat, "sem": sem, "amt": amt, "grp": grp, "after": after})
+        return len(ops) - 1
 
-    def cols(x):
-        key = repr(x)
-        if key not in cache:
-            ix = x[1][1:]
-            m = np.arange(size(x[0])).reshape(SHAPE[x[0]][1][1:])
-            cache[key] = m[ix].ravel() if ix else m.ravel()
-        return cache[key]
+    def span(out, i, rate):
+        if out[0] == "ind":
+            return 0.05 + 16 * len(cols(out[2])[0]) * 3.8 * CY
+        if i[0] == "ind":
+            return 0.05 + 16 * len(cols(i[2])[0]) * PAR["gat"] * CY
+        return 0.05 + max(64, len(cols(i)[0]) * rate) * CY
 
-    def need(q, rd, wr):
-        req = {}
-        own = "q" + q
-
-        def take(tab, x, skip):
-            ps = SHAPE[x[0]][0] == "psum"
-            for s, arr in tab.get(x[0], {}).items():
-                if s == own and skip:
-                    continue
-                n = int(arr.max() if ps and s != own else arr[cols(x)].max())
-                if n > req.get(s, 0):
-                    req[s] = n
-        for x in rd:
-            take(W, x, False)
-            if SHAPE[x[0]][0] == "psum":
-                take(R, x, True)
-        for x in wr:
-            take(W, x, True)
-            take(R, x, True)
-        return req
-
-    def waits(q, req):
-        for s, n in sorted(req.items(), key=lambda z: -len(hist.get(z, ()))):
-            if clk[q].get(s, 0) < n:
-                eng[q].wait_ge(T.sem[s], n)
-                clk[q][s] = n
-                for s2, n2 in hist.get((s, n), {}).items():
-                    clk[q][s2] = max(clk[q].get(s2, 0), n2)
-
-    def note(tab, x, s, n):
-        d = tab.setdefault(x[0], {})
-        if s not in d:
-            d[s] = np.zeros(size(x[0]), np.int64)
-        d[s][cols(x)] = n
-
-    def op(q, fn, rd, wr, sem=None, amt=1):
-        rd, wr = parts(rd), parts(wr)
-        waits(q, need(q, rd, wr))
-        s = sem or "q" + q
-        cnt[s] = cnt.get(s, 0) + amt
-        n = cnt[s]
-        fn().then_inc(T.sem[s], amt)
-        hist[(s, n)] = dict(clk[q])
-        if sem is None:
-            hist[(s, n)][s] = n
-        for x in rd:
-            note(R, x, s, n)
-        for x in wr:
-            note(W, x, s, n)
-
-    v, sc, te = g.vector, g.scalar, g.tensor
+    def half(*xs):
+        return 0.5 if all(x[0] != "ind" and two(x) for x in xs) else 1.0
 
     def vt(out, i0, i1, o):
-        op("v", lambda: v.tensor_tensor(ap(out), ap(i0), ap(i1), o), [i0, i1] + ([out[2]] if out[0] == "ind" else []), [out[1] if out[0] == "ind" else out])
+        rate = 1.0 if i0[0] == "ind" or psum(i0) or psum(i1) else 2.0
+        op("v", lambda: v.tensor_tensor(ap(out), ap(i0), ap(i1), o), [i0, i1] + ([out[2]] if out[0] == "ind" else []),
+           [out[1] if out[0] == "ind" else out], span(out, i0, rate))
 
     def vs(out, i0, s1, o1, s2=None, o2=None):
-        a = [ap(x) if isinstance(x, tuple) else x for x in (s1, s2)]
-        if o2 is None:
-            op("v", lambda: v.tensor_scalar(ap(out), ap(i0), a[0], None, o1), [i0, s1], [out])
-        else:
-            op("v", lambda: v.tensor_scalar(ap(out), ap(i0), a[0], a[1], o1, o2), [i0, s1, s2], [out])
+        def fn():
+            a = [ap(x) if isinstance(x, tuple) else x for x in (s1, s2)]
+            if o2 is None:
+                return v.tensor_scalar(ap(out), ap(i0), a[0], None, o1)
+            return v.tensor_scalar(ap(out), ap(i0), a[0], a[1], o1, o2)
+        op("v", fn, [i0, s1, s2], [out], span(out, i0, half(out, i0)))
 
     def vc(out, i):
-        op("v", lambda: v.tensor_copy(ap(out), ap(i)), [i], [out])
+        op("v", lambda: v.tensor_copy(ap(out), ap(i)), [i], [out], span(out, i, half(out, i)))
 
     def ms(out, c):
-        op("v", lambda: v.memset(ap(out), c), [], [out])
+        op("v", lambda: v.memset(ap(out), c), [], [out], span(out, out, half(out)))
 
     def scan(out, d0, d1, o0, o1):
-        op("v", lambda: v.tensor_tensor_scan(ap(out), ap(d0), ap(d1), 0.0, o0, o1), [d0, d1], [out])
+        op("v", lambda: v.tensor_tensor_scan(ap(out), ap(d0), ap(d1), 0.0, o0, o1), [d0, d1], [out], span(out, d0, 1.0))
 
     def act(out, i, f=F.Identity, bias=0.0, scale=1.0):
-        a = [ap(x) if isinstance(x, tuple) else x for x in (bias, scale)]
-        op("s", lambda: sc.activation(ap(out), ap(i), f, bias=a[0], scale=a[1]), [i, bias, scale], [out])
+        def fn():
+            a = [ap(x) if isinstance(x, tuple) else x for x in (bias, scale)]
+            return sc.activation(ap(out), ap(i), f, bias=a[0], scale=a[1])
+        op("s", fn, [i, bias, scale], [out], 0.01 + span(out, i, 1.0))
 
-    def mm(out, l, r, start, stop):
-        op("p", lambda: te.matmul(ap(out), ap(l), ap(r), bool(start), bool(stop)), [l, r], [out])
+    todo = {}
+
+    def mm(out, l, r, grp=None):
+        grp = grp or ("one", len(ops))
+        first = grp not in todo
+        todo[grp] = todo.get(grp, 0) + 1
+
+        def fn():
+            todo[grp] -= 1
+            return te.matmul(ap(out), ap(l), ap(r), first, todo[grp] == 0)
+        cyc = max(min(64, len(cols(l)[0])), len(cols(r)[0])) * (1 if two(l) else 4)
+        op("p", fn, [l, r], [out], cyc * CY / 2, 0.1, grp=grp)
+
+    def group():
+        return ("grp", len(ops))
 
     def iota(out, pat, base, cm):
         kw = {} if SCRATCH[out[0]][2] == _i else {"allow_small_or_imprecise_dtypes": True}
-        op("g", lambda: g.iota(ap(out), pat, base, cm, **kw), [], [out])
+        op("g", lambda: g.iota(ap(out), pat, base, cm, **kw), [], [out], 0.13 + 2 * len(cols(out)[0]) * CY)
 
-    def dma(out, i):
+    ndma = [0]
+
+    def dma(out, i, lat, q="y"):
         s = "d%d" % ndma[0]
         ndma[0] += 1
-        o_, i_ = (ap(x) if x[0] in SCRATCH else T[x[0]][x[1]] for x in (out, i))
-        op("y", lambda: g.sync.dma_start(o_, i_), [i] if i[0] in SCRATCH else [], [out] if out[0] in SCRATCH else [], s, 16)
+        op(q, lambda: eng[q].dma_start(ap(out), ap(i)), [i], [out], 0.1, lat, s, 16)
 
     nls = [0]
-
-    def send(src, items, ne):
-        waits("g", need("g", [src], []))
-        tr, k = [], 0
-        for d, dst, sem in items:
-            to = T.cores[(rank - d) % N]
-            rid, pid = topo.addr(to)[:2]
-            es = topo.engines(core, to)[k:k + ne]
-            k += ne
-            tr.append(RemoteDMATransfer(dst_ids=[DstId(rid=rid, pnc=pid)], dma_engine_mask=sum(1 << e for e in es), remote_sem=T.sem[sem], src=ap(src), dst=T[dst][:], alu_op=0))
-            nls[0] += ne
-        g.remote_dma_fused(tr, local_sem=T.sem.ls)
-
-    def arrives(dst, sem, ne):
-        cnt[sem] = ne
-        note(W, b(dst), sem, ne)
-
-    fills = []
-
-    def fill(n=1):
-        for _ in range(n):
-            if fills:
-                fills.pop(0)()
-    full = S_[:]
     NE = 4
-    dma(b("raw"), ("ctl", S_[:]))
-    dma(b("holI"), ("hol", S_[:]))
-    dma(b("X"), ("sha", S_[:]))
-    iota(b("pi"), [[0, 1]], 0, 1)
-    iota(b("IF"), [[1, 256]], 0, 0)
-    iota(b("JG"), [[1, 16], [0, 16]], 0, 0)
-    iota(b("JM"), [[0, 16], [1, 16]], 0, 0)
-    col = {n: b("cols", S_[j:j + 1]) for j, n in enumerate(("p", "q", "g", "g15", "is", "po", "w", "po2"))}
-    vs(b("qi"), b("pi"), 15, A.bitwise_and)
-    vc(col["p"], b("pi"))
-    vc(col["q"], b("qi"))
-    vt(col["g15"], b("pi"), b("qi"), A.subtract)
-    vs(b("cni"), b("qi"), 1, A.bitwise_and)
-    vs(col["g"], col["g15"], 1.0 / 16, A.mult)
-    vs(col["is"], col["q"], 2.0, A.is_lt)
-    vc(col["po"], b("cni"))
-    vs(col["g15"], col["g15"], 15.0, A.add)
 
-    def eye(n, c):
-        vs(b(n), b("IF", S_[0:128]), col["p"], A.is_equal, c, A.mult)
-
-    def blk(n, c):
-        vs(b(n), b("JG", S_[0:128]), col["g"], A.is_equal, c, A.mult)
-
-    def b8(n, c):
-        vs(b(n), b("IF", S_[0:8]), col["g"], A.is_equal, c, A.mult)
-    blk("Blk", 1.0)
-    vs(b("km"), b("IF", S_[0:16]), col["q"], A.is_equal)
-    for k in range(16):
-        act(b("EK", S_[128 * k:128 * k + 128]), b("Blk"), F.Copy, scale=b("km", S_[k:k + 1]))
-    eye("I", 1.0)
-    vs(b("HL", S_[0:128]), b("raw"), 2048.0, A.add)
-    vt(b("rawd"), b("raw"), b("HL", S_[0:128]), A.subtract)
-    vs(b("HL", S_[128:256]), b("rawd"), 2048.0, A.add)
-    ms(b("tab0"), 0.0)
-    send(b("HL"), [(1, "la1", "a1"), (2, "la2", "a2")], NE)
-    send(b("HL"), [(4, "la4", "a4"), (3, "la3", "a3")], NE)
-    send(b("HL"), [(6, "la6", "a6")], NE)
-    for d in DEL:
-        arrives("la%d" % d, "a%d" % d, NE)
-    for t in NEXT:
-        for d in NEXT[t]:
-            arrives("lb%d%d" % (t, d), "b%d%d" % (t, d), NE)
-
-    def expand(n, src):
-        o = [bp(n, S_[h:128:16], S_[:]) for h in (0, 1)]
-        waits("y", need("y", [b(src)], [o[0]]))
-        for h in (0, 1):
-            s = "d%d" % ndma[0]
-            ndma[0] += 1
-            cnt[s] = 16
-            g.sync.dma_start(ap(o[h]), ap(b(src, S_[128 * h:128 * h + 128]))).then_inc(T.sem[s], 16)
-            hist[(s, 16)] = dict(clk["y"])
-            note(R, b(src), s, 16)
-            note(W, o[h], s, 16)
-    expand("tab0", "HL")
-    vs(b("KSc", S_[0:143]), b("IF", S_[0:143]), col["g15"], A.is_equal, col["is"], A.mult)
-    for d in (1, 2):
-        ms(b("tab%d" % d), 0.0)
-    expand("tab1", "la1")
-    expand("tab2", "la2")
-    vs(col["w"], col["po"], -2.0, A.mult, 1.0, A.add)
-    vs(col["po2"], col["po"], 2048.0, A.mult)
-    for n, o, c in (("nI", "I", -1.0), ("I16", "I", 16.0), ("I256", "I", 256.0), ("I32", "I", 1.0), ("Iw", "I", col["w"]), ("Ip32", "I", col["po"]), ("Blk32", "Blk", 1.0),
-                    ("B4096", "Blk", 4096.0), ("BlkC", "Blk", col["is"])):
-        act(b(n), b(o), F.Copy, scale=c)
-    for n, c in (("Blk8", 1.0), ("Blk8c", col["is"]), ("B8h", 0.5), ("B8nh", -0.5)):
-        b8(n, c)
-
-    def hl_v(t):
-        act(b("vR"), b("vG%d" % t), bias=2048.0)
-        act(b("vU"), b("vG%d" % t), bias=2048.0)
-        mm(b("k4", S_[0:8]), b("Iw"), b("vR"), True, False)
-        mm(b("k4", S_[0:8]), b("Ip32"), b("vU"), False, True)
-        act(b("vHL%d" % t), b("k4", S_[0:8]))
-
-    def vals(t):
-        iota(b("VV"), [[8, 256], [0, 16]], t, 0)
-
-    def wrap(bank, src, lo, hi):
-        bk = b(bank, S_[lo // 32:hi // 32])
-        for q in range(16):
-            mm(bk, b("KSc", S_[15 - q:143 - q]), b(src, S_[16 * lo + q:16 * hi:16]), q == 0, q == 15)
-
-    def unwrap(bank, out, lo, hi):
-        vs(b(out, S_[lo:hi]), b(bank, S_[lo // 32:hi // 32]), -2048.0, A.add)
+    def send(src, items, lat):
+        def fn():
+            tr, k = [], 0
+            for d, dst, sem in items:
+                to = T.cores[(rank - d) % N]
+                rid, pid = topo.addr(to)[:2]
+                es = topo.engines(core, to)[k:k + NE]
+                k += NE
+                tr.append(RemoteDMATransfer(dst_ids=[DstId(rid=rid, pnc=pid)], dma_engine_mask=sum(1 << e for e in es), remote_sem=T.sem[sem], src=ap(src), dst=T[dst][:], alu_op=0))
+                nls[0] += NE
+            g.remote_dma_fused(tr, local_sem=T.sem.ls)
+        j = op("g", fn, [src], [], 0.6, sem="")
+        for d, dst, sem in items:
+            op("", None, [], [b(dst)], lat, sem=sem, amt=NE, after=(j,))
 
     def gath(e, out, w, o):
         if e == "s":
@@ -311,403 +293,369 @@ def rank_program(g, core, T, topo):
         else:
             vc(out, ind(w, o))
 
-    def c1(s, h, e):
-        gath(e, b("T1", S_[1024 * h:1024 * h + 1024]), b("tab%d" % s, S_[:]), b("off0", S_[64 * h:64 * h + 64]))
-
-    def c2(u, h, e):
-        gath(e, b("DT", S_[1024 * h:1024 * h + 1024]), b("tab%d" % u, S_[:]), b("off1", S_[64 * h:64 * h + 64]))
-
-    def gather_d(lo, hi, e):
-        gath(e, b("dR", S_[16 * lo:16 * hi]), b("DT", S_[:]), b("a16", S_[lo:hi]))
-
-    def gather_x(h):
-        gath("s", b("xk", S_[2048 * h:2048 * h + 2048]), b("X", S_[:]), b("a16", S_[128 * h:128 * h + 128]))
-
-    def sk_piece(t, j):
-        w = b("O", S_[0:2048]) if t else b("holI", S_[:])
-        vt(b("sk", S_[512 * j:512 * j + 512]), ind(w, b("a16", S_[32 * j:32 * j + 32])), b("VV", S_[512 * j:512 * j + 512]), A.is_equal)
-
-    def xv_mm(t):
-        for k in (0, 1):
-            mm(b("k0", S_[k::2]), b("I"), b("X", S_[t:2048:8]), True, True)
-
-    def min_v(p):
-        vt(b("mR", S_[512 * p:512 * p + 512]), b("xk", S_[p::8]), b("k0"), A.min)
-
-    def min_s(t, p):
-        bk = "k1" if p % 2 else "k2"
-        mm(b(bk), b("I"), b("xk", S_[p::8]), True, False)
-        for kk in (0, 1):
-            mm(b(bk, full, S_[kk::2]), b("nI"), b("X", S_[t:2048:8]), False, kk)
-        act(b("mR", S_[512 * p:512 * p + 512]), b(bk), F.Abs)
-
-    def m_mm(t, p):
-        for k in (p, p + 8):
-            for h in (0, 1):
-                l = b("mR", S_[512 * p + 256 * h + k // 8:512 * p + 256 * h + 256:2])
-                for o in ((k, k + 16) if k < 8 else (k,)):
-                    out = b("k5", S_[8 * h:8 * h + 8], o)
-                    if p < NV["min"]:
-                        mm(out, l, b("Blk8"), True, True)
-                    else:
-                        mm(out, b("xk", S_[2048 * h + k:2048 * h + 2048:16]), b("B8h"), True, False)
-                        mm(out, b("X", S_[1024 * h + t:1024 * h + 1024:8]), b("B8h"), False, False)
-                        mm(out, l, b("B8nh"), False, True)
-
-    def spread_max(src, least, mid=None):
-        mm(bp("k1", S_[0:16], S_[0:4]), b(src, S_[15::16]), b("I32"), True, True)
-        vs(bp("mx16", S_[0:16], S_[:]), bp("k1", S_[0:16], S_[0:4], full), least, A.max)
-        if mid:
-            mid()
-        for h in (0, 1):
-            mm(b("k2", S_[4 * h:4 * h + 4]), bp("E1", S_[0:16], S_[128 * h:128 * h + 128]), bp("mx16", S_[0:16], S_[:]), True, True)
-
-    rest = b("k7", S_[256:512])
-
-    def sellers(t):
-        vt(rest, b("O", S_[t:2048:8]), rest, A.mult)
-        vt(b("O", S_[t:2048:8]), b("sb"), rest, A.add)
-
-    ms(b("fm", full, S_[0:NV["far"]]), 16.0)
-    ms(b("fm", full, S_[NV["far"]:8]), 0.0)
-    ms(b("zer"), 0.0)
-    ms(b("o16"), 1.0 / 16)
-    ms(b("Z"), 9.0)
-    ms(b("O", S_[2048:2304]), 0.0)
-    vs(b("dumW"), b("IF", S_[0:16]), 16.0, A.mult, col["q"], A.add)
-    vt(b("BlkV"), b("Blk"), b("fm"), A.mult)
-    vs(b("dumW"), b("dumW"), 2048.0, A.add)
-    vc(b("a16"), b("holI", S_[0:2048:8]))
-    wrap("k3", "tab0", 0, 128)
-    gather_x(0)
-    unwrap("k3", "off0", 0, 128)
-    vals(0)
+    full = S_[:]
+    H = (0, 1)
+    dma(b("raw"), ("ctl", full), 2.2)
+    dma(b("holI"), ("hol", full), 6.0)
+    dma(b("X"), ("sha", full), 6.0, "s")
+    vc(b("rawf"), b("raw"))
+    vc(b("rawh"), b("raw"))
+    send(b("rawf"), [(1, "la1", "a1"), (2, "la2", "a2")], PAR["arr0"])
+    send(b("rawf"), [(4, "la4", "a4"), (3, "la3", "a3")], PAR["arr0"])
+    send(b("rawf"), [(6, "la6", "a6")], PAR["arr0"])
+    iota(b("pi"), [[0, 1]], 0, 1)
+    iota(b("IF"), [[1, 144]], 0, 0)
+    iota(b("JG"), [[1, 8], [0, 16]], 0, 0)
+    iota(b("JM"), [[0, 16], [1, 16]], 0, 0)
+    iota(b("k15"), [[0, 8], [-1, 16]], 15, 0)
+    iota(b("kc"), [[0, 8], [-1, 16]], 31, 0)
+    iota(b("ID"), [[1, 2048]], 0, 0)
     for t in range(RO):
         iota(b("vG%d" % t), [[8, 256]], t, 0)
-    iota(b("JM3"), [[0, 16], [1, 16]], 0, 0)
-    iota(b("k15"), [[0, 16], [-1, 16]], 15, 0)
-    for n, c in (("B8s", 1.0 / 16), ("B816", 16.0), ("B8n32", -32.0)):
-        b8(n, c)
-    vs(b("rst"), b("JM"), 0.0, A.is_gt)
-    vs(b("maskW"), b("JM"), col["q"], A.is_equal)
-    vs(b("kc"), b("JM"), -1.0, A.mult, 31.0, A.add)
-    vs(b("E1"), b("JG"), col["p"], A.is_equal)
-    vs(b("dumG"), b("IF"), 2048.0, A.add)
-    c1(1, 0, "s")
-    c1(1, 1, "v")
-    for j in range(3):
+    col = {n: b("cols", S_[j:j + 1]) for j, n in enumerate(("p", "q", "g", "g15", "q0", "p15", "q8"))}
+    vs(b("qi"), b("pi"), 15, A.bitwise_and)
+    vc(col["p"], b("pi"))
+    vc(col["q"], b("qi"))
+    vt(col["g15"], b("pi"), b("qi"), A.subtract)
+    vs(col["g"], col["g15"], 1.0 / 16, A.mult)
+    vs(col["q0"], col["q"], 1.0, A.is_lt)
+    vs(col["g15"], col["g15"], 15.0, A.add)
+    vs(col["p15"], col["p"], 16.0, A.mult, 15.0, A.add)
+    vs(col["q8"], col["q"], 8.0, A.mult)
+    vs(b("Blk"), b("JG"), col["g"], A.is_equal)
+    vs(b("km"), b("IF", S_[0:16]), col["q"], A.is_equal)
+    vs(b("I"), b("IF", S_[0:128]), col["p"], A.is_equal)
+    vs(b("KSa"), b("IF"), col["g15"], A.is_equal)
+    vs(b("KS8"), b("IF"), col["p15"], A.is_equal)
+    act(b("KS0"), b("KSa"), F.Copy, scale=col["q0"])
+    for k in range(16):
+        act(b("EK", S_[128 * k:128 * k + 128]), b("Blk"), F.Copy, scale=b("km", S_[k:k + 1]))
+    for n, c in (("I16", 16.0), ("I256", 256.0), ("I5", 1.0 / 32), ("nIU", -U), ("I32", 1.0), ("nI32", -1.0)):
+        act(b(n), b("I"), F.Copy, scale=c)
+    for n, c in (("Blk8", 1.0), ("Blk8c", col["q0"]), ("B816", 16.0), ("B8n32", -32.0)):
+        vs(b(n), b("IF", S_[0:8]), col["g"], A.is_equal, c, A.mult)
+    ms(b("lift"), 3840.0)
+    vs(b("rst"), b("JM", S_[0:8]), 0.0, A.is_gt)
+    ms(b("zer"), 0.0)
+    ms(b("one32"), 1.0)
+    ms(b("thr", S_[0:1]), 1.0)
+    ms(b("O", S_[2048:2304]), 0.0)
+    vs(b("tri"), b("JM"), col["q"], A.is_gt)
+    vs(b("dumW"), b("IF", S_[0:16]), 16.0, A.mult, col["q"], A.add)
+    vs(b("vW", S_[0:16]), b("IF", S_[0:16]), 128.0, A.mult, col["q8"], A.add)
+    for t in (1, 2):
+        vs(b("vW", S_[16 * t:16 * t + 16]), b("vW", S_[0:16]), float(t), A.add)
+    for d in DEL:
+        for j in range(2):
+            if d in HOPS[0]:
+                ms(b("tab%d" % d, S_[1024 * j:1024 * j + 1024]), 0.0)
+            else:
+                iota(b("tab%d" % d, S_[1024 * j:1024 * j + 1024]), [[0, 1024]], 0, 0)
+        dma(bp("tab%d" % d, S_[0:128:16], full), b("la%d" % d), 2.0)
+    dma(bp("C8", S_[0:8], full), b("rawh"), 2.0)
+    dma(bp("ycS", S_[0:128:16], full), b("rawf"), 2.0)
+    gr = group()
+    for q in range(16):
+        mm(b("k0", S_[0:4]), bp("KS8", S_[0:8], S_[15 - q:143 - q]), bp("C8", S_[0:8], full, S_[8 * q:8 * q + 8]), gr)
+    for e in range(8):
+        vc(b("off0", S_[16 * e:16 * e + 16]), b("k0", S_[0:4], S_[e::8]))
+    for j in range(4):
         vc(b("O", S_[512 * j:512 * j + 512]), b("holI", S_[512 * j:512 * j + 512]))
-    gather_x(1)
-    for h in (1, 0):
-        wrap("k3", "T1", 64 * h, 64 * h + 64)
-    xv_mm(0)
-    for h in (1, 0):
-        unwrap("k3", "off1", 64 * h, 64 * h + 64)
-        c2(2, h, "v")
-    gather_d(0, 128, "s")
-    gather_d(128, 256, "v")
-    vt(b("aD"), b("holI", S_[0:2048:8]), b("dumG"), A.subtract)
-    fills.append(lambda: vs(b("tri"), b("JM3"), col["q"], A.is_gt))
-    for j in range(3, 4):
-        fills.append(lambda j=j: vc(b("O", S_[512 * j:512 * j + 512]), b("holI", S_[512 * j:512 * j + 512])))
-    for d in (4, 3, 6):
-        dma(b("tab%d" % d), b("tab0"))
-        expand("tab%d" % d, "la%d" % d)
 
+    def wrap(out, src, gr):
+        for q in range(16):
+            mm(out, b("KSa", S_[15 - q:143 - q]), b(src, S_[q:256:16]), gr)
+
+    def chase(t):
+        s, u = HOPS[t]
+        for h in H:
+            gath(PAR["c1" if t else "c10"][h], b("T1", S_[1024 * h:1024 * h + 1024]), b("tab%d" % s, full), b("off0", S_[64 * h:64 * h + 64]))
+        for h in H:
+            bk, gr = b("k%d" % h, S_[0:2]), group()
+            for q in sorted(range(16), key=lambda q: q % 8):
+                o = 256 * (q % 8) + q // 8 + 128 * h
+                mm(bk, b("KS0", S_[15 - q:143 - q]), b("T1", S_[o:o + 127:2]), gr)
+            vc(b("off1", S_[64 * h:64 * h + 64]), bk)
+            gath(PAR["c2" if t else "c20"][h], b("DT", S_[1024 * h:1024 * h + 1024]), b("tab%d" % u, full), b("off1", S_[64 * h:64 * h + 64]))
+
+    feed = [0]
+
+    def sbank():
+        feed[0] += 1
+        return "k%d" % (feed[0] % 2)
+
+    def lanes(n, h):
+        return b(n, S_[128 * h:128 * h + 128])
+
+    def block(n, h, j):
+        return b(n, S_[2048 * h + j:2048 * h + 2048:4])
+
+    def done(n, h, j):
+        return b(n, S_[2048 * h + 512 * j:2048 * h + 512 * j + 512])
+
+    def row(n, h, k):
+        return b(n, S_[2048 * h + k:2048 * h + 2048:16])
+
+    def drow(n, h, k):
+        o = 2048 * h + 512 * (k % 4)
+        return b(n, S_[o + k // 4:o + 512:4])
+
+    def four(h, src):
+        for u in range(4):
+            mm(b("k%d" % (2 + h), full, S_[u::4]), b("I"), src)
+
+    def top(h):
+        K = "k%d" % (6 + h)
+        back = slice(128 * h + 127, 128 * h - 1 if h else None, -1)
+        scan(lanes("run", h), b("rst"), b(K, S_[0:128]), A.mult, A.max)
+        scan(b("mxB", back), b("rst"), b("run", back), A.mult, A.max)
+        vt(lanes("hotL", h), lanes("mxB", h), b(K, S_[0:128]), A.is_equal)
+        mm(b(K, S_[128:256]), lanes("hotL", h), b("I"))
+        return b(K, S_[128:256])
+
+    chase(0)
     for t in range(RO):
+        src = "O" if t else "holI"
+        Ot = b("O", S_[t:2048:8])
+        nk = PAR["sk"]
+        for j in range(4):
+            iota(b("VV", S_[1024 * j:1024 * j + 1024]), [[8, 64], [0, 16]], t + 512 * j, 0)
+        for h in H:
+            vc(lanes("a16", h), b(src, S_[1024 * h + t:1024 * h + 1024:8]))
+        for j in range(4):
+            for n, w, key in (("xk", "X", "gx"), ("dR", "DT", "gd")):
+                gath(PAR[key if t else key + "0"][j], b(n, S_[1024 * j:1024 * j + 1024]), b(w, full), b("a16", S_[64 * j:64 * j + 64]))
         if t:
-            gather_x(0)
-            gather_x(1)
-            gather_d(NV["d"], 256, "v")
-            sellers(t - 1)
-            gather_d(0, NV["d"], "s")
-            xv_mm(t)
-            vs(b("Z"), b("cnp"), 9.0, A.add)
-            for j in range(NV["sk"]):
-                sk_piece(t, j)
-            vt(b("aD"), b("O", S_[t:2048:8]), b("dumG"), A.subtract)
-        fills[0:0] = [lambda j=j, t=t: sk_piece(t, j) for j in range(NV["sk"] if t else 0, 8)]
-        for p in range(NV["min"]):
-            min_v(p)
-        if t:
-            fill(NV["sk2"])
-        for p in range(NV["min"], 8):
-            min_s(t, p)
-
-        def c_mm(h):
+            sellers()
+        for j in range(nk):
+            w = 4096 // nk
+            vt(b("sk", S_[w * j:w * j + w]), ind(b(src, S_[0:2048]), b("a16", S_[w // 16 * j:w // 16 * (j + 1)])), b("VV", S_[w * j:w * j + w]), A.is_equal)
+        act(b("aD"), Ot, bias=-2048.0)
+        for h in H:
+            Ah, Kh = "k%d" % (4 + h), "k%d" % (6 + h)
+            four(h, b("X", S_[1024 * h + t:1024 * h + 1024:8]))
+            for j in range(4):
+                vt(done("mR", h, j), block("xk", h, j), b("k%d" % (2 + h)), A.min)
             for k in range(16):
-                mm(b("k4", S_[8 * h:8 * h + 8], k), b("dR", S_[2048 * h + k:2048 * h + 2048:16]), b("Blk8c"), True, True)
-        for p in range(8):
-            if p == NV["c0"]:
-                c_mm(0)
-            if p == NV["c1"]:
-                c_mm(1)
-            m_mm(t, p)
-        act(b("md"), b("k5", full, S_[0:24]))
-        c4 = b("k4", full, S_[0:16])
-        vc(b("cd", full, S_[0:16]), c4)
-        vc(b("cd", full, S_[16:24]), b("k4", full, S_[0:8]))
-        pool = b("k6", full, S_[0:16])
-        mm(pool, b("I"), b("k15"), True, False)
-        mm(pool, b("I16"), b("md", full, S_[0:16]), False, False)
-        back = [(1, s) for s in range(1, 9 - NA)] + [x for s in range(9 - NA, 9) for x in ((1, s), (0, s)) if x != (1, 8)]
-        for s in range(1, 9):
-            eq = b("EQ", S_[16 * s - 16:16 * s], full)
-            vt(eq, b("cd", full, S_[s:s + 16]), c4, A.is_equal)
-            for j, (way, r) in enumerate(back):
-                if r != s:
-                    continue
-                bank = "k1" if j // 2 % 2 == 0 else "k2"
-                reg = b(bank, full, S_[16 * (j % 2):16 * (j % 2) + 16])
-                mm(reg, b("I256"), eq, True, False)
-                mm(reg, b("I"), b("md", full, S_[0:16] if way else S_[s:s + 16]), False, True)
-                if j % 2:
-                    act(b("PB", S_[8 * j - 8:8 * j + 8], full), b(bank, full, full), F.Relu, bias=-256.0)
-        act(b("cS"), c4)
+                for o in ((k, k + 16) if k < 8 else (k,)):
+                    mm(b(Ah, S_[0:8], o), row("dR", h, k), b("Blk8c"))
+                for o in (k, k + 16):
+                    mm(b(Ah, S_[8:16], o), drow("mR", h, k), b("Blk8"))
+            zm = S_[8 * h:8 * h + 8]
+            act(lanes("cS", h), b(Ah, S_[0:8], S_[0:16]))
+            act(b("cm", zm), b(Ah, S_[8:16]))
+            mm(b(Kh, S_[128:256]), lanes("cS", h), b("I"))
+            act(lanes("cK", h), b(Kh, S_[128:256]))
+            key, gr = b(Kh, S_[0:128]), group()
+            mm(key, b("I"), b("k15"), gr)
+            mm(key, b("I16"), b("cm", zm, S_[0:16]), gr)
 
-        def pool_b(j):
-            way, s = back[j]
-            z, o = S_[16 * (j // 2):16 * (j // 2) + 16], 16 * (j % 2)
-            if way:
-                mm(b("k6", full, S_[s:16]), b("I16"), b("PB", z, S_[o:o + 16 - s]), False, False)
-                mm(b("k6", full, S_[0:s]), b("I16"), b("PB", z, S_[o + 16 - s:o + 16]), False, False)
-            else:
-                mm(pool, b("I16"), b("PB", z, S_[o:o + 16]), False, j == len(back) - 1)
-        for s in range(1, 9 - NA):
-            eq = b("EQ", S_[16 * s - 16:16 * s], full)
-            vt(b("PA", S_[16 * s - 16:16 * s], full), eq, b("k5", full, S_[s:s + 16]), A.mult)
-            mm(pool, b("I16"), b("PA", S_[16 * s - 16:16 * s], full), False, False)
-            if s > 1:
-                pool_b(s - 2)
-        for j in range(7 - NA, len(back)):
-            pool_b(j)
-        fill(1)
-        for h in (0, 1):
-            mm(b("k3", S_[4 * h:4 * h + 4]), b("cS", S_[128 * h:128 * h + 128]), b("I32"), True, True)
-        act(b("cK"), b("k3", S_[0:8]), bias=-2048.0)
-        vc(b("keyS"), pool)
-        scan(b("mxS"), b("rst"), b("keyS"), A.mult, A.max)
-        for h in (0, 1):
-            mm(b("k3", S_[8 + 4 * h:12 + 4 * h]), b("keyS", S_[128 * h:128 * h + 128]), b("I32"), True, True)
-        act(b("keyK"), b("k3", S_[8:16]))
-        fl = b("k7", S_[0:256])
-        if t == 1:
-            for d in (3, 6):
-                act(b("tab%d" % d, S_[0:2048:8]), b("lb0%d" % d))
-        fl = b("k7", S_[0:256])
-
-        def far_const():
-            mm(fl, b("I"), b("kc"), True, False)
-            for p in range(NV["far"]):
-                for k in (p, p + 8):
-                    for h in (0, 1):
-                        mm(b("k7", S_[128 * h + k:128 * h + 128:16]), b("xk", S_[2048 * h + k:2048 * h + 2048:16]), b("B816"), False, False)
-        fill(1)
-        spread_max("mxS", 0.0, lambda: fill(1))
-        hl_v(t)
-
-        def stakes(h):
+            def eq(s):
+                return b("EQ", S_[64 * h + 8 * s - 8:64 * h + 8 * s])
+            for s in range(1, 9):
+                vt(eq(s), lanes("cS", h), b(Ah, S_[0:8], S_[s:s + 16]), A.is_equal)
+            nv = PAR["prod"]
+            jobs = [(1, s) for s in range(1, 8)] + [(0, s) for s in range(1, 9 - nv)]
+            jobs.sort(key=lambda z: z[1])
+            feeds = []
+            for c in range(0, len(jobs), 4):
+                bank, part = sbank(), jobs[c:c + 4]
+                for j, (way, s) in enumerate(part):
+                    z, o, g2 = S_[8 * (j // 2):8 * (j // 2) + 8], 16 * (j % 2), group()
+                    mm(b(bank, z, S_[o:o + 16]), b("I"), b("cm", zm, S_[16 - s:32 - s] if way else S_[s:s + 16]), g2)
+                    if way:
+                        mm(b(bank, z, S_[o + s:o + 16]), b("I256"), eq(s) [0:1] + (eq(s)[1] + (S_[0:16 - s],),), g2)
+                        mm(b(bank, z, S_[o:o + s]), b("I256"), eq(s)[0:1] + (eq(s)[1] + (S_[16 - s:16],),), g2)
+                    else:
+                        mm(b(bank, z, S_[o:o + 16]), b("I256"), eq(s), g2)
+                r0, m = 64 * h + 4 * c, len(part)
+                if m == 3:
+                    mm(b(bank, S_[8:16], S_[16:32]), b("I"), b("zer", S_[0:128]))
+                nr, nc = (16 if m > 2 else 8), (32 if m > 1 else 16)
+                act(b("PB", S_[r0:r0 + nr], S_[0:nc]), b(bank, S_[0:nr], S_[0:nc]), F.Relu, bias=-256.0)
+                feeds += [(way, s, S_[r0 + 8 * (j // 2):r0 + 8 * (j // 2) + 8], 16 * (j % 2)) for j, (way, s) in enumerate(part)]
+            for way, s, z, o in feeds:
+                mm(key, b("I16"), b("PB", z, S_[o:o + 16]), gr)
+            for s in range(9 - nv, 9):
+                pa = b("PA", S_[64 * h + 8 * s - 8:64 * h + 8 * s])
+                vt(pa, eq(s), b(Ah, S_[8:16], S_[s:s + 16]), A.mult)
+                mm(key, b("I16"), pa, gr)
+        for h in H:
+            Kh = "k%d" % (6 + h)
+            vt(lanes("ohc", h), lanes("cK", h), top(h), A.mult)
+            mm(b(Kh, S_[256:384]), b("Blk"), lanes("ohc", h))
+            vt(lanes("mine", h), lanes("cK", h), b(Kh, S_[256:384]), A.is_equal)
+            if PAR["win"]:
+                act(lanes("w1", h), lanes("mine", h), scale=2.0, bias=-1.0)
+        bW, vW = b("k2", 0, S_[0:16]), b("vW", S_[16 * t:16 * t + 16])
+        wrap(bW, "ohc", group())
+        vc(b("bo"), bW)
+        vt(b("dbv"), bW, vW, A.subtract)
+        act(b("xb"), ind(b("X", full), b("bo")))
+        for h in H:
+            Ah = "k%d" % (4 + h)
             for k in range(16):
-                mm(b("k6", S_[8 + 4 * h:12 + 4 * h], S_[k::16]), b("sk", S_[2048 * h + k:2048 * h + 2048:16]), b("B8s"), True, True)
-        hot = b("k1", S_[8:16])
-        vt(hot, b("keyK"), b("k2", S_[0:8]), A.is_equal)
-        vt(b("ohc"), b("cK"), hot, A.mult)
-        bG = b("k0", S_[0:256])
-        mm(bG, b("Blk32"), b("ohc"), True, True)
-        far_const()
-        fill(1)
-        vt(b("mine"), b("cK"), bG, A.is_equal)
-        vs(b("w1"), b("mine"), 2.0, A.mult, -1.0, A.add)
-        act(b("w16"), b("mine"), scale=32.0, bias=-16.0)
-        vt(b("bw"), bG, b("maskW"), A.mult)
-        scan(b("bws"), b("rst"), b("bw"), A.mult, A.add)
-        vc(b("bo"), b("bws", S_[15::16]))
-        dps = b("k5", S_[0:8])
-        first = [True]
-        nv, ns_ = [0], [0]
-
-        def vbank():
-            nv[0] += 1
-            return "k1" if nv[0] % 2 else "k2"
-
-        def sbank():
-            ns_[0] += 1
-            return "k4" if ns_[0] % 2 else "k3"
-
-        def win_feed(p):
-            vec = p < NV["win"]
-            bk = vbank() if vec else sbank()
-            if not vec:
-                mm(b(bk), b("I"), b("xk", S_[p::8]), True, False)
-            for kk in (0, 1):
-                k = p + 8 * kk
-                mm(b(bk, full, S_[kk::2]), b("EK", S_[128 * k:128 * k + 128]), b("w1" if vec else "w16"), vec, vec or kk)
-            o = b("pR", S_[512 * p:512 * p + 512])
-            if vec:
-                vt(o, b("xk", S_[p::8]), b(bk), A.mult)
-            else:
-                act(o, b(bk), F.Abs)
-
-        def win_acc(p, last):
-            for kk in (0, 1):
-                mm(dps, b("I"), b("pR", S_[512 * p + kk:512 * p + 512:2]), first[0], last and kk)
-                first[0] = False
-
-        def mix(nv_):
-            vps, sps = list(range(nv_)), list(range(nv_, 8))
-            out = []
-            for j in range(8):
-                out += vps[j:j + 1] + sps[j:j + 1]
-            return out
-        order = mix(NV["win"])
-        for p in order[:2]:
-            win_feed(p)
-        fill(99)
-        for p in order[2:4]:
-            win_feed(p)
-        act(b("xb"), ind(b("X", S_[:]), b("bo")))
-        hd = b("k0", S_[256:512])
-        act(b("hR"), bG, bias=2048.0)
-        act(b("hU"), bG, bias=col["po2"], scale=col["po"])
-        act(b("bU"), bG)
-        stakes(0)
-        for j, p in enumerate(order):
-            if j == 2:
-                mm(hd, b("Iw"), b("hR"), True, False)
-                mm(hd, b("nI"), b("vHL%d" % t), False, True)
-            win_acc(p, j == 7)
-            if j + 4 < 8:
-                win_feed(order[j + 4])
-        for kk in (0, 1):
-            mm(b("k2", full, S_[kk::2]), b("I"), b("xb"), True, True)
-        for h in (0, 1):
-            mm(b("k7", S_[128 * h:128 * h + 128]), b("xb", S_[128 * h:128 * h + 128]), b("BlkV"), False, False)
-        forder = mix(NV["far"])
-
-        def far_feed(p):
-            o = b("mR", S_[512 * p:512 * p + 512])
-            if p < NV["far"]:
-                vt(o, b("xk", S_[p::8]), b("k2"), A.min)
-            else:
-                bk = sbank()
-                mm(b(bk), b("I"), b("xk", S_[p::8]), True, False)
-                for kk in (0, 1):
-                    mm(b(bk, full, S_[kk::2]), b("nI"), b("xb"), False, kk)
-                act(o, b(bk), F.Abs)
-
-        def far_acc(p, last):
-            for k in (p, p + 8):
-                for h in (0, 1):
-                    mm(b("k7", S_[128 * h + k:128 * h + 128:16]), b("mR", S_[512 * p + 256 * h + k // 8:512 * p + 256 * h + 256:2]),
-                       b("B8n32" if p < NV["far"] else "B816"), False, last and k > 7 and h)
-        vs(b("gt"), dps, 32.0 * (8 - NV["win"]), A.is_gt)
-        for p in forder[:2]:
-            far_feed(p)
-        for h in (0, 1):
-            mm(b("k1", S_[4 * h:4 * h + 4]), b("gt", S_[128 * h:128 * h + 128]), b("Blk"), True, True)
-        mm(b("k1", S_[8:16]), b("Blk"), b("gt"), True, True)
-        far_feed(forder[2])
-        stakes(1)
-        act(b("st"), b("k6", S_[8:16]), F.Sign)
-        mm(b("k6", S_[0:8]), b("zer", S_[0:128]), b("zer"), True, False)
-        for h in (0, 1):
-            mm(b("k6", S_[4 * h:4 * h + 4]), b("mine", S_[128 * h:128 * h + 128]), b("nI"), False, False)
-        vs(b("wl"), b("k1", S_[0:8]), b("Z"), A.is_ge)
-        mm(b("k6", S_[0:8]), b("I"), b("st"), False, False)
-        mm(b("k6", S_[0:8]), b("I"), b("wl"), False, True)
-        act(b("elw"), b("k6", S_[0:8]), F.Relu, bias=-1.0)
-        vt(hd, b("hU"), hd, A.add)
-        vs(b("winG"), b("k1", S_[8:16]), b("Z"), A.is_ge)
-        vt(hd, b("winG"), hd, A.mult)
-        CN = "CN%d" % t
-        vt(b(CN), b("vHL%d" % t), hd, A.add)
+                mm(b(Ah, S_[8:12], S_[k::16]), row("sk", h, k), b("Blk8"))
+            act(lanes("st", h), b(Ah, S_[8:12]), F.Relu, bias=1.0, scale=-1.0)
+            for j in range(4):
+                if j < PAR["win"]:
+                    bank = "k3"
+                    for u in range(4):
+                        k = j + 4 * u
+                        mm(b(bank, full, S_[u::4]), b("EK", S_[128 * k:128 * k + 128]), lanes("w1", h))
+                    vt(done("pR", h, j), block("xk", h, j), b(bank), A.mult)
+                else:
+                    bank, gr = sbank(), group()
+                    mm(b(bank), b("I5"), block("xk", h, j), gr)
+                    for u in range(4):
+                        k = j + 4 * u
+                        mm(b(bank, full, S_[u::4]), b("EK", S_[128 * k:128 * k + 128]), lanes("mine", h), gr)
+                    act(done("pR", h, j), b(bank), F.Abs, scale=32.0, bias=-16.0)
+            gr = group()
+            for k in range(16):
+                kk = 4 * (k % 4) + k // 4
+                mm(b(Ah, S_[0:4]), b("I"), drow("pR", h, kk), gr)
+            act(lanes("gt", h), b(Ah, S_[0:4]), F.Sign, bias=-64.0 * (4 - PAR["win"]) - 0.5)
+            mm(b(Ah, S_[4:8]), lanes("gt", h), b("Blk"))
+            act(lanes("wl", h), b(Ah, S_[4:8]), F.Relu, bias=b("thr", S_[t:t + 1]), scale=-1.0)
+        cW, nW = b("k4", 12, S_[0:16]), b("nW%d" % t)
+        wrap(cW, "gt", group())
+        vs(b("winW"), cW, b("thr", S_[t:t + 1]), A.is_gt)
+        vt(b("tw"), b("winW"), b("dbv"), A.mult)
+        vt(b("nw"), b("tw"), vW, A.add)
+        vc(nW, b("nw"))
+        act(b("ycS", S_[t:2048:8]), ind(b("ID", full), nW))
         if t in NEXT:
             ds = NEXT[t]
             for j in range(0, len(ds), 2):
-                send(b(CN), [(d, "lb%d%d" % (t, d), "b%d%d" % (t, d)) for d in ds[j:j + 2]], NE)
-            vals(t + 1)
-        vc(b("tab0", S_[t:2048:8]), b(CN))
-        for p in forder[3:6]:
-            far_feed(p)
-        for p in forder[:3]:
-            far_acc(p, False)
-        nxt = t < RO - 1
-        goal = b("k5", full, S_[0:16])
-        if nxt:
-            wrap("k5", "tab0", 0, 128)
-        for p in forder[3:5]:
-            far_acc(p, False)
-        for j in (6, 7):
-            far_feed(forder[j])
-        for j in (5, 6, 7):
-            far_acc(forder[j], j == 7)
-        vt(b("FK"), b("elw"), fl, A.mult)
-        scan(b("fS"), b("rst"), b("FK"), A.mult, A.max)
-        for h in (0, 1):
-            mm(b("k4", S_[4 * h:4 * h + 4]), b("FK", S_[128 * h:128 * h + 128]), b("I32"), True, True)
-        act(b("FKk"), b("k4", S_[0:8]))
-        if nxt:
-            unwrap("k5", "off0", 0, 128)
-            op("v", lambda: v.tensor_reduce(ap(b("cnw")), ap(b("winG")), AxisListType.X, A.add), [b("winG")], [b("cnw")])
-        spread_max("fS", 1.0)
-        if nxt:
-            mm(b("k3", 15, S_[31:32]), b("o16"), b("cnw"), True, True)
-            vc(b("cni"), b("k3", 15, S_[31:32]))
+                send(nW, [(d, "lb%d%d" % (t, d), "b%d%d" % (t, d)) for d in ds[j:j + 2]], PAR["arr"])
+            vc(b("off0", S_[16 * t:16 * t + 16]), b("nw"))
+            for d in ds:
+                act(b("tab%d" % d, S_[t:2048:8]), ind(b("ID", full), b("lb%d%d" % (t, d))))
+            op("v", lambda: v.tensor_reduce(ap(b("cnw")), ap(b("winW")), AxisListType.X, A.add), [b("winW")], [b("cnw")], 0.1)
+            mm(b("k5", 13, S_[0:1]), b("one32"), b("cnw"))
+            vc(b("cni"), b("k5", 13, S_[0:1]))
             vs(b("cnp"), b("cni"), 1, A.bitwise_and)
-            s_, u_ = NEXT[t][0] if t == 0 else 3, NEXT[t][1] if t == 0 else 6
-            for d in (s_, u_):
-                act(b("tab%d" % d, S_[t:2048:8]), b("lb%d%d" % (t, d)))
-        mm(goal, b("I32"), b("dumG"), True, False)
-        vt(hot, b("FKk"), b("k2", S_[0:8]), A.is_equal)
-        vt(b("ga"), b("aD"), hot, A.mult)
-        mm(goal, b("Blk32"), b("ga"), False, True)
-        vt(b("ca"), b("cK"), hot, A.mult)
-        csG = b("k6", S_[0:8])
-        mm(csG, b("Blk32"), b("ca"), True, True)
-        mm(hd, b("I32"), b("vG%d" % t), True, True)
-        vt(b("sb"), b("bU"), hot, A.mult)
-        if nxt:
-            for h in (0, 1):
-                c1(s_, h, "s")
-        vt(b("gw"), goal, b("maskW"), A.mult)
-        scan(b("gws"), b("rst"), b("gw"), A.mult, A.add)
-        vc(b("gSu"), goal)
-        vc(b("go"), b("gws", S_[15::16]))
-        act(b("OG"), ind(b("O", S_[:]), b("go")))
-        act(rest, hot, scale=-1.0, bias=1.0)
-        dup = b("k4", full, S_[0:16])
-        mm(dup, b("I"), b("zer"), True, False)
+            vs(b("thr", S_[t + 1:t + 2]), b("cnp"), 2.0, A.mult, 1.0, A.add)
+        for h in H:
+            Kh = "k%d" % (6 + h)
+            four(h, lanes("xb", h))
+            key, gr = b(Kh, S_[0:128]), group()
+            mm(key, b("I"), b("kc"), gr)
+            mm(key, b("I"), b("lift"), gr)
+            for k in range(16):
+                mm(b(Kh, S_[k:128:16]), row("xk", h, k), b("B816"), gr)
+            mm(key, lanes("mine", h), b("nIU"), gr)
+            mm(key, b("nIU"), lanes("st", h), gr)
+            for j in range(4):
+                vt(done("mR", h, j), block("xk", h, j), b("k%d" % (2 + h)), A.min)
+            for k in range(16):
+                mm(b(Kh, S_[k:128:16]), drow("mR", h, k), b("B8n32"), gr)
+            mm(key, b("nIU"), lanes("wl", h), gr)
+        if t in NEXT:
+            chase(t + 1)
+        for h in H:
+            hot = top(h)
+            vt(lanes("ga", h), lanes("aD", h), hot, A.mult)
+            vt(lanes("ca", h), lanes("cK", h), hot, A.mult)
+            act(lanes("hotS", h), hot)
+        gW, gG, cs, vP, triP = b("k3", 0, S_[0:16]), b("k2", S_[0:8]), b("k2", S_[8:16]), b("k5", S_[0:8]), b("k4", S_[0:8])
+        mm(gG, b("Blk"), b("ga"))
+        wrap(gW, "ga", group())
+        act(b("gS"), gG, bias=2048.0)
+        vs(b("gw"), gW, 2048.0, A.add)
+        vs(b("go"), gW, 2048.0, A.add)
+        act(b("gwh"), gW)
+        act(b("OG"), ind(b("O", full), b("go")))
+        mm(vP, b("I32"), b("vG%d" % t))
+        mm(triP, b("I"), b("tri"))
+        gr = group()
+        mm(cs, b("Blk"), b("ca"), gr)
+        mm(cs, b("nI32"), b("OG"), gr)
+        gr = group()
+        dup = b("k6", S_[0:256])
+        mm(dup, b("I"), b("zer"), gr)
         for c in range(16):
-            vs(b("E3", c, S_[0:256 - 16 * c]), b("gSu", S_[16 * c:256]), b("gws", S_[16 * c + 15:16 * c + 16]), A.is_equal)
+            vs(b("E3", c, S_[0:256 - 16 * c]), b("gS", S_[16 * c:256]), b("gw", S_[c:c + 1]), A.is_equal)
             if c < 15:
-                mm(b("k4", S_[c + 1:16], S_[0:16]), b("B4096"), b("E3", c, S_[16:256 - 16 * c]), False, False)
-            if nxt and c in (1, 6):
-                h = c // 6
-                wrap("k3", "T1", 64 * h, 64 * h + 64)
-            if nxt and c in (13, 15):
-                h = c // 15
-                unwrap("k3", "off1", 64 * h, 64 * h + 64)
-                c2(u_, h, "s")
-        vt(b("E3", full, S_[0:16]), b("E3", full, S_[0:16]), b("tri"), A.mult)
-        mm(dup, b("B4096"), b("E3", full, S_[0:16]), False, True)
-        vt(b("eqv"), b("OG"), hd, A.is_equal)
-        vt(csG, csG, b("OG"), A.subtract)
-        vt(b("tt"), b("eqv"), csG, A.mult)
-        vt(b("dw"), dup, b("maskW"), A.mult)
-        scan(b("dws"), b("rst"), b("dw"), A.mult, A.add)
-        vt(b("t1"), b("dws", S_[15::16]), b("dumW"), A.min)
-        vt(b("t2"), b("t1"), b("gws", S_[15::16]), A.max)
-        vc(b("so"), b("t2"))
-        vt(ind(b("O", S_[:]), b("so")), b("OG"), b("tt"), A.add)
-        if not nxt:
-            break
-        vc(b("a16"), b("O", S_[t + 1:2048:8]))
-    sellers(RO - 1)
-    for j, bk in enumerate(("k1", "k2", "k3", "k4")):
-        mm(b(bk), b("BlkC"), b("tab0", S_[512 * j:512 * j + 512]), True, True)
-        act(b("ycS", S_[512 * j:512 * j + 512]), b(bk), bias=-2048.0)
-    dma(("yo", S_[:]), b("O", S_[0:2048]))
-    dma(("yc", S_[:]), bp("ycS", S_[0:128:16], S_[:]))
+                mm(b("k6", S_[16 * c + 16:256]), b("Blk"), b("E3", c, S_[16:256 - 16 * c]), gr)
+        vt(b("E3", full, S_[0:16]), b("E3", full, S_[0:16]), triP, A.mult)
+        mm(dup, b("Blk"), b("E3", full, S_[0:16]), gr)
+        act(b("dupS"), dup, scale=256.0)
+        dW, gr = b("k3", 1, S_[0:16]), group()
+        mm(dW, b("I"), b("gwh"), gr)
+        wrap(dW, "dupS", gr)
+        vt(b("eqv"), b("OG"), vP, A.is_equal)
+        vt(b("tt"), b("eqv"), cs, A.mult)
+        vt(b("t1"), dW, b("dumW"), A.min)
+        vs(b("so"), b("t1"), 2048.0, A.add)
+        vt(ind(b("O", full), b("so")), b("OG"), b("tt"), A.add)
+
+        def sellers(Ot=Ot):
+            P, gr = b("k7", S_[256:512]), group()
+            mm(P, b("Blk"), b("ohc"), gr)
+            mm(P, b("nI32"), Ot, gr)
+            vt(P, b("hotS"), P, A.mult)
+            vt(Ot, Ot, P, A.add)
+    sellers()
+    dma(("yo", full), b("O", S_[0:2048]), 5.0)
+    dma(("yc", full), bp("ycS", S_[0:128:16], full), 2.0)
+
+    if "order" not in _memo:
+        _memo["order"] = order(ops)
+    cnt, clk, hist, W, R = {}, {q: {} for q in eng}, {}, {}, {}
+
+    def need(q, rd, wr):
+        req = {}
+        own = "q" + q
+
+        def take(tab, x, skip):
+            for s, arr in tab.get(x[0], {}).items():
+                if s == own and skip:
+                    continue
+                n = int(arr.max() if psum(x) and s != own else arr[cols(x)[0]].max())
+                if n > req.get(s, 0):
+                    req[s] = n
+        for x in rd:
+            take(W, x, False)
+            if psum(x):
+                take(R, x, True)
+        for x in wr:
+            take(W, x, True)
+            take(R, x, True)
+        return req
+
+    def note(tab, x, s, n):
+        d = tab.setdefault(x[0], {})
+        if s not in d:
+            d[s] = np.zeros(int(np.prod(SCRATCH[x[0]][1][1:])), np.int64)
+        d[s][cols(x)[0]] = n
+
+    for i in _memo["order"]:
+        o = ops[i]
+        q = o["q"]
+        if q:
+            req = need(q, o["rd"], o["wr"])
+            for s, n in sorted(req.items(), key=lambda z: -len(hist.get(z, ()))):
+                if clk[q].get(s, 0) < n:
+                    eng[q].wait_ge(T.sem[s], n)
+                    clk[q][s] = n
+                    for s2, n2 in hist.get((s, n), {}).items():
+                        clk[q][s2] = max(clk[q].get(s2, 0), n2)
+        if o["sem"] == "":
+            o["fn"]()
+            continue
+        s = o["sem"] or "q" + q
+        cnt[s] = n = cnt.get(s, 0) + o["amt"]
+        if q:
+            o["fn"]().then_inc(T.sem[s], o["amt"])
+            hist[(s, n)] = dict(clk[q])
+            if o["sem"] is None:
+                hist[(s, n)][s] = n
+        for x in o["rd"]:
+            note(R, x, s, n)
+        for x in o["wr"]:
+            note(W, x, s, n)
     for s, n in cnt.items():
         g.wait_ge(T.sem[s], n)
     g.wait_ge(T.sem.ls, nls[0])

@@ -6,30 +6,30 @@ V, D, L, RO, N = 2048, 8, 256, 3, 8
 DEL = (1, 2, 4, 3, 6)
 HOPS = ((1, 2), (2, 4), (3, 6))
 NEXT = {0: (2, 4, 3, 6), 1: (3, 6)}
-PAR = {"prod": 6, "win": 0, "gx": "svsv", "gd": "ssss", "c1": "ss", "c2": "ss", "gx0": "ssss", "gd0": "svsv", "c10": "sv", "c20": "sv",
-       "sk": 16, "look": 1.0, "gat": 1.56, "arr": 3.0, "arr0": 6.0}
+PAR = {"fp": ("012", "012"), "fw": ("01", "01"), "prod": 8, "win": (0, 0), "far": (0, 1), "gx": "svsv", "gd": "ssvs", "conv": "s", "gw": "v", "fill": (1,), "late": 5.0, "c1": "ss", "c2": "ss", "gx0": "svss", "gd0": "svsv", "c10": "sv", "c20": "sv",
+       "sk": 16, "gat": 1.5, "arr": 3.0, "arr0": 6.5, "first": ((1, 2), (4, 3), (6,)), "hop": 0.2, "nv": 0.03, "ns": 0.11, "pe": 0.06, "lean": 0.0, "turns": 3, "mv": "s", "small": "x", "pb": "s", "load": 4.0}
 S_ = np.s_
 U = 8192.0
 
 _bf, _f, _i, _u, _h = "bfloat16", "float32", "int32", "uint16", "float16"
 _shapes = {
     "O": ([2304], _f), "holI": ([2048], _i), "X": ([2048], _bf), "raw": ([128], _i), "rawf": ([128], _f), "rawh": ([128], _h),
-    "C8": ([16, 128], _h), "VV": ([4096], _f), "xk": ([4096], _bf), "sk": ([4096], _bf), "dR": ([4096], _h),
+    "C8": ([16, 128], _h), "VV0": ([4096], _f), "VV1": ([4096], _f), "xk": ([4096], _bf), "sk": ([4096], _bf), "dR": ([4096], _h),
     "mR": ([4096], _bf), "pR": ([4096], _bf), "T1": ([2048], _h), "DT": ([2048], _f), "EK": ([2048], _bf), "ID": ([2048], _f),
     "E3": ([16, 272], _bf), "ycS": ([2048], _f),
     "cS": ([256], _h), "cm": ([16, 32], _h), "EQ": ([128, 16], _bf), "PA": ([128, 16], _bf), "PB": ([128, 32], _bf),
     "off0": ([128], _u), "off1": ([128], _u), "a16": ([256], _u), "bo": ([16], _u), "go": ([16], _u), "so": ([16], _u),
     "run": ([256], _f), "mxB": ([256], _f), "hotL": ([256], _bf), "cK": ([256], _h), "ohc": ([256], _h), "mine": ([256], _bf), "w1": ([256], _bf),
     "xb": ([256], _bf), "gt": ([256], _bf), "wl": ([256], _bf), "st": ([256], _bf), "aD": ([256], _h), "ga": ([256], _h), "ca": ([256], _h),
-    "hotS": ([256], _bf), "gS": ([256], _h), "gw": ([16], _f), "gwh": ([16], _h), "OG": ([256], _f), "eqv": ([256], _bf), "tt": ([256], _f),
-    "dupS": ([256], _bf), "t1": ([16], _f), "dbv": ([16], _f), "winW": ([16], _f), "tw": ([16], _f), "nw": ([16], _f),
-    "cnw": ([1], _f), "cni": ([1], _i), "cnp": ([1], _i), "thr": ([RO], _f),
+    "hotS": ([256], _bf), "gS": ([256], _h), "gw": ([16], _f), "OG": ([256], _f), "eqv": ([256], _bf), "tt": ([256], _f),
+    "dbv": ([16], _f), "winW": ([16], _f), "tw": ([16], _f), "nw": ([16], _f),
+    "cnw": ([1], _f), "cni": ([1], _i), "cnj": ([16], _f), "thr": ([RO], _f),
     "IF": ([144], _f), "JG": ([128], _f), "JM": ([16, 16], _f), "pi": ([1], _i), "qi": ([1], _i), "cols": ([8], _f),
     "I": ([128], _bf), "I16": ([128], _bf), "I256": ([128], _bf), "I5": ([128], _bf), "nIU": ([128], _bf),
     "I32": ([128], _f), "nI32": ([128], _f), "one32": ([128], _f), "Blk": ([128], _bf),
-    "Blk8": ([8], _bf), "Blk8c": ([8], _bf), "B816": ([8], _bf), "B8n32": ([8], _bf),
-    "KSa": ([144], _bf), "KS0": ([144], _bf), "KS8": ([144], _bf), "km": ([16], _f), "rst": ([128], _f), "k15": ([128], _bf),
-    "kc": ([128], _bf), "lift": ([128], _bf), "tri": ([16, 16], _bf), "dumW": ([16], _f), "vW": ([48], _f), "zer": ([256], _bf),
+    "Blk8": ([8], _bf), "twice": ([16], _bf), "twice0": ([16], _bf), "B816": ([8], _bf), "B8n32": ([8], _bf),
+    "KSa": ([144], _bf), "KS0": ([144], _bf), "KS8": ([144], _bf), "km": ([16], _f), "rst": ([256], _f), "k15": ([128], _bf),
+    "kc": ([256], _bf), "LT": ([1920], _bf), "BlkV": ([256], _bf), "nI": ([128], _bf), "tri": ([16], _f), "dumG": ([256], _f), "BlkU": ([128], _bf), "vW": ([48], _f), "zer": ([256], _bf),
 }
 SCRATCH = {n: ("sbuf", [128] + s, d) for n, (s, d) in _shapes.items()}
 for _d in DEL:
@@ -39,11 +39,10 @@ for _t in NEXT:
     for _d in NEXT[_t]:
         SCRATCH["lb%d%d" % (_t, _d)] = ("sbuf", [128, 16], _u)
 for _t in range(RO):
-    SCRATCH["nW%d" % _t] = ("sbuf", [128, 16], _u)
     SCRATCH["vG%d" % _t] = ("sbuf", [128, 256], _f)
 for _k in range(8):
     SCRATCH["k%d" % _k] = ("psum", [128, 16, 32] if _k < 6 else [128, 512], _f)
-SEMAPHORES = ["qv", "qs", "qp", "qg", "ls"] + ["d%d" % k for k in range(16)] + ["a%d" % d for d in DEL] + ["b%d%d" % (t, d) for t in NEXT for d in NEXT[t]]
+SEMAPHORES = ["qv", "qs", "qp", "qg", "ls"] + ["d%d" % k for k in range(20)] + ["a%d" % d for d in DEL] + ["b%d%d" % (t, d) for t in NEXT for d in NEXT[t]]
 _memo = {}
 
 
@@ -130,53 +129,89 @@ def order(ops):
         for j in pre[i]:
             suc[j].append(i)
 
-    def gap(j, i):
-        return ops[j]["lat"] + (0.0 if ops[j]["q"] == ops[i]["q"] else 0.06)
+    hop = PAR["hop"]
+    lat = [o["lat"] for o in ops]
+    ways = [sorted(o["q"].items()) for o in ops]
+    banks = [sorted(set(x[0] for x in o["rd"] + o["wr"] if psum(x))) for o in ops]
+
+    def place(rank, before, after, fwd):
+        left = [len(p) for p in before]
+        ready = sorted((rank[i], i) for i in range(n) if not left[i])
+        beg, end, on = [0.0] * n, [0.0] * n, [""] * n
+        busy, held = {}, {}
+        while ready:
+            i = ready.pop(0)[1]
+            best = None
+            for q, (cost, fn) in ways[i]:
+                t = 0.0 if fwd else lat[i]
+                for j in before[i]:
+                    x, y = (j, i) if fwd else (i, j)
+                    t = max(t, end[j] + (0.0 if x in ops[y]["after"] else lat[x]) + (0.0 if on[j] == q else hop))
+                pad = lat[i] + hop
+                a, z = (0.0, pad) if fwd else (pad, 0.0)
+                moved = bool(q)
+                while moved:
+                    moved = False
+                    lst = busy.setdefault(q, [])
+                    k = seek(lst, t)
+                    while k < len(lst) and lst[k][1] < t + cost - 1e-9:
+                        t = max(t, lst[k][0])
+                        k += 1
+                    for bank in banks[i]:
+                        for q2, l2 in held.setdefault(bank, {}).items():
+                            if q2 != q:
+                                k2 = seek(l2, t - a)
+                                if k2 < len(l2) and l2[k2][1] < t + cost + z - 1e-9:
+                                    t = l2[k2][0] + a
+                                    moved = True
+                score = t + cost + (PAR["lean"] if q == "v" else 0.0)
+                if best is None or score < best[0]:
+                    best = (score, t, q, cost, a, z)
+            score, t, q, cost, a, z = best
+            beg[i], end[i], on[i] = t, t + cost, q
+            if q:
+                lst = busy[q]
+                lst.insert(seek(lst, t), (t + cost, t))
+                for bank in banks[i]:
+                    lst = held[bank].setdefault(q, [])
+                    k = seek(lst, t - a)
+                    lo, hi = t - a, t + cost + z
+                    while k < len(lst) and lst[k][1] <= hi:
+                        e, s = lst.pop(k)
+                        lo, hi = min(lo, s), max(hi, e)
+                    lst.insert(k, (hi, lo))
+            for j in after[i]:
+                left[j] -= 1
+                if not left[j]:
+                    ready.insert(seek(ready, rank[j]), (rank[j], j))
+        return beg, end, on
     way = [0.0] * n
     for i in range(n - 1, -1, -1):
-        way[i] = ops[i]["cost"] + max([way[j] + gap(i, j) for j in suc[i]], default=ops[i]["lat"])
-    left = [len(p) for p in pre]
-    banks = [set(x[0] for x in o["rd"] + o["wr"] if psum(x)) for o in ops]
-    ready, end, at, free, used, out = {}, [0.0] * n, [0.0] * n, {}, {}, []
-    for i in range(n):
-        if not left[i]:
-            ready.setdefault(ops[i]["q"], []).append(i)
+        way[i] = min(c for q, (c, fn) in ways[i]) + lat[i] + max([way[j] + hop for j in suc[i]], default=0.0)
+    rank, best = [-w for w in way], None
+    for _ in range(PAR["turns"]):
+        beg, end, on = place(rank, pre, suc, True)
+        span = max(e + x for e, x in zip(end, lat))
+        if best is None or span < best[0]:
+            best = (span, beg, on)
+        _memo.setdefault("spans", []).append(round(span, 1))
+        rank = [-e for e in place([-e - x for e, x in zip(end, lat)], suc, pre, False)[1]]
+        if PAR.get("noise"):
+            rank = [r + PAR["noise"] * x for r, x in zip(rank, np.random.rand(n))]
+    span, beg, on = best
+    _memo["span"] = span
+    return [(i, on[i]) for i in sorted(range(n), key=lambda i: (beg[i], i))]
 
-    def start(i):
-        q = ops[i]["q"]
-        t = max(at[i], free.get(q, 0.0))
-        for k in banks[i]:
-            for q2, e in used.get(k, {}).items():
-                if q2 != q and e > t:
-                    t = e
-        return t
-    while len(out) < n:
-        best = None
-        for q, lst in ready.items():
-            if lst:
-                st = [(start(i), i) for i in lst]
-                t0 = min(st)[0]
-                if best is None or t0 < best[0]:
-                    best = (t0, q, st)
-        t0, q, st = best
-        x = max((i for s, i in st if s <= t0 + 1e-9), key=lambda i: (way[i], -i))
-        s0 = t0
-        for s, i in st:
-            if way[i] > way[x] and t0 < s and (s - t0) < PAR["look"] * (s0 + ops[x]["cost"] - s):
-                x, s0 = i, s
-        ready[q].remove(x)
-        out.append(x)
-        end[x] = s0 + ops[x]["cost"]
-        if q:
-            free[q] = end[x]
-        for k in banks[x]:
-            used.setdefault(k, {})[q] = end[x] + ops[x]["lat"] + 0.06
-        for j in suc[x]:
-            at[j] = max(at[j], end[x] + gap(x, j))
-            left[j] -= 1
-            if not left[j]:
-                ready.setdefault(ops[j]["q"], []).append(j)
-    return out
+
+def seek(lst, t):
+    lo, hi = 0, len(lst)
+    while lo < hi:
+        mid = (lo + hi) // 2
+        if lst[mid][0] > t + 1e-9:
+            hi = mid
+        else:
+            lo = mid + 1
+    return lo
 
 
 def rank_program(g, core, T, topo):
@@ -201,15 +236,23 @@ def rank_program(g, core, T, topo):
         return [x for x in out if x[0] in SCRATCH]
 
     def op(q, fn, rd, wr, cost, lat=0.0, sem=None, amt=1, grp=None, after=()):
-        ops.append({"q": q, "fn": fn, "rd": parts(rd), "wr": parts(wr), "cost": cost, "lat": lat, "sem": sem, "amt": amt, "grp": grp, "after": after})
+        ops.append({"q": {q: (cost, fn)}, "rd": parts(rd), "wr": parts(wr), "lat": lat, "sem": sem, "amt": amt, "grp": grp, "after": after})
         return len(ops) - 1
+
+    def either(e, on_v, on_s):
+        if e != "s":
+            on_v()
+        if e != "v":
+            on_s()
+        if e not in "vs":
+            ops[-2]["q"].update(ops.pop()["q"])
 
     def span(out, i, rate):
         if out[0] == "ind":
             return 0.05 + 16 * len(cols(out[2])[0]) * 3.8 * CY
         if i[0] == "ind":
             return 0.05 + 16 * len(cols(i[2])[0]) * PAR["gat"] * CY
-        return 0.05 + max(64, len(cols(i)[0]) * rate) * CY
+        return PAR["nv"] + max(64, len(cols(i)[0]) * rate) * CY
 
     def half(*xs):
         return 0.5 if all(x[0] != "ind" and two(x) for x in xs) else 1.0
@@ -240,7 +283,7 @@ def rank_program(g, core, T, topo):
         def fn():
             a = [ap(x) if isinstance(x, tuple) else x for x in (bias, scale)]
             return sc.activation(ap(out), ap(i), f, bias=a[0], scale=a[1])
-        op("s", fn, [i, bias, scale], [out], 0.01 + span(out, i, 1.0))
+        op("s", fn, [i, bias, scale], [out], (0.01 if i[0] == "ind" else PAR["ns"] - PAR["nv"]) + span(out, i, 1.0))
 
     todo = {}
 
@@ -253,7 +296,7 @@ def rank_program(g, core, T, topo):
             todo[grp] -= 1
             return te.matmul(ap(out), ap(l), ap(r), first, todo[grp] == 0)
         cyc = max(min(64, len(cols(l)[0])), len(cols(r)[0])) * (1 if two(l) else 4)
-        op("p", fn, [l, r], [out], cyc * CY / 2, 0.1, grp=grp)
+        op("p", fn, [l, r], [out], cyc * CY / 2, PAR["pe"], grp=grp)
 
     def group():
         return ("grp", len(ops))
@@ -270,9 +313,11 @@ def rank_program(g, core, T, topo):
         op(q, lambda: eng[q].dma_start(ap(out), ap(i)), [i], [out], 0.1, lat, s, 16)
 
     nls = [0]
-    NE = 4
+    sent = []
 
     def send(src, items, lat):
+        NE = 8 // len(items)
+
         def fn():
             tr, k = [], 0
             for d, dst, sem in items:
@@ -283,32 +328,43 @@ def rank_program(g, core, T, topo):
                 tr.append(RemoteDMATransfer(dst_ids=[DstId(rid=rid, pnc=pid)], dma_engine_mask=sum(1 << e for e in es), remote_sem=T.sem[sem], src=ap(src), dst=T[dst][:], alu_op=0))
                 nls[0] += NE
             g.remote_dma_fused(tr, local_sem=T.sem.ls)
-        j = op("g", fn, [src], [], 0.6, sem="")
+        j = op("g", fn, [src], [], 0.4, sem="", after=tuple(sent[-1:]))
+        sent.append(j)
         for d, dst, sem in items:
             op("", None, [], [b(dst)], lat, sem=sem, amt=NE, after=(j,))
 
     def gath(e, out, w, o):
-        if e == "s":
-            act(out, ind(w, o))
-        else:
-            vc(out, ind(w, o))
+        either(e, lambda: vc(out, ind(w, o)), lambda: act(out, ind(w, o)))
+
+    def move(out, i, bias=0.0, floor=False, e=None):
+        either(e or PAR["mv"], lambda: vs(out, i, bias, A.add, 0.0, A.max) if floor else vs(out, i, bias, A.add),
+               lambda: act(out, i, F.Relu if floor else F.Identity, bias=bias))
+
+    def under(out, i, bar):
+        either(PAR["mv"], lambda: vs(out, i, bar, A.is_lt),
+               lambda: act(out, i, F.Relu, bias=bar if isinstance(bar, tuple) else 2 * bar, scale=-1.0))
+
+    def lanes(n, h):
+        return b(n, S_[128 * h:128 * h + 128])
 
     full = S_[:]
     H = (0, 1)
-    dma(b("raw"), ("ctl", full), 2.2)
-    dma(b("holI"), ("hol", full), 6.0)
-    dma(b("X"), ("sha", full), 6.0, "s")
+    dma(b("raw"), ("ctl", full), 1.4)
+    ops[-1]["after"] = ()
+    dma(b("holI"), ("hol", full), PAR["load"])
+    ops[-1]["after"] = (0,)
+    dma(b("X"), ("sha", full), PAR["load"] + 1.5)
+    ops[-1]["after"] = (1,)
     vc(b("rawf"), b("raw"))
     vc(b("rawh"), b("raw"))
-    send(b("rawf"), [(1, "la1", "a1"), (2, "la2", "a2")], PAR["arr0"])
-    send(b("rawf"), [(4, "la4", "a4"), (3, "la3", "a3")], PAR["arr0"])
-    send(b("rawf"), [(6, "la6", "a6")], PAR["arr0"])
+    for j, ds in enumerate(PAR["first"]):
+        send(b("rawf"), [(d, "la%d" % d, "a%d" % d) for d in ds], PAR["arr0"] + 1.5 * j)
     iota(b("pi"), [[0, 1]], 0, 1)
     iota(b("IF"), [[1, 144]], 0, 0)
     iota(b("JG"), [[1, 8], [0, 16]], 0, 0)
     iota(b("JM"), [[0, 16], [1, 16]], 0, 0)
     iota(b("k15"), [[0, 8], [-1, 16]], 15, 0)
-    iota(b("kc"), [[0, 8], [-1, 16]], 31, 0)
+    iota(b("kc"), [[0, 16], [-1, 16]], 31, 0)
     iota(b("ID"), [[1, 2048]], 0, 0)
     for t in range(RO):
         iota(b("vG%d" % t), [[8, 256]], t, 0)
@@ -330,29 +386,41 @@ def rank_program(g, core, T, topo):
     act(b("KS0"), b("KSa"), F.Copy, scale=col["q0"])
     for k in range(16):
         act(b("EK", S_[128 * k:128 * k + 128]), b("Blk"), F.Copy, scale=b("km", S_[k:k + 1]))
-    for n, c in (("I16", 16.0), ("I256", 256.0), ("I5", 1.0 / 32), ("nIU", -U), ("I32", 1.0), ("nI32", -1.0)):
+    for n, c in (("I16", 16.0), ("I256", 256.0), ("I5", 1.0 / 32), ("nIU", -U), ("nI", -1.0), ("I32", 1.0), ("nI32", -1.0)):
         act(b(n), b("I"), F.Copy, scale=c)
-    for n, c in (("Blk8", 1.0), ("Blk8c", col["q0"]), ("B816", 16.0), ("B8n32", -32.0)):
+    vs(b("twice"), b("JG", S_[0:128:8]), col["g"], A.is_equal)
+    vs(b("twice0"), b("JG", S_[0:128:8]), col["g"], A.is_equal, col["q0"], A.mult)
+    for n, c in (("Blk8", 1.0), ("B816", 16.0), ("B8n32", -32.0)):
         vs(b(n), b("IF", S_[0:8]), col["g"], A.is_equal, c, A.mult)
-    ms(b("lift"), 3840.0)
-    vs(b("rst"), b("JM", S_[0:8]), 0.0, A.is_gt)
+    vs(b("rst"), b("JM"), 0.0, A.is_gt)
     ms(b("zer"), 0.0)
     ms(b("one32"), 1.0)
     ms(b("thr", S_[0:1]), 1.0)
     ms(b("O", S_[2048:2304]), 0.0)
-    vs(b("tri"), b("JM"), col["q"], A.is_gt)
-    vs(b("dumW"), b("IF", S_[0:16]), 16.0, A.mult, col["q"], A.add)
+    vs(b("tri"), b("IF", S_[0:16]), col["q"], A.is_gt, U, A.mult)
+    for e in range(1, 16):
+        act(b("LT", S_[128 * e - 128:128 * e]), b("Blk"), F.Copy, scale=b("tri", S_[e:e + 1]))
+    for h in H:
+        act(lanes("BlkV", h), b("Blk"), F.Copy, scale=16.0)
+        for j in range(4 - PAR["far"][h], 4):
+            ms(b("BlkV", S_[128 * h + j:128 * h + 128:4]), 0.0)
+    iota(b("run"), [[1, 256]], 2048, 0)
+    vs(b("mxB"), b("JM"), col["q"], A.is_equal)
+    vt(b("dumG"), b("run"), b("mxB"), A.mult)
+    act(b("BlkU"), b("Blk"), F.Copy, scale=U)
     vs(b("vW", S_[0:16]), b("IF", S_[0:16]), 128.0, A.mult, col["q8"], A.add)
     for t in (1, 2):
         vs(b("vW", S_[16 * t:16 * t + 16]), b("vW", S_[0:16]), float(t), A.add)
     for d in DEL:
         for j in range(2):
-            if d in HOPS[0]:
+            if d in PAR["fill"]:
                 ms(b("tab%d" % d, S_[1024 * j:1024 * j + 1024]), 0.0)
-            else:
+            elif d in HOPS[0]:
                 iota(b("tab%d" % d, S_[1024 * j:1024 * j + 1024]), [[0, 1024]], 0, 0)
+        if d not in HOPS[0]:
+            dma(b("tab%d" % d), b("ID"), 4.0)
         dma(bp("tab%d" % d, S_[0:128:16], full), b("la%d" % d), 2.0)
-    dma(bp("C8", S_[0:8], full), b("rawh"), 2.0)
+    dma(bp("C8", S_[0:8], full), b("rawh"), PAR["late"])
     dma(bp("ycS", S_[0:128:16], full), b("rawf"), 2.0)
     gr = group()
     for q in range(16):
@@ -360,7 +428,7 @@ def rank_program(g, core, T, topo):
     for e in range(8):
         vc(b("off0", S_[16 * e:16 * e + 16]), b("k0", S_[0:4], S_[e::8]))
     for j in range(4):
-        vc(b("O", S_[512 * j:512 * j + 512]), b("holI", S_[512 * j:512 * j + 512]))
+        move(b("O", S_[512 * j:512 * j + 512]), b("holI", S_[512 * j:512 * j + 512]), e=PAR["conv"])
 
     def wrap(out, src, gr):
         for q in range(16):
@@ -368,24 +436,25 @@ def rank_program(g, core, T, topo):
 
     def chase(t):
         s, u = HOPS[t]
-        for h in H:
-            gath(PAR["c1" if t else "c10"][h], b("T1", S_[1024 * h:1024 * h + 1024]), b("tab%d" % s, full), b("off0", S_[64 * h:64 * h + 64]))
+        def pieces(who, out, tab, off, h=None):
+            w = 128 // len(who)
+            for j, e in enumerate(who):
+                if h is None or j * w // 64 == h:
+                    gath(e, b(out, S_[16 * w * j:16 * w * (j + 1)]), b(tab, full), b(off, S_[w * j:w * (j + 1)]))
+        pieces(PAR["c1" if t else "c10"], "T1", "tab%d" % s, "off0")
         for h in H:
             bk, gr = b("k%d" % h, S_[0:2]), group()
             for q in sorted(range(16), key=lambda q: q % 8):
                 o = 256 * (q % 8) + q // 8 + 128 * h
                 mm(bk, b("KS0", S_[15 - q:143 - q]), b("T1", S_[o:o + 127:2]), gr)
             vc(b("off1", S_[64 * h:64 * h + 64]), bk)
-            gath(PAR["c2" if t else "c20"][h], b("DT", S_[1024 * h:1024 * h + 1024]), b("tab%d" % u, full), b("off1", S_[64 * h:64 * h + 64]))
+            pieces(PAR["c2" if t else "c20"], "DT", "tab%d" % u, "off1", h)
 
     feed = [0]
 
-    def sbank():
+    def sbank(among="01"):
         feed[0] += 1
-        return "k%d" % (feed[0] % 2)
-
-    def lanes(n, h):
-        return b(n, S_[128 * h:128 * h + 128])
+        return "k" + among[feed[0] % len(among)]
 
     def block(n, h, j):
         return b(n, S_[2048 * h + j:2048 * h + 2048:4])
@@ -407,8 +476,8 @@ def rank_program(g, core, T, topo):
     def top(h):
         K = "k%d" % (6 + h)
         back = slice(128 * h + 127, 128 * h - 1 if h else None, -1)
-        scan(lanes("run", h), b("rst"), b(K, S_[0:128]), A.mult, A.max)
-        scan(b("mxB", back), b("rst"), b("run", back), A.mult, A.max)
+        scan(lanes("run", h), lanes("rst", 0), b(K, S_[0:128]), A.mult, A.max)
+        scan(b("mxB", back), lanes("rst", 0), b("run", back), A.mult, A.max)
         vt(lanes("hotL", h), lanes("mxB", h), b(K, S_[0:128]), A.is_equal)
         mm(b(K, S_[128:256]), lanes("hotL", h), b("I"))
         return b(K, S_[128:256])
@@ -417,35 +486,37 @@ def rank_program(g, core, T, topo):
     for t in range(RO):
         src = "O" if t else "holI"
         Ot = b("O", S_[t:2048:8])
-        nk = PAR["sk"]
+        nk, VV = PAR["sk"], "VV%d" % (t % 2)
         for j in range(4):
-            iota(b("VV", S_[1024 * j:1024 * j + 1024]), [[8, 64], [0, 16]], t + 512 * j, 0)
+            iota(b(VV, S_[1024 * j:1024 * j + 1024]), [[8, 64], [0, 16]], t + 512 * j, 0)
+            if t == 2:
+                ops[-1]["after"] = (quiet,)
         for h in H:
             vc(lanes("a16", h), b(src, S_[1024 * h + t:1024 * h + 1024:8]))
-        for j in range(4):
-            for n, w, key in (("xk", "X", "gx"), ("dR", "DT", "gd")):
-                gath(PAR[key if t else key + "0"][j], b(n, S_[1024 * j:1024 * j + 1024]), b(w, full), b("a16", S_[64 * j:64 * j + 64]))
+        for n, w, key in (("xk", "X", "gx"), ("dR", "DT", "gd")):
+            who = PAR[key if t else key + "0"]
+            c = 256 // len(who)
+            for j, e in enumerate(who):
+                gath(e, b(n, S_[16 * c * j:16 * c * (j + 1)]), b(w, full), b("a16", S_[c * j:c * (j + 1)]))
         if t:
             sellers()
         for j in range(nk):
             w = 4096 // nk
-            vt(b("sk", S_[w * j:w * j + w]), ind(b(src, S_[0:2048]), b("a16", S_[w // 16 * j:w // 16 * (j + 1)])), b("VV", S_[w * j:w * j + w]), A.is_equal)
-        act(b("aD"), Ot, bias=-2048.0)
+            vt(b("sk", S_[w * j:w * j + w]), ind(b(src, S_[0:2048]), b("a16", S_[w // 16 * j:w // 16 * (j + 1)])), b(VV, S_[w * j:w * j + w]), A.is_equal)
+        move(b("aD"), Ot, -2048.0)
         for h in H:
             Ah, Kh = "k%d" % (4 + h), "k%d" % (6 + h)
             four(h, b("X", S_[1024 * h + t:1024 * h + 1024:8]))
             for j in range(4):
                 vt(done("mR", h, j), block("xk", h, j), b("k%d" % (2 + h)), A.min)
             for k in range(16):
-                for o in ((k, k + 16) if k < 8 else (k,)):
-                    mm(b(Ah, S_[0:8], o), row("dR", h, k), b("Blk8c"))
-                for o in (k, k + 16):
-                    mm(b(Ah, S_[8:16], o), drow("mR", h, k), b("Blk8"))
+                mm(b(Ah, S_[0:8], S_[k::16]), row("dR", h, k), b("twice0"))
+                mm(b(Ah, S_[8:16], S_[k::16]), drow("mR", h, k), b("twice"))
             zm = S_[8 * h:8 * h + 8]
-            act(lanes("cS", h), b(Ah, S_[0:8], S_[0:16]))
-            act(b("cm", zm), b(Ah, S_[8:16]))
+            move(lanes("cS", h), b(Ah, S_[0:8], S_[0:16]))
+            move(b("cm", zm), b(Ah, S_[8:16]))
             mm(b(Kh, S_[128:256]), lanes("cS", h), b("I"))
-            act(lanes("cK", h), b(Kh, S_[128:256]))
+            move(lanes("cK", h), b(Kh, S_[128:256]))
             key, gr = b(Kh, S_[0:128]), group()
             mm(key, b("I"), b("k15"), gr)
             mm(key, b("I16"), b("cm", zm, S_[0:16]), gr)
@@ -459,7 +530,7 @@ def rank_program(g, core, T, topo):
             jobs.sort(key=lambda z: z[1])
             feeds = []
             for c in range(0, len(jobs), 4):
-                bank, part = sbank(), jobs[c:c + 4]
+                bank, part = sbank(PAR["fp"][h]), jobs[c:c + 4]
                 for j, (way, s) in enumerate(part):
                     z, o, g2 = S_[8 * (j // 2):8 * (j // 2) + 8], 16 * (j % 2), group()
                     mm(b(bank, z, S_[o:o + 16]), b("I"), b("cm", zm, S_[16 - s:32 - s] if way else S_[s:s + 16]), g2)
@@ -472,7 +543,7 @@ def rank_program(g, core, T, topo):
                 if m == 3:
                     mm(b(bank, S_[8:16], S_[16:32]), b("I"), b("zer", S_[0:128]))
                 nr, nc = (16 if m > 2 else 8), (32 if m > 1 else 16)
-                act(b("PB", S_[r0:r0 + nr], S_[0:nc]), b(bank, S_[0:nr], S_[0:nc]), F.Relu, bias=-256.0)
+                move(b("PB", S_[r0:r0 + nr], S_[0:nc]), b(bank, S_[0:nr], S_[0:nc]), -256.0, True, PAR["pb"])
                 feeds += [(way, s, S_[r0 + 8 * (j // 2):r0 + 8 * (j // 2) + 8], 16 * (j % 2)) for j, (way, s) in enumerate(part)]
             for way, s, z, o in feeds:
                 mm(key, b("I16"), b("PB", z, S_[o:o + 16]), gr)
@@ -485,27 +556,29 @@ def rank_program(g, core, T, topo):
             vt(lanes("ohc", h), lanes("cK", h), top(h), A.mult)
             mm(b(Kh, S_[256:384]), b("Blk"), lanes("ohc", h))
             vt(lanes("mine", h), lanes("cK", h), b(Kh, S_[256:384]), A.is_equal)
-            if PAR["win"]:
+            if PAR["win"][h]:
                 act(lanes("w1", h), lanes("mine", h), scale=2.0, bias=-1.0)
-        bW, vW = b("k2", 0, S_[0:16]), b("vW", S_[16 * t:16 * t + 16])
-        wrap(bW, "ohc", group())
-        vc(b("bo"), bW)
-        vt(b("dbv"), bW, vW, A.subtract)
-        act(b("xb"), ind(b("X", full), b("bo")))
+            bW, gr, z = b(Kh, S_[384:392]), group(), S_[8 * h:8 * h + 8]
+            for q in range(16):
+                mm(bW, b("KSa", S_[15 - q:143 - q]), b("ohc", S_[128 * h + q:128 * h + 128:16]), gr)
+            vc(b("bo", z), bW)
+            vt(b("dbv", z), bW, b("vW", S_[16 * t + 8 * h:16 * t + 8 * h + 8]), A.subtract)
+            gath(PAR["small"], lanes("xb", h), b("X", full), b("bo", z))
+        vW = b("vW", S_[16 * t:16 * t + 16])
         for h in H:
             Ah = "k%d" % (4 + h)
             for k in range(16):
                 mm(b(Ah, S_[8:12], S_[k::16]), row("sk", h, k), b("Blk8"))
-            act(lanes("st", h), b(Ah, S_[8:12]), F.Relu, bias=1.0, scale=-1.0)
+            under(lanes("st", h), b(Ah, S_[8:12]), 0.5)
             for j in range(4):
-                if j < PAR["win"]:
-                    bank = "k3"
+                if j < PAR["win"][h]:
+                    bank = "k%d" % (2 + j % 2)
                     for u in range(4):
                         k = j + 4 * u
                         mm(b(bank, full, S_[u::4]), b("EK", S_[128 * k:128 * k + 128]), lanes("w1", h))
                     vt(done("pR", h, j), block("xk", h, j), b(bank), A.mult)
                 else:
-                    bank, gr = sbank(), group()
+                    bank, gr = sbank(PAR["fw"][h]), group()
                     mm(b(bank), b("I5"), block("xk", h, j), gr)
                     for u in range(4):
                         k = j + 4 * u
@@ -515,80 +588,91 @@ def rank_program(g, core, T, topo):
             for k in range(16):
                 kk = 4 * (k % 4) + k // 4
                 mm(b(Ah, S_[0:4]), b("I"), drow("pR", h, kk), gr)
-            act(lanes("gt", h), b(Ah, S_[0:4]), F.Sign, bias=-64.0 * (4 - PAR["win"]) - 0.5)
+            act(lanes("gt", h), b(Ah, S_[0:4]), F.Sign, bias=-64.0 * (4 - PAR["win"][h]) - 0.5)
             mm(b(Ah, S_[4:8]), lanes("gt", h), b("Blk"))
-            act(lanes("wl", h), b(Ah, S_[4:8]), F.Relu, bias=b("thr", S_[t:t + 1]), scale=-1.0)
-        cW, nW = b("k4", 12, S_[0:16]), b("nW%d" % t)
+            under(lanes("wl", h), b(Ah, S_[4:8]), b("thr", S_[t:t + 1]))
+        cW, nW = b("k4", 12, S_[0:16]), b("off0", S_[16 * t:16 * t + 16])
         wrap(cW, "gt", group())
         vs(b("winW"), cW, b("thr", S_[t:t + 1]), A.is_gt)
         vt(b("tw"), b("winW"), b("dbv"), A.mult)
         vt(b("nw"), b("tw"), vW, A.add)
         vc(nW, b("nw"))
-        act(b("ycS", S_[t:2048:8]), ind(b("ID", full), nW))
+        gath(PAR["small"], b("ycS", S_[t:2048:8]), b("ID", full), nW)
         if t in NEXT:
             ds = NEXT[t]
-            for j in range(0, len(ds), 2):
-                send(nW, [(d, "lb%d%d" % (t, d), "b%d%d" % (t, d)) for d in ds[j:j + 2]], PAR["arr"])
-            vc(b("off0", S_[16 * t:16 * t + 16]), b("nw"))
+            for j, part in enumerate((ds[0:1], ds[1:2], ds[2:4])):
+                if part:
+                    send(nW, [(d, "lb%d%d" % (t, d), "b%d%d" % (t, d)) for d in part], PAR["arr"] + j)
+            if t == 0:
+                quiet = sent[-1]
             for d in ds:
-                act(b("tab%d" % d, S_[t:2048:8]), ind(b("ID", full), b("lb%d%d" % (t, d))))
-            op("v", lambda: v.tensor_reduce(ap(b("cnw")), ap(b("winW")), AxisListType.X, A.add), [b("winW")], [b("cnw")], 0.1)
-            mm(b("k5", 13, S_[0:1]), b("one32"), b("cnw"))
-            vc(b("cni"), b("k5", 13, S_[0:1]))
-            vs(b("cnp"), b("cni"), 1, A.bitwise_and)
-            vs(b("thr", S_[t + 1:t + 2]), b("cnp"), 2.0, A.mult, 1.0, A.add)
+                gath(PAR["small"], b("tab%d" % d, S_[t:2048:8]), b("ID", full), b("lb%d%d" % (t, d)))
+            op("s", lambda: sc.activation(ap(b("cnj")), ap(b("winW")), F.Identity, bias=1.0 / 2048, scale=2.0, accum_out=ap(b("cnw"))),
+               [b("winW")], [b("cnj"), b("cnw")], 0.14)
+            odd = b("k5", 13, S_[0:1])
+            mm(odd, b("one32"), b("cnw"))
+            vs(b("cni"), odd, 0.25, A.mult, -0.5, A.add)
+            vs(b("thr", S_[t + 1:t + 2]), b("cni"), -4.0, A.mult, odd, A.add)
+        gr = group()
+        mm(b("k6", S_[0:256]), b("I"), b("kc"), gr)
         for h in H:
-            Kh = "k%d" % (6 + h)
-            four(h, lanes("xb", h))
-            key, gr = b(Kh, S_[0:128]), group()
-            mm(key, b("I"), b("kc"), gr)
-            mm(key, b("I"), b("lift"), gr)
-            for k in range(16):
-                mm(b(Kh, S_[k:128:16]), row("xk", h, k), b("B816"), gr)
+            key, nv = lanes("k6", h), 4 - PAR["far"][h]
+            if nv:
+                four(h, lanes("xb", h))
+                mm(key, lanes("xb", h), lanes("BlkV", h), gr)
             mm(key, lanes("mine", h), b("nIU"), gr)
             mm(key, b("nIU"), lanes("st", h), gr)
             for j in range(4):
-                vt(done("mR", h, j), block("xk", h, j), b("k%d" % (2 + h)), A.min)
+                if j < nv:
+                    vt(done("mR", h, j), block("xk", h, j), b("k%d" % (2 + h)), A.min)
+                else:
+                    bank, g2 = sbank(), group()
+                    mm(b(bank), b("I"), block("xk", h, j), g2)
+                    for u in range(4):
+                        mm(b(bank, full, S_[u::4]), b("nI"), lanes("xb", h), g2)
+                    act(done("mR", h, j), b(bank), F.Abs)
             for k in range(16):
-                mm(b(Kh, S_[k:128:16]), drow("mR", h, k), b("B8n32"), gr)
+                o = b("k6", S_[128 * h + k:128 * h + 128:16])
+                if k % 4 < nv:
+                    mm(o, row("xk", h, k), b("B816"), gr)
+                mm(o, drow("mR", h, k), b("B8n32" if k % 4 < nv else "B816"), gr)
             mm(key, b("nIU"), lanes("wl", h), gr)
         if t in NEXT:
             chase(t + 1)
+        hot = b("k7", S_[0:256])
+        scan(b("run"), b("rst"), b("k6", S_[0:256]), A.mult, A.max)
+        scan(b("mxB", S_[::-1]), b("rst"), b("run", S_[::-1]), A.mult, A.max)
+        vt(b("hotL"), b("mxB"), b("k6", S_[0:256]), A.is_equal)
         for h in H:
-            hot = top(h)
-            vt(lanes("ga", h), lanes("aD", h), hot, A.mult)
-            vt(lanes("ca", h), lanes("cK", h), hot, A.mult)
-            act(lanes("hotS", h), hot)
-        gW, gG, cs, vP, triP = b("k3", 0, S_[0:16]), b("k2", S_[0:8]), b("k2", S_[8:16]), b("k5", S_[0:8]), b("k4", S_[0:8])
+            mm(lanes("k7", h), lanes("hotL", h), b("I"))
+        vt(b("ga"), b("aD"), hot, A.mult)
+        vt(b("ca"), b("cK"), hot, A.mult)
+        move(b("hotS"), hot)
+        gW, gG, cs, vP = b("k3", 0, S_[0:16]), b("k2", S_[0:8]), b("k4", S_[0:8]), b("k5", S_[0:8])
         mm(gG, b("Blk"), b("ga"))
         wrap(gW, "ga", group())
-        act(b("gS"), gG, bias=2048.0)
-        vs(b("gw"), gW, 2048.0, A.add)
+        move(b("gS"), gG, 2048.0)
+        move(b("gw"), gW, 2048.0, e=PAR["gw"])
         vs(b("go"), gW, 2048.0, A.add)
-        act(b("gwh"), gW)
-        act(b("OG"), ind(b("O", full), b("go")))
+        gath(PAR["small"], b("OG"), b("O", full), b("go"))
         mm(vP, b("I32"), b("vG%d" % t))
-        mm(triP, b("I"), b("tri"))
         gr = group()
         mm(cs, b("Blk"), b("ca"), gr)
         mm(cs, b("nI32"), b("OG"), gr)
         gr = group()
-        dup = b("k6", S_[0:256])
-        mm(dup, b("I"), b("zer"), gr)
+        dup = b("k6", S_[256:512])
+        mm(dup, b("I"), b("gS"), gr)
         for c in range(16):
             vs(b("E3", c, S_[0:256 - 16 * c]), b("gS", S_[16 * c:256]), b("gw", S_[c:c + 1]), A.is_equal)
             if c < 15:
-                mm(b("k6", S_[16 * c + 16:256]), b("Blk"), b("E3", c, S_[16:256 - 16 * c]), gr)
-        vt(b("E3", full, S_[0:16]), b("E3", full, S_[0:16]), triP, A.mult)
-        mm(dup, b("Blk"), b("E3", full, S_[0:16]), gr)
-        act(b("dupS"), dup, scale=256.0)
-        dW, gr = b("k3", 1, S_[0:16]), group()
-        mm(dW, b("I"), b("gwh"), gr)
-        wrap(dW, "dupS", gr)
+                mm(b("k6", S_[16 * c + 272:512]), b("BlkU"), b("E3", c, S_[16:256 - 16 * c]), gr)
+        for e in range(1, 16):
+            mm(b("k6", S_[256 + e:512:16]), b("LT", S_[128 * e - 128:128 * e]), b("E3", full, e), gr)
         vt(b("eqv"), b("OG"), vP, A.is_equal)
         vt(b("tt"), b("eqv"), cs, A.mult)
-        vt(b("t1"), dW, b("dumW"), A.min)
-        vs(b("so"), b("t1"), 2048.0, A.add)
+        vt(b("run"), b("dumG"), dup, A.min)
+        scan(b("mxB"), b("rst"), b("run"), A.mult, A.max)
+        vc(b("so"), b("mxB", S_[15:256:16]))
         vt(ind(b("O", full), b("so")), b("OG"), b("tt"), A.add)
 
         def sellers(Ot=Ot):
@@ -631,9 +715,9 @@ def rank_program(g, core, T, topo):
             d[s] = np.zeros(int(np.prod(SCRATCH[x[0]][1][1:])), np.int64)
         d[s][cols(x)[0]] = n
 
-    for i in _memo["order"]:
+    for i, q in _memo["order"]:
         o = ops[i]
-        q = o["q"]
+        fn = o["q"][q][1]
         if q:
             req = need(q, o["rd"], o["wr"])
             for s, n in sorted(req.items(), key=lambda z: -len(hist.get(z, ()))):
@@ -643,12 +727,12 @@ def rank_program(g, core, T, topo):
                     for s2, n2 in hist.get((s, n), {}).items():
                         clk[q][s2] = max(clk[q].get(s2, 0), n2)
         if o["sem"] == "":
-            o["fn"]()
+            fn()
             continue
         s = o["sem"] or "q" + q
         cnt[s] = n = cnt.get(s, 0) + o["amt"]
         if q:
-            o["fn"]().then_inc(T.sem[s], o["amt"])
+            fn().then_inc(T.sem[s], o["amt"])
             hist[(s, n)] = dict(clk[q])
             if o["sem"] is None:
                 hist[(s, n)][s] = n

@@ -6,8 +6,8 @@ V, D, L, RO, N = 2048, 8, 256, 3, 8
 DEL = (1, 2, 4, 3, 6)
 HOPS = ((1, 2), (2, 4), (3, 6))
 NEXT = {0: (2, 4, 3, 6), 1: (3, 6)}
-PAR = {"fp": ("012", "012"), "fw": ("01", "01"), "prod": 8, "win": (0, 0), "far": (0, 1), "gx": "svsv", "gd": "ssvs", "conv": "s", "gw": "v", "fill": (1,), "late": 5.0, "c1": "ss", "c2": "ss", "gx0": "svss", "gd0": "svsv", "c10": "sv", "c20": "sv",
-       "sk": 16, "gat": 1.5, "arr": 3.0, "arr0": 6.5, "first": ((1, 2), (4, 3), (6,)), "hop": 0.2, "nv": 0.03, "ns": 0.11, "pe": 0.06, "lean": 0.0, "turns": 3, "mv": "s", "small": "x", "pb": "s", "load": 4.0}
+PAR = {"haste": {"xb0": 5, "xb1": 6}, "cst": "s", "junk": ("vv", "gg"), "pz": "v", "round": "vv", "u16": "vvvv", "fp": ("012", "012"), "fw": ("01", "01"), "prod": 0, "win": (0, 0), "far": (0, 2), "gx": "svsv", "gd": "svss", "conv": "s", "gw": "v", "late": 5.0, "c1": "ss", "c2": "ss", "gx0": "svvs", "gd0": "svsv", "c10": "sv", "c20": "sv",
+       "sk": 8, "gat": 1.5, "arr": 2.8, "arr0": 5.5, "first": ((1,), (2,), (4, 3), (6,)), "hop": 0.17, "nv": 0.03, "ns": 0.11, "pe": 0.06, "turns": 2, "mend": (3, 1.5, 0.7, 2), "give": 1.0, "mv": "s", "small": "s", "pb": "s", "load": 4.0}
 S_ = np.s_
 U = 8192.0
 
@@ -17,8 +17,8 @@ _shapes = {
     "C8": ([16, 128], _h), "VV0": ([4096], _f), "VV1": ([4096], _f), "xk": ([4096], _bf), "sk": ([4096], _bf), "dR": ([4096], _h),
     "mR": ([4096], _bf), "pR": ([4096], _bf), "T1": ([2048], _h), "DT": ([2048], _f), "EK": ([2048], _bf), "ID": ([2048], _f),
     "E3": ([16, 272], _bf), "ycS": ([2048], _f),
-    "cS": ([256], _h), "cm": ([16, 32], _h), "EQ": ([128, 16], _bf), "PA": ([128, 16], _bf), "PB": ([128, 32], _bf),
-    "off0": ([128], _u), "off1": ([128], _u), "a16": ([256], _u), "bo": ([16], _u), "go": ([16], _u), "so": ([16], _u),
+    "cS": ([256], _h), "cm": ([16, 24], _h), "EQ": ([128, 16], _bf), "PA": ([240, 16], _bf), "PB": ([64, 32], _bf), "PW": ([112, 32], _bf), "dupS": ([256], _bf), "gwh": ([16], _h), "t1": ([16], _f), "dumW": ([16], _f),
+    "off0": ([128], _u), "off1": ([128], _u), "a16": ([256], _u), "nW": ([48], _u), "bo": ([16], _u), "go": ([16], _u), "so": ([16], _u),
     "run": ([256], _f), "mxB": ([256], _f), "hotL": ([256], _bf), "cK": ([256], _h), "ohc": ([256], _h), "mine": ([256], _bf), "w1": ([256], _bf),
     "xb": ([256], _bf), "gt": ([256], _bf), "wl": ([256], _bf), "st": ([256], _bf), "aD": ([256], _h), "ga": ([256], _h), "ca": ([256], _h),
     "hotS": ([256], _bf), "gS": ([256], _h), "gw": ([16], _f), "OG": ([256], _f), "eqv": ([256], _bf), "tt": ([256], _f),
@@ -27,13 +27,14 @@ _shapes = {
     "IF": ([144], _f), "JG": ([128], _f), "JM": ([16, 16], _f), "pi": ([1], _i), "qi": ([1], _i), "cols": ([8], _f),
     "I": ([128], _bf), "I16": ([128], _bf), "I256": ([128], _bf), "I5": ([128], _bf), "nIU": ([128], _bf),
     "I32": ([128], _f), "nI32": ([128], _f), "one32": ([128], _f), "Blk": ([128], _bf),
-    "Blk8": ([8], _bf), "twice": ([16], _bf), "twice0": ([16], _bf), "B816": ([8], _bf), "B8n32": ([8], _bf),
+    "Blk8": ([8], _bf), "twice0": ([16], _bf), "B816": ([8], _bf), "B8n32": ([8], _bf),
     "KSa": ([144], _bf), "KS0": ([144], _bf), "KS8": ([144], _bf), "km": ([16], _f), "rst": ([256], _f), "k15": ([128], _bf),
-    "kc": ([256], _bf), "LT": ([1920], _bf), "BlkV": ([256], _bf), "nI": ([128], _bf), "tri": ([16], _f), "dumG": ([256], _f), "BlkU": ([128], _bf), "vW": ([48], _f), "zer": ([256], _bf),
+    "kc": ([256], _bf), "BlkV": ([256], _bf), "nI": ([128], _bf), "tri": ([16, 16], _bf), "sx": ([256], _bf), "bS": ([256], _h), "sb": ([256], _f), "dumG": ([256], _f), "BlkU": ([128], _bf), "vW": ([48], _f), "zer": ([256], _bf),
 }
 SCRATCH = {n: ("sbuf", [128] + s, d) for n, (s, d) in _shapes.items()}
+TAB = {1: "tabA", 4: "tabA", 6: "tabA", 2: "tabB", 3: "tabB"}
 for _d in DEL:
-    SCRATCH["tab%d" % _d] = ("sbuf", [128, 2048], _f)
+    SCRATCH[TAB[_d]] = ("sbuf", [128, 2048], _f)
     SCRATCH["la%d" % _d] = ("sbuf", [128, 128], _f)
 for _t in NEXT:
     for _d in NEXT[_t]:
@@ -131,87 +132,105 @@ def order(ops):
 
     hop = PAR["hop"]
     lat = [o["lat"] for o in ops]
-    ways = [sorted(o["q"].items()) for o in ops]
+    on, cost, index = [o["q"] for o in ops], [o["cost"] for o in ops], np.arange(n)
     banks = [sorted(set(x[0] for x in o["rd"] + o["wr"] if psum(x))) for o in ops]
+    mine = [[k + on[i] for k in banks[i]] for i in range(n)]
+    others = [[k + q for k in banks[i] for q in "vsp" if q != on[i]] for i in range(n)]
+    places = list("vspgy") + ["k%d%s" % (k, q) for k in range(8) for q in "vsp"]
+
+    def gap(j, i):
+        return (0.0 if j in ops[i]["after"] else lat[j]) + (0.0 if on[j] == on[i] else hop)
+    ahead = [[(j, gap(j, i)) for j in pre[i]] for i in range(n)]
+    behind = [[(j, gap(i, j)) for j in suc[i]] for i in range(n)]
 
     def place(rank, before, after, fwd):
-        left = [len(p) for p in before]
-        ready = sorted((rank[i], i) for i in range(n) if not left[i])
-        beg, end, on = [0.0] * n, [0.0] * n, [""] * n
-        busy, held = {}, {}
-        while ready:
-            i = ready.pop(0)[1]
-            best = None
-            for q, (cost, fn) in ways[i]:
-                t = 0.0 if fwd else lat[i]
-                for j in before[i]:
-                    x, y = (j, i) if fwd else (i, j)
-                    t = max(t, end[j] + (0.0 if x in ops[y]["after"] else lat[x]) + (0.0 if on[j] == q else hop))
-                pad = lat[i] + hop
-                a, z = (0.0, pad) if fwd else (pad, 0.0)
-                moved = bool(q)
-                while moved:
-                    moved = False
-                    lst = busy.setdefault(q, [])
-                    k = seek(lst, t)
-                    while k < len(lst) and lst[k][1] < t + cost - 1e-9:
-                        t = max(t, lst[k][0])
+        edges = ahead if fwd else behind
+        rank = list(rank)
+        for i in (range(n) if fwd else range(n - 1, -1, -1)):
+            r = rank[i]
+            for j, d in edges[i]:
+                if rank[j] > r:
+                    r = rank[j]
+            rank[i] = r
+        beg, end = [0.0] * n, [0.0] * n
+        busy = {k: [] for k in places}
+        for i in np.lexsort((index if fwd else -index, rank)).tolist():
+            t, c = (0.0 if fwd else lat[i]), cost[i]
+            for j, d in edges[i]:
+                if end[j] + d > t:
+                    t = end[j] + d
+            if on[i]:
+                a, z = (0.0, lat[i] + hop) if fwd else (lat[i] + hop, 0.0)
+                own = busy[on[i]]
+                while True:
+                    k = seek(own, t)
+                    while k < len(own) and own[k][1] < t + c - 1e-9:
+                        t = own[k][0]
                         k += 1
-                    for bank in banks[i]:
-                        for q2, l2 in held.setdefault(bank, {}).items():
-                            if q2 != q:
-                                k2 = seek(l2, t - a)
-                                if k2 < len(l2) and l2[k2][1] < t + cost + z - 1e-9:
-                                    t = l2[k2][0] + a
-                                    moved = True
-                score = t + cost + (PAR["lean"] if q == "v" else 0.0)
-                if best is None or score < best[0]:
-                    best = (score, t, q, cost, a, z)
-            score, t, q, cost, a, z = best
-            beg[i], end[i], on[i] = t, t + cost, q
-            if q:
-                lst = busy[q]
-                lst.insert(seek(lst, t), (t + cost, t))
-                for bank in banks[i]:
-                    lst = held[bank].setdefault(q, [])
-                    k = seek(lst, t - a)
-                    lo, hi = t - a, t + cost + z
-                    while k < len(lst) and lst[k][1] <= hi:
-                        e, s = lst.pop(k)
-                        lo, hi = min(lo, s), max(hi, e)
-                    lst.insert(k, (hi, lo))
-            for j in after[i]:
-                left[j] -= 1
-                if not left[j]:
-                    ready.insert(seek(ready, rank[j]), (rank[j], j))
+                    t0 = t
+                    for key in others[i]:
+                        lst = busy[key]
+                        k = seek(lst, t - a)
+                        if k < len(lst) and lst[k][1] < t + c + z - 1e-9:
+                            t = lst[k][0] + a
+                    if t == t0:
+                        break
+                take(own, t, t + c)
+                for key in mine[i]:
+                    take(busy[key], t - a, t + c + z)
+            beg[i], end[i] = t, t + c
         return beg, end, on
     way = [0.0] * n
     for i in range(n - 1, -1, -1):
-        way[i] = min(c for q, (c, fn) in ways[i]) + lat[i] + max([way[j] + hop for j in suc[i]], default=0.0)
+        way[i] = cost[i] + lat[i] + max([way[j] + hop for j in suc[i]], default=0.0)
     rank, best = [-w for w in way], None
+    _memo["dbg"] = (ops, pre, suc, way)
     for _ in range(PAR["turns"]):
+        rank = [r - o["haste"] for r, o in zip(rank, ops)]
         beg, end, on = place(rank, pre, suc, True)
         span = max(e + x for e, x in zip(end, lat))
         if best is None or span < best[0]:
             best = (span, beg, on)
         _memo.setdefault("spans", []).append(round(span, 1))
         rank = [-e for e in place([-e - x for e, x in zip(end, lat)], suc, pre, False)[1]]
-        if PAR.get("noise"):
-            rank = [r + PAR["noise"] * x for r, x in zip(rank, np.random.rand(n))]
+    steps = {}
+    for i, o in enumerate(ops):
+        steps.setdefault(o["step"], []).append(i)
+    for shift in PAR["mend"]:
+        for name, who in steps.items():
+            for d in (-shift, shift):
+                rank = list(best[1])
+                for i in who:
+                    rank[i] += d
+                for turn in range(2):
+                    beg, end, on = place(rank, pre, suc, True)
+                    span = max(e + x for e, x in zip(end, lat))
+                    if span < best[0] - 0.01:
+                        best = (span, beg, on)
+                    if turn == 0:
+                        if span > best[0] + PAR["give"]:
+                            break
+                        rank = [-e for e in place([-e - x for e, x in zip(end, lat)], suc, pre, False)[1]]
+        _memo.setdefault("spans", []).append(round(best[0], 1))
     span, beg, on = best
     _memo["span"] = span
     return [(i, on[i]) for i in sorted(range(n), key=lambda i: (beg[i], i))]
 
 
 def seek(lst, t):
-    lo, hi = 0, len(lst)
-    while lo < hi:
-        mid = (lo + hi) // 2
-        if lst[mid][0] > t + 1e-9:
-            hi = mid
-        else:
-            lo = mid + 1
-    return lo
+    k = len(lst)
+    t += 1e-9
+    while k and lst[k - 1][0] > t:
+        k -= 1
+    return k
+
+
+def take(lst, lo, hi):
+    k = seek(lst, lo - 2e-6)
+    while k < len(lst) and lst[k][1] <= hi + 1e-6:
+        e, s = lst.pop(k)
+        lo, hi = min(lo, s), max(hi, e)
+    lst.insert(k, (hi, lo))
 
 
 def rank_program(g, core, T, topo):
@@ -220,7 +239,7 @@ def rank_program(g, core, T, topo):
         return
     eng = {"v": g.vector, "s": g.scalar, "p": g.tensor, "g": g, "y": g.sync}
     v, sc, te = g.vector, g.scalar, g.tensor
-    ops = []
+    ops, haste = [], [0.0, "", 0]
     CY = 0.83e-3
 
     def ap(x):
@@ -236,16 +255,15 @@ def rank_program(g, core, T, topo):
         return [x for x in out if x[0] in SCRATCH]
 
     def op(q, fn, rd, wr, cost, lat=0.0, sem=None, amt=1, grp=None, after=()):
-        ops.append({"q": {q: (cost, fn)}, "rd": parts(rd), "wr": parts(wr), "lat": lat, "sem": sem, "amt": amt, "grp": grp, "after": after})
+        ops.append({"q": q, "cost": cost, "fn": fn, "rd": parts(rd), "wr": parts(wr), "lat": lat, "sem": sem, "amt": amt, "grp": grp, "after": after, "haste": haste[0], "step": haste[1]})
         return len(ops) - 1
 
+    def at(step, h=""):
+        haste[0] = PAR["haste"].get(step + str(h), 0.0)
+        haste[1] = (step, h, haste[2])
+
     def either(e, on_v, on_s):
-        if e != "s":
-            on_v()
-        if e != "v":
-            on_s()
-        if e not in "vs":
-            ops[-2]["q"].update(ops.pop()["q"])
+        (on_v if e == "v" else on_s)()
 
     def span(out, i, rate):
         if out[0] == "ind":
@@ -351,14 +369,18 @@ def rank_program(g, core, T, topo):
     H = (0, 1)
     dma(b("raw"), ("ctl", full), 1.4)
     ops[-1]["after"] = ()
-    dma(b("holI"), ("hol", full), PAR["load"])
+    dma(b("holI", S_[0:1024]), b("hol", S_[0:1024]), PAR["load"] - 1.5)
     ops[-1]["after"] = (0,)
-    dma(b("X"), ("sha", full), PAR["load"] + 1.5)
+    dma(b("X"), ("sha", full), PAR["load"])
     ops[-1]["after"] = (1,)
+    dma(b("holI", S_[1024:2048]), b("hol", S_[1024:2048]), PAR["load"] + 1.5)
+    ops[-1]["after"] = (2,)
     vc(b("rawf"), b("raw"))
     vc(b("rawh"), b("raw"))
     for j, ds in enumerate(PAR["first"]):
+        at("snd", min(j, 1))
         send(b("rawf"), [(d, "la%d" % d, "a%d" % d) for d in ds], PAR["arr0"] + 1.5 * j)
+    at("")
     iota(b("pi"), [[0, 1]], 0, 1)
     iota(b("IF"), [[1, 144]], 0, 0)
     iota(b("JG"), [[1, 8], [0, 16]], 0, 0)
@@ -383,12 +405,28 @@ def rank_program(g, core, T, topo):
     vs(b("I"), b("IF", S_[0:128]), col["p"], A.is_equal)
     vs(b("KSa"), b("IF"), col["g15"], A.is_equal)
     vs(b("KS8"), b("IF"), col["p15"], A.is_equal)
-    act(b("KS0"), b("KSa"), F.Copy, scale=col["q0"])
+
+    def times(out, i, c):
+        either(PAR["cst"], lambda: vs(out, i, c, A.mult), lambda: act(out, i, F.Copy, scale=c))
+    times(b("KS0"), b("KSa"), col["q0"])
+    at("ek")
     for k in range(16):
-        act(b("EK", S_[128 * k:128 * k + 128]), b("Blk"), F.Copy, scale=b("km", S_[k:k + 1]))
+        times(b("EK", S_[128 * k:128 * k + 128]), b("Blk"), b("km", S_[k:k + 1]))
+    at("cst")
     for n, c in (("I16", 16.0), ("I256", 256.0), ("I5", 1.0 / 32), ("nIU", -U), ("nI", -1.0), ("I32", 1.0), ("nI32", -1.0)):
-        act(b(n), b("I"), F.Copy, scale=c)
-    vs(b("twice"), b("JG", S_[0:128:8]), col["g"], A.is_equal)
+        times(b(n), b("I"), c)
+    for h in H:
+        at("paz")
+        zs = [b("PA", S_[120 * h + 64 - 8 * PAR["prod"]:120 * h + (64 if PAR["round"][h] == "s" else 120)])] if PAR["prod"] or PAR["round"][h] != "s" else []
+        if PAR["round"][h] == "s":
+            zs.append(b("PW", S_[56 * h:56 * h + 56], S_[16:32]))
+        for z in zs:
+            if PAR["pz"] == "g":
+                iota(z, [[0, len(cols(z)[0])]], 0, 0)
+            else:
+                ms(z, 0.0)
+    at("cst")
+    ms(b("cm", S_[0:16], S_[16:24]), 0.0)
     vs(b("twice0"), b("JG", S_[0:128:8]), col["g"], A.is_equal, col["q0"], A.mult)
     for n, c in (("Blk8", 1.0), ("B816", 16.0), ("B8n32", -32.0)):
         vs(b(n), b("IF", S_[0:8]), col["g"], A.is_equal, c, A.mult)
@@ -397,36 +435,45 @@ def rank_program(g, core, T, topo):
     ms(b("one32"), 1.0)
     ms(b("thr", S_[0:1]), 1.0)
     ms(b("O", S_[2048:2304]), 0.0)
-    vs(b("tri"), b("IF", S_[0:16]), col["q"], A.is_gt, U, A.mult)
-    for e in range(1, 16):
-        act(b("LT", S_[128 * e - 128:128 * e]), b("Blk"), F.Copy, scale=b("tri", S_[e:e + 1]))
+    vs(b("tri"), b("JM"), col["q"], A.is_gt)
     for h in H:
-        act(lanes("BlkV", h), b("Blk"), F.Copy, scale=16.0)
+        times(lanes("BlkV", h), b("Blk"), 16.0)
         for j in range(4 - PAR["far"][h], 4):
             ms(b("BlkV", S_[128 * h + j:128 * h + 128:4]), 0.0)
     iota(b("run"), [[1, 256]], 2048, 0)
     vs(b("mxB"), b("JM"), col["q"], A.is_equal)
     vt(b("dumG"), b("run"), b("mxB"), A.mult)
-    act(b("BlkU"), b("Blk"), F.Copy, scale=U)
+    times(b("BlkU"), b("Blk"), U)
     vs(b("vW", S_[0:16]), b("IF", S_[0:16]), 128.0, A.mult, col["q8"], A.add)
     for t in (1, 2):
         vs(b("vW", S_[16 * t:16 * t + 16]), b("vW", S_[0:16]), float(t), A.add)
-    for d in DEL:
+    for n, who in zip(("tabA", "tabB"), PAR["junk"]):
+        at(n)
         for j in range(2):
-            if d in PAR["fill"]:
-                ms(b("tab%d" % d, S_[1024 * j:1024 * j + 1024]), 0.0)
-            elif d in HOPS[0]:
-                iota(b("tab%d" % d, S_[1024 * j:1024 * j + 1024]), [[0, 1024]], 0, 0)
-        if d not in HOPS[0]:
-            dma(b("tab%d" % d), b("ID"), 4.0)
-        dma(bp("tab%d" % d, S_[0:128:16], full), b("la%d" % d), 2.0)
+            z = S_[1024 * j:1024 * j + 1024]
+            if who[j] == "s":
+                act(b(n, z), b("holI", S_[0:1024]))
+            elif who[j] == "v":
+                ms(b(n, z), 0.0)
+            else:
+                iota(b(n, z), [[0, 1024]], 0, 0)
+
+    def table(d, t):
+        at("")
+        dma(bp(TAB[d], S_[0:128:16], full), b("la%d" % d), 2.0)
+        for r in range(t):
+            at("upd", 2 if r < t - 1 else HOPS[t].index(d))
+            gath(PAR["small"], b(TAB[d], S_[r:2048:8]), b("ID", full), b("lb%d%d" % (r, d)))
     dma(bp("C8", S_[0:8], full), b("rawh"), PAR["late"])
     dma(bp("ycS", S_[0:128:16], full), b("rawf"), 2.0)
     gr = group()
+    at("off")
+    mm(b("k0", S_[0:4]), b("I"), lanes("zer", 0), gr)
     for q in range(16):
-        mm(b("k0", S_[0:4]), bp("KS8", S_[0:8], S_[15 - q:143 - q]), bp("C8", S_[0:8], full, S_[8 * q:8 * q + 8]), gr)
-    for e in range(8):
-        vc(b("off0", S_[16 * e:16 * e + 16]), b("k0", S_[0:4], S_[e::8]))
+        for e in range(8):
+            mm(b("k0", S_[e // 4:4:2], S_[8 * (e % 4):8 * (e % 4) + 8]), bp("KS8", S_[0:8], S_[15 - q:143 - q]), bp("C8", S_[0:8], full, 8 * q + e), gr)
+    vc(b("off0"), b("k0", S_[0:4]))
+    at("conv")
     for j in range(4):
         move(b("O", S_[512 * j:512 * j + 512]), b("holI", S_[512 * j:512 * j + 512]), e=PAR["conv"])
 
@@ -436,19 +483,29 @@ def rank_program(g, core, T, topo):
 
     def chase(t):
         s, u = HOPS[t]
-        def pieces(who, out, tab, off, h=None):
+        if t == 1:
+            at("upd", 0)
+            gath(PAR["small"], b(TAB[s], S_[0:2048:8]), b("ID", full), b("lb0%d" % s))
+        else:
+            table(s, t)
+        table(u, t)
+
+        def pieces(who, out, tab, off, h):
             w = 128 // len(who)
             for j, e in enumerate(who):
-                if h is None or j * w // 64 == h:
+                if j * w // 64 == h:
                     gath(e, b(out, S_[16 * w * j:16 * w * (j + 1)]), b(tab, full), b(off, S_[w * j:w * (j + 1)]))
-        pieces(PAR["c1" if t else "c10"], "T1", "tab%d" % s, "off0")
         for h in H:
+            at("c1", h)
+            pieces(PAR["c1" if t else "c10"], "T1", TAB[s], "off0", h)
             bk, gr = b("k%d" % h, S_[0:2]), group()
-            for q in sorted(range(16), key=lambda q: q % 8):
-                o = 256 * (q % 8) + q // 8 + 128 * h
+            at("c2", h)
+            for q in range(16):
+                o = 1024 * h + 128 * (q % 8) + q // 8
                 mm(bk, b("KS0", S_[15 - q:143 - q]), b("T1", S_[o:o + 127:2]), gr)
-            vc(b("off1", S_[64 * h:64 * h + 64]), bk)
-            pieces(PAR["c2" if t else "c20"], "DT", "tab%d" % u, "off1", h)
+            move(b("off1", S_[64 * h:64 * h + 64]), bk, e=PAR["u16"][0])
+            pieces(PAR["c2" if t else "c20"], "DT", TAB[u], "off1", h)
+        at("")
 
     feed = [0]
 
@@ -484,92 +541,121 @@ def rank_program(g, core, T, topo):
 
     chase(0)
     for t in range(RO):
+        haste[2] = t + 1
         src = "O" if t else "holI"
         Ot = b("O", S_[t:2048:8])
         nk, VV = PAR["sk"], "VV%d" % (t % 2)
+        at("vv", t)
         for j in range(4):
             iota(b(VV, S_[1024 * j:1024 * j + 1024]), [[8, 64], [0, 16]], t + 512 * j, 0)
             if t == 2:
                 ops[-1]["after"] = (quiet,)
         for h in H:
+            at("gx", h)
             vc(lanes("a16", h), b(src, S_[1024 * h + t:1024 * h + 1024:8]))
         for n, w, key in (("xk", "X", "gx"), ("dR", "DT", "gd")):
             who = PAR[key if t else key + "0"]
             c = 256 // len(who)
             for j, e in enumerate(who):
+                at(key, j * c // 128)
                 gath(e, b(n, S_[16 * c * j:16 * c * (j + 1)]), b(w, full), b("a16", S_[c * j:c * (j + 1)]))
         if t:
             sellers()
         for j in range(nk):
             w = 4096 // nk
+            at("sk", 2 * j // nk)
             vt(b("sk", S_[w * j:w * j + w]), ind(b(src, S_[0:2048]), b("a16", S_[w // 16 * j:w // 16 * (j + 1)])), b(VV, S_[w * j:w * j + w]), A.is_equal)
+        at("ad")
         move(b("aD"), Ot, -2048.0)
         for h in H:
             Ah, Kh = "k%d" % (4 + h), "k%d" % (6 + h)
+            at("min", h)
             four(h, b("X", S_[1024 * h + t:1024 * h + 1024:8]))
             for j in range(4):
                 vt(done("mR", h, j), block("xk", h, j), b("k%d" % (2 + h)), A.min)
             for k in range(16):
+                at("c", h)
                 mm(b(Ah, S_[0:8], S_[k::16]), row("dR", h, k), b("twice0"))
-                mm(b(Ah, S_[8:16], S_[k::16]), drow("mR", h, k), b("twice"))
+                at("m", h)
+                mm(b(Ah, S_[8:16], k), drow("mR", h, k), b("Blk8"))
+            nv = 4 - PAR["far"][h]
+            at("sx", h)
+            if nv:
+                for k in range(16):
+                    mm(b("k%d" % h, S_[0:4], S_[k::16]), row("xk", h, k), b("Blk8" if k % 4 < nv else "zer", S_[0:8]))
+                move(lanes("sx", h), b("k%d" % h, S_[0:4]))
             zm = S_[8 * h:8 * h + 8]
+            at("c", h)
             move(lanes("cS", h), b(Ah, S_[0:8], S_[0:16]))
-            move(b("cm", zm), b(Ah, S_[8:16]))
+            at("m", h)
+            move(b("cm", zm, S_[0:16]), b(Ah, S_[8:16], S_[0:16]))
+            at("ck", h)
             mm(b(Kh, S_[128:256]), lanes("cS", h), b("I"))
             move(lanes("cK", h), b(Kh, S_[128:256]))
             key, gr = b(Kh, S_[0:128]), group()
             mm(key, b("I"), b("k15"), gr)
             mm(key, b("I16"), b("cm", zm, S_[0:16]), gr)
 
-            def eq(s):
-                return b("EQ", S_[64 * h + 8 * s - 8:64 * h + 8 * s])
+            ns = 8 - PAR["prod"]
             for s in range(1, 9):
-                vt(eq(s), lanes("cS", h), b(Ah, S_[0:8], S_[s:s + 16]), A.is_equal)
-            nv = PAR["prod"]
-            jobs = [(1, s) for s in range(1, 8)] + [(0, s) for s in range(1, 9 - nv)]
-            jobs.sort(key=lambda z: z[1])
-            feeds = []
-            for c in range(0, len(jobs), 4):
-                bank, part = sbank(PAR["fp"][h]), jobs[c:c + 4]
-                for j, (way, s) in enumerate(part):
+                z = S_[64 * h + 8 * s - 8:64 * h + 8 * s]
+                at("eq", h)
+                vt(b("EQ", z), lanes("cS", h), b(Ah, S_[0:8], S_[s:s + 16]), A.is_equal)
+                at("pa", h)
+                for far, lo, n in ((s, 0, 16 - s), (16 - s, 16 - s, s)) if s < 8 else ((s, 0, 8),):
+                    if far <= ns or (far > 8 and PAR["round"][h] == "s"):
+                        continue
+                    y = S_[120 * h + 8 * far - 8:120 * h + 8 * far]
+                    vt(b("PA", y, S_[0:n]), b("EQ", z, S_[lo:lo + n]), b(Ah, S_[8:16], S_[far:16]), A.mult)
+                    mm(key, b("I16"), b("PA", y), gr)
+            at("pb", h)
+            for c in range(0, ns, 4):
+                bank, part = sbank(PAR["fp"][h]), range(c + 1, min(c + 4, ns) + 1)
+                for j, s in enumerate(part):
                     z, o, g2 = S_[8 * (j // 2):8 * (j // 2) + 8], 16 * (j % 2), group()
-                    mm(b(bank, z, S_[o:o + 16]), b("I"), b("cm", zm, S_[16 - s:32 - s] if way else S_[s:s + 16]), g2)
-                    if way:
-                        mm(b(bank, z, S_[o + s:o + 16]), b("I256"), eq(s) [0:1] + (eq(s)[1] + (S_[0:16 - s],),), g2)
-                        mm(b(bank, z, S_[o:o + s]), b("I256"), eq(s)[0:1] + (eq(s)[1] + (S_[16 - s:16],),), g2)
-                    else:
-                        mm(b(bank, z, S_[o:o + 16]), b("I256"), eq(s), g2)
-                r0, m = 64 * h + 4 * c, len(part)
+                    mm(b(bank, z, S_[o:o + 16]), b("I"), b("cm", zm, S_[s:s + 16]), g2)
+                    mm(b(bank, z, S_[o:o + 16]), b("I256"), b("EQ", S_[64 * h + 8 * s - 8:64 * h + 8 * s]), g2)
+                r0, m = 32 * h + 4 * c, len(part)
                 if m == 3:
                     mm(b(bank, S_[8:16], S_[16:32]), b("I"), b("zer", S_[0:128]))
                 nr, nc = (16 if m > 2 else 8), (32 if m > 1 else 16)
                 move(b("PB", S_[r0:r0 + nr], S_[0:nc]), b(bank, S_[0:nr], S_[0:nc]), -256.0, True, PAR["pb"])
-                feeds += [(way, s, S_[r0 + 8 * (j // 2):r0 + 8 * (j // 2) + 8], 16 * (j % 2)) for j, (way, s) in enumerate(part)]
-            for way, s, z, o in feeds:
-                mm(key, b("I16"), b("PB", z, S_[o:o + 16]), gr)
-            for s in range(9 - nv, 9):
-                pa = b("PA", S_[64 * h + 8 * s - 8:64 * h + 8 * s])
-                vt(pa, eq(s), b(Ah, S_[8:16], S_[s:s + 16]), A.mult)
-                mm(key, b("I16"), pa, gr)
+                for j, s in enumerate(part):
+                    mm(key, b("I16"), b("PB", S_[r0 + 8 * (j // 2):r0 + 8 * (j // 2) + 8], S_[16 * (j % 2):16 * (j % 2) + 16]), gr)
+            if PAR["round"][h] == "s":
+                bank = sbank(PAR["fp"][h])
+                at("pw", h)
+                for s in range(1, 8):
+                    g2 = group()
+                    mm(b(bank, S_[2 * s - 2:2 * s]), b("I"), b("cm", zm, S_[8:16]), g2)
+                    mm(b(bank, S_[2 * s - 2:2 * s]), b("I256"), b("EQ", S_[64 * h + 8 * s - 8:64 * h + 8 * s], S_[8:16]), g2)
+                move(b("PW", S_[56 * h:56 * h + 56], S_[8:16]), b(bank, S_[0:14]), -256.0, True, PAR["pb"])
+                for s in range(1, 8):
+                    mm(key, b("I16"), b("PW", S_[56 * h + 8 * s - 8:56 * h + 8 * s], S_[16 - s:32 - s]), gr)
         for h in H:
             Kh = "k%d" % (6 + h)
+            at("top", h)
             vt(lanes("ohc", h), lanes("cK", h), top(h), A.mult)
             mm(b(Kh, S_[256:384]), b("Blk"), lanes("ohc", h))
             vt(lanes("mine", h), lanes("cK", h), b(Kh, S_[256:384]), A.is_equal)
             if PAR["win"][h]:
                 act(lanes("w1", h), lanes("mine", h), scale=2.0, bias=-1.0)
             bW, gr, z = b(Kh, S_[384:392]), group(), S_[8 * h:8 * h + 8]
+            at("xb", h)
             for q in range(16):
                 mm(bW, b("KSa", S_[15 - q:143 - q]), b("ohc", S_[128 * h + q:128 * h + 128:16]), gr)
-            vc(b("bo", z), bW)
-            vt(b("dbv", z), bW, b("vW", S_[16 * t + 8 * h:16 * t + 8 * h + 8]), A.subtract)
+            move(b("bo", z), bW, e=PAR["u16"][1])
             gath(PAR["small"], lanes("xb", h), b("X", full), b("bo", z))
+            at("dbv")
+            vt(b("dbv", z), bW, b("vW", S_[16 * t + 8 * h:16 * t + 8 * h + 8]), A.subtract)
         vW = b("vW", S_[16 * t:16 * t + 16])
         for h in H:
             Ah = "k%d" % (4 + h)
+            at("st", h)
             for k in range(16):
-                mm(b(Ah, S_[8:12], S_[k::16]), row("sk", h, k), b("Blk8"))
-            under(lanes("st", h), b(Ah, S_[8:12]), 0.5)
+                mm(b("k7", S_[256 * h + k:256 * h + 128:16]), row("sk", h, k), b("Blk8"))
+            under(lanes("st", h), b("k7", S_[256 * h:256 * h + 128]), 0.5)
+            at("win", h)
             for j in range(4):
                 if j < PAR["win"][h]:
                     bank = "k%d" % (2 + j % 2)
@@ -585,18 +671,22 @@ def rank_program(g, core, T, topo):
                         mm(b(bank, full, S_[u::4]), b("EK", S_[128 * k:128 * k + 128]), lanes("mine", h), gr)
                     act(done("pR", h, j), b(bank), F.Abs, scale=32.0, bias=-16.0)
             gr = group()
+            at("sum", h)
             for k in range(16):
                 kk = 4 * (k % 4) + k // 4
                 mm(b(Ah, S_[0:4]), b("I"), drow("pR", h, kk), gr)
             act(lanes("gt", h), b(Ah, S_[0:4]), F.Sign, bias=-64.0 * (4 - PAR["win"][h]) - 0.5)
+            at("wl", h)
             mm(b(Ah, S_[4:8]), lanes("gt", h), b("Blk"))
             under(lanes("wl", h), b(Ah, S_[4:8]), b("thr", S_[t:t + 1]))
-        cW, nW = b("k4", 12, S_[0:16]), b("off0", S_[16 * t:16 * t + 16])
+        cW, nW = b("k4", 12, S_[0:16]), b("nW", S_[16 * t:16 * t + 16])
+        at("new")
         wrap(cW, "gt", group())
         vs(b("winW"), cW, b("thr", S_[t:t + 1]), A.is_gt)
         vt(b("tw"), b("winW"), b("dbv"), A.mult)
         vt(b("nw"), b("tw"), vW, A.add)
         vc(nW, b("nw"))
+        at("yc")
         gath(PAR["small"], b("ycS", S_[t:2048:8]), b("ID", full), nW)
         if t in NEXT:
             ds = NEXT[t]
@@ -605,8 +695,10 @@ def rank_program(g, core, T, topo):
                     send(nW, [(d, "lb%d%d" % (t, d), "b%d%d" % (t, d)) for d in part], PAR["arr"] + j)
             if t == 0:
                 quiet = sent[-1]
-            for d in ds:
-                gath(PAR["small"], b("tab%d" % d, S_[t:2048:8]), b("ID", full), b("lb%d%d" % (t, d)))
+            at("own")
+            for h in H:
+                move(b("off0", S_[64 * h + 8 * t:64 * h + 8 * t + 8]), b("nw", S_[8 * h:8 * h + 8]), e=PAR["u16"][3])
+            at("z")
             op("s", lambda: sc.activation(ap(b("cnj")), ap(b("winW")), F.Identity, bias=1.0 / 2048, scale=2.0, accum_out=ap(b("cnw"))),
                [b("winW")], [b("cnj"), b("cnw")], 0.14)
             odd = b("k5", 13, S_[0:1])
@@ -614,60 +706,80 @@ def rank_program(g, core, T, topo):
             vs(b("cni"), odd, 0.25, A.mult, -0.5, A.add)
             vs(b("thr", S_[t + 1:t + 2]), b("cni"), -4.0, A.mult, odd, A.add)
         gr = group()
+        at("key")
         mm(b("k6", S_[0:256]), b("I"), b("kc"), gr)
         for h in H:
             key, nv = lanes("k6", h), 4 - PAR["far"][h]
             if nv:
+                at("xb", h)
                 four(h, lanes("xb", h))
+                at("key")
                 mm(key, lanes("xb", h), lanes("BlkV", h), gr)
+                mm(key, b("I16"), lanes("sx", h), gr)
             mm(key, lanes("mine", h), b("nIU"), gr)
             mm(key, b("nIU"), lanes("st", h), gr)
             for j in range(4):
                 if j < nv:
+                    at("far", h)
                     vt(done("mR", h, j), block("xk", h, j), b("k%d" % (2 + h)), A.min)
                 else:
+                    at("fars", h)
                     bank, g2 = sbank(), group()
                     mm(b(bank), b("I"), block("xk", h, j), g2)
                     for u in range(4):
                         mm(b(bank, full, S_[u::4]), b("nI"), lanes("xb", h), g2)
                     act(done("mR", h, j), b(bank), F.Abs)
+            at("key")
             for k in range(16):
                 o = b("k6", S_[128 * h + k:128 * h + 128:16])
-                if k % 4 < nv:
-                    mm(o, row("xk", h, k), b("B816"), gr)
                 mm(o, drow("mR", h, k), b("B8n32" if k % 4 < nv else "B816"), gr)
             mm(key, b("nIU"), lanes("wl", h), gr)
         if t in NEXT:
             chase(t + 1)
         hot = b("k7", S_[0:256])
+        at("sold")
         scan(b("run"), b("rst"), b("k6", S_[0:256]), A.mult, A.max)
         scan(b("mxB", S_[::-1]), b("rst"), b("run", S_[::-1]), A.mult, A.max)
         vt(b("hotL"), b("mxB"), b("k6", S_[0:256]), A.is_equal)
         for h in H:
             mm(lanes("k7", h), lanes("hotL", h), b("I"))
         vt(b("ga"), b("aD"), hot, A.mult)
+        at("ca")
         vt(b("ca"), b("cK"), hot, A.mult)
-        move(b("hotS"), hot)
+        at("sell")
+        rest = b("k7", S_[256:512])
+        if t in NEXT:
+            move(b("hotS"), hot)
+        else:
+            mm(rest, b("Blk"), b("ohc"))
+            move(b("bS"), rest)
+            vt(b("sb"), b("bS"), hot, A.mult)
+            act(rest, hot, scale=-1.0, bias=1.0)
         gW, gG, cs, vP = b("k3", 0, S_[0:16]), b("k2", S_[0:8]), b("k4", S_[0:8]), b("k5", S_[0:8])
+        at("goal")
         mm(gG, b("Blk"), b("ga"))
         wrap(gW, "ga", group())
         move(b("gS"), gG, 2048.0)
         move(b("gw"), gW, 2048.0, e=PAR["gw"])
-        vs(b("go"), gW, 2048.0, A.add)
+        at("og")
+        move(b("go"), gW, 2048.0, e=PAR["u16"][2])
         gath(PAR["small"], b("OG"), b("O", full), b("go"))
+        triP = b("k3", S_[8:16])
         mm(vP, b("I32"), b("vG%d" % t))
+        mm(triP, b("I"), b("tri"))
         gr = group()
         mm(cs, b("Blk"), b("ca"), gr)
         mm(cs, b("nI32"), b("OG"), gr)
         gr = group()
+        at("dup")
         dup = b("k6", S_[256:512])
         mm(dup, b("I"), b("gS"), gr)
         for c in range(16):
             vs(b("E3", c, S_[0:256 - 16 * c]), b("gS", S_[16 * c:256]), b("gw", S_[c:c + 1]), A.is_equal)
             if c < 15:
                 mm(b("k6", S_[16 * c + 272:512]), b("BlkU"), b("E3", c, S_[16:256 - 16 * c]), gr)
-        for e in range(1, 16):
-            mm(b("k6", S_[256 + e:512:16]), b("LT", S_[128 * e - 128:128 * e]), b("E3", full, e), gr)
+        vt(b("E3", full, S_[0:16]), b("E3", full, S_[0:16]), triP, A.mult)
+        mm(dup, b("BlkU"), b("E3", full, S_[0:16]), gr)
         vt(b("eqv"), b("OG"), vP, A.is_equal)
         vt(b("tt"), b("eqv"), cs, A.mult)
         vt(b("run"), b("dumG"), dup, A.min)
@@ -677,11 +789,13 @@ def rank_program(g, core, T, topo):
 
         def sellers(Ot=Ot):
             P, gr = b("k7", S_[256:512]), group()
+            at("sell")
             mm(P, b("Blk"), b("ohc"), gr)
             mm(P, b("nI32"), Ot, gr)
             vt(P, b("hotS"), P, A.mult)
             vt(Ot, Ot, P, A.add)
-    sellers()
+    vt(rest, Ot, rest, A.mult)
+    vt(Ot, b("sb"), rest, A.add)
     dma(("yo", full), b("O", S_[0:2048]), 5.0)
     dma(("yc", full), bp("ycS", S_[0:128:16], full), 2.0)
 
@@ -695,15 +809,17 @@ def rank_program(g, core, T, topo):
 
         def take(tab, x, skip):
             for s, arr in tab.get(x[0], {}).items():
-                if s == own and skip:
+                if s == own and skip and (q == "p" or skip == 2):
                     continue
                 n = int(arr.max() if psum(x) and s != own else arr[cols(x)[0]].max())
+                if s == own and skip and n <= cnt[own] - 4:
+                    continue
                 if n > req.get(s, 0):
                     req[s] = n
         for x in rd:
             take(W, x, False)
             if psum(x):
-                take(R, x, True)
+                take(R, x, 2)
         for x in wr:
             take(W, x, True)
             take(R, x, True)
@@ -717,7 +833,7 @@ def rank_program(g, core, T, topo):
 
     for i, q in _memo["order"]:
         o = ops[i]
-        fn = o["q"][q][1]
+        fn = o["fn"]
         if q:
             req = need(q, o["rd"], o["wr"])
             for s, n in sorted(req.items(), key=lambda z: -len(hist.get(z, ()))):

import numpy as np
from concourse.mybir import AluOpType as A, ActivationFunctionType as F, AxisListType
from concourse.bass import DstId, RemoteDMATransfer

V, D, L, RO, N = 2048, 8, 256, 3, 8
DEL = (1, 2, 4, 3, 6)
HOPS = ((1, 2), (2, 4), (3, 6))
NEXT = {0: (2, 4, 3, 6), 1: (3, 6)}
PAR = {"haste": {"xb0": 5, "xb1": 6}, "cst": "s", "junk": ("vv", "gg"), "pz": "v", "round": "vv", "u16": "vvvv", "fp": ("012", "012"), "fw": ("01", "01"), "prod": 0, "win": (0, 0), "far": (0, 2), "gx": "svsv", "gd": "svss", "conv": "s", "gw": "v", "late": 5.0, "c1": "ss", "c2": "ss", "gx0": "svvs", "gd0": "svsv", "c10": "sv", "c20": "sv",
       "sk": 8, "gat": 1.5, "arr": 2.8, "arr0": 5.5, "first": ((1,), (2,), (4, 3), (6,)), "hop": 0.17, "nv": 0.03, "ns": 0.11, "pe": 0.06, "turns": 2, "mend": (3, 1.5, 0.7, 2), "give": 1.0, "mv": "s", "small": "s", "pb": "s", "load": 4.0}
S_ = np.s_
U = 8192.0

_bf, _f, _i, _u, _h = "bfloat16", "float32", "int32", "uint16", "float16"
_shapes = {
    "O": ([2304], _f), "holI": ([2048], _i), "X": ([2048], _bf), "raw": ([128], _i), "rawf": ([128], _f), "rawh": ([128], _h),
    "C8": ([16, 128], _h), "VV0": ([4096], _f), "VV1": ([4096], _f), "xk": ([4096], _bf), "sk": ([4096], _bf), "dR": ([4096], _h),
    "mR": ([4096], _bf), "pR": ([4096], _bf), "T1": ([2048], _h), "DT": ([2048], _f), "EK": ([2048], _bf), "ID": ([2048], _f),
    "E3": ([16, 272], _bf), "ycS": ([2048], _f),
    "cS": ([256], _h), "cm": ([16, 24], _h), "EQ": ([128, 16], _bf), "PA": ([240, 16], _bf), "PB": ([64, 32], _bf), "PW": ([112, 32], _bf), "dupS": ([256], _bf), "gwh": ([16], _h), "t1": ([16], _f), "dumW": ([16], _f),
    "off0": ([128], _u), "off1": ([128], _u), "a16": ([256], _u), "nW": ([48], _u), "bo": ([16], _u), "go": ([16], _u), "so": ([16], _u),
    "run": ([256], _f), "mxB": ([256], _f), "hotL": ([256], _bf), "cK": ([256], _h), "ohc": ([256], _h), "mine": ([256], _bf), "w1": ([256], _bf),
    "xb": ([256], _bf), "gt": ([256], _bf), "wl": ([256], _bf), "st": ([256], _bf), "aD": ([256], _h), "ga": ([256], _h), "ca": ([256], _h),
    "hotS": ([256], _bf), "gS": ([256], _h), "gw": ([16], _f), "OG": ([256], _f), "eqv": ([256], _bf), "tt": ([256], _f),
    "dbv": ([16], _f), "winW": ([16], _f), "tw": ([16], _f), "nw": ([16], _f),
    "cnw": ([1], _f), "cni": ([1], _i), "cnj": ([16], _f), "thr": ([RO], _f),
    "IF": ([144], _f), "JG": ([128], _f), "JM": ([16, 16], _f), "pi": ([1], _i), "qi": ([1], _i), "cols": ([8], _f),
    "I": ([128], _bf), "I16": ([128], _bf), "I256": ([128], _bf), "I5": ([128], _bf), "nIU": ([128], _bf),
    "I32": ([128], _f), "nI32": ([128], _f), "one32": ([128], _f), "Blk": ([128], _bf),
    "Blk8": ([8], _bf), "twice0": ([16], _bf), "B816": ([8], _bf), "B8n32": ([8], _bf),
    "KSa": ([144], _bf), "KS0": ([144], _bf), "KS8": ([144], _bf), "km": ([16], _f), "rst": ([256], _f), "k15": ([128], _bf),
    "kc": ([256], _bf), "BlkV": ([256], _bf), "nI": ([128], _bf), "tri": ([16, 16], _bf), "sx": ([256], _bf), "bS": ([256], _h), "sb": ([256], _f), "dumG": ([256], _f), "BlkU": ([128], _bf), "vW": ([48], _f), "zer": ([256], _bf),
}
SCRATCH = {n: ("sbuf", [128] + s, d) for n, (s, d) in _shapes.items()}
TAB = {1: "tabA", 4: "tabA", 6: "tabA", 2: "tabB", 3: "tabB"}
for _d in DEL:
    SCRATCH[TAB[_d]] = ("sbuf", [128, 2048], _f)
    SCRATCH["la%d" % _d] = ("sbuf", [128, 128], _f)
for _t in NEXT:
    for _d in NEXT[_t]:
        SCRATCH["lb%d%d" % (_t, _d)] = ("sbuf", [128, 16], _u)
for _t in range(RO):
    SCRATCH["vG%d" % _t] = ("sbuf", [128, 256], _f)
for _k in range(8):
    SCRATCH["k%d" % _k] = ("psum", [128, 16, 32] if _k < 6 else [128, 512], _f)
SEMAPHORES = ["qv", "qs", "qp", "qg", "ls"] + ["d%d" % k for k in range(20)] + ["a%d" % d for d in DEL] + ["b%d%d" % (t, d) for t in NEXT for d in NEXT[t]]
_memo = {}


def b(n, *ix):
    return (n, (slice(None),) + ix)


def bp(n, p, *ix):
    return (n, (p,) + ix)


def ind(w, o):
    return ("ind", w, o)


def cols(x):
    key = repr(x)
    if key not in _memo:
        ix = x[1][1:]
        sh = SCRATCH[x[0]][1][1:]
        m = np.arange(int(np.prod(sh))).reshape(sh)
        c = m[ix].ravel() if ix else m.ravel()
        bits = np.zeros(m.size, np.uint8)
        bits[c] = 1
        _memo[key] = (c, int.from_bytes(np.packbits(bits).tobytes(), "big"))
    return _memo[key]


def psum(x):
    return SCRATCH[x[0]][0] == "psum"


def two(x):
    return SCRATCH[x[0]][2] in (_bf, _h, _u)


def order(ops):
    n = len(ops)
    pre = [set() for _ in range(n)]
    Wr, Rd, bar, single, union, members = {}, {}, {}, {}, {}, {}
    for i, o in enumerate(ops):
        if o["grp"] is not None:
            union[o["grp"]] = union.get(o["grp"], 0) | cols(o["wr"][0])[1]
            members.setdefault(o["grp"], []).append(i)

    def write(name, m, who, i):
        for tab in (Wr, Rd):
            keep = []
            for j, mj in tab.get(name, ()):
                if mj & m:
                    pre[i].add(j)
                    mj &= ~m
                if mj:
                    keep.append((j, mj))
            tab[name] = keep
        Wr[name] += [(j, m) for j in who]
    for i, o in enumerate(ops):
        pre[i].update(o["after"])
        for x in o["rd"]:
            m = cols(x)[1]
            pre[i].update(j for j, mj in Wr.get(x[0], ()) if mj & m)
        gr = o["grp"]
        if gr is not None:
            bank, mem = o["wr"][0][0], members[gr]
            if i == mem[0]:
                pre[i].update(bar.get(bank, ()))
                if len(mem) > 1:
                    pre[i].update(single.pop(bank, ()))
                    bar[bank] = mem
                else:
                    single.setdefault(bank, []).append(i)
                write(bank, union[gr], mem, i)
            else:
                pre[i].add(mem[0])
        else:
            for x in o["wr"]:
                write(x[0], cols(x)[1], [i], i)
        for x in o["rd"]:
            Rd.setdefault(x[0], []).append((i, cols(x)[1]))
        pre[i].discard(i)
    suc = [[] for _ in range(n)]
    for i in range(n):
        assert all(j < i for j in pre[i])
        for j in pre[i]:
            suc[j].append(i)

    hop = PAR["hop"]
    lat = [o["lat"] for o in ops]
    on, cost, index = [o["q"] for o in ops], [o["cost"] for o in ops], np.arange(n)
    banks = [sorted(set(x[0] for x in o["rd"] + o["wr"] if psum(x))) for o in ops]
    mine = [[k + on[i] for k in banks[i]] for i in range(n)]
    others = [[k + q for k in banks[i] for q in "vsp" if q != on[i]] for i in range(n)]
    places = list("vspgy") + ["k%d%s" % (k, q) for k in range(8) for q in "vsp"]

    def gap(j, i):
        return (0.0 if j in ops[i]["after"] else lat[j]) + (0.0 if on[j] == on[i] else hop)
    ahead = [[(j, gap(j, i)) for j in pre[i]] for i in range(n)]
    behind = [[(j, gap(i, j)) for j in suc[i]] for i in range(n)]

    def place(rank, before, after, fwd):
        edges = ahead if fwd else behind
        rank = list(rank)
        for i in (range(n) if fwd else range(n - 1, -1, -1)):
            r = rank[i]
            for j, d in edges[i]:
                if rank[j] > r:
                    r = rank[j]
            rank[i] = r
        beg, end = [0.0] * n, [0.0] * n
        busy = {k: [] for k in places}
        for i in np.lexsort((index if fwd else -index, rank)).tolist():
            t, c = (0.0 if fwd else lat[i]), cost[i]
            for j, d in edges[i]:
                if end[j] + d > t:
                    t = end[j] + d
            if on[i]:
                a, z = (0.0, lat[i] + hop) if fwd else (lat[i] + hop, 0.0)
                own = busy[on[i]]
                while True:
                    k = seek(own, t)
                    while k < len(own) and own[k][1] < t + c - 1e-9:
                        t = own[k][0]
                        k += 1
                    t0 = t
                    for key in others[i]:
                        lst = busy[key]
                        k = seek(lst, t - a)
                        if k < len(lst) and lst[k][1] < t + c + z - 1e-9:
                            t = lst[k][0] + a
                    if t == t0:
                        break
                take(own, t, t + c)
                for key in mine[i]:
                    take(busy[key], t - a, t + c + z)
            beg[i], end[i] = t, t + c
        return beg, end, on
    way = [0.0] * n
    for i in range(n - 1, -1, -1):
        way[i] = cost[i] + lat[i] + max([way[j] + hop for j in suc[i]], default=0.0)
    rank, best = [-w for w in way], None
    _memo["dbg"] = (ops, pre, suc, way)
    for _ in range(PAR["turns"]):
        rank = [r - o["haste"] for r, o in zip(rank, ops)]
        beg, end, on = place(rank, pre, suc, True)
        span = max(e + x for e, x in zip(end, lat))
        if best is None or span < best[0]:
            best = (span, beg, on)
        _memo.setdefault("spans", []).append(round(span, 1))
        rank = [-e for e in place([-e - x for e, x in zip(end, lat)], suc, pre, False)[1]]
    steps = {}
    for i, o in enumerate(ops):
        steps.setdefault(o["step"], []).append(i)
    for shift in PAR["mend"]:
        for name, who in steps.items():
            for d in (-shift, shift):
                rank = list(best[1])
                for i in who:
                    rank[i] += d
                for turn in range(2):
                    beg, end, on = place(rank, pre, suc, True)
                    span = max(e + x for e, x in zip(end, lat))
                    if span < best[0] - 0.01:
                        best = (span, beg, on)
                    if turn == 0:
                        if span > best[0] + PAR["give"]:
                            break
                        rank = [-e for e in place([-e - x for e, x in zip(end, lat)], suc, pre, False)[1]]
        _memo.setdefault("spans", []).append(round(best[0], 1))
    span, beg, on = best
    _memo["span"] = span
    return [(i, on[i]) for i in sorted(range(n), key=lambda i: (beg[i], i))]


def seek(lst, t):
    k = len(lst)
    t += 1e-9
    while k and lst[k - 1][0] > t:
        k -= 1
    return k


def take(lst, lo, hi):
    k = seek(lst, lo - 2e-6)
    while k < len(lst) and lst[k][1] <= hi + 1e-6:
        e, s = lst.pop(k)
        lo, hi = min(lo, s), max(hi, e)
    lst.insert(k, (hi, lo))


def rank_program(g, core, T, topo):
    rank = T.rank_of(core)
    if rank is None:
        return
    eng = {"v": g.vector, "s": g.scalar, "p": g.tensor, "g": g, "y": g.sync}
    v, sc, te = g.vector, g.scalar, g.tensor
    ops, haste = [], [0.0, "", 0]
    CY = 0.83e-3

    def ap(x):
        if x[0] == "ind":
            return T[x[1][0]][x[1][1]].indirect(T[x[2][0]][x[2][1]])
        return T[x[0]][x[1]]

    def parts(xs):
        out = []
        for x in xs:
            if isinstance(x, tuple):
                out += [x[1], x[2]] if x[0] == "ind" else [x]
        return [x for x in out if x[0] in SCRATCH]

    def op(q, fn, rd, wr, cost, lat=0.0, sem=None, amt=1, grp=None, after=()):
        ops.append({"q": q, "cost": cost, "fn": fn, "rd": parts(rd), "wr": parts(wr), "lat": lat, "sem": sem, "amt": amt, "grp": grp, "after": after, "haste": haste[0], "step": haste[1]})
        return len(ops) - 1

    def at(step, h=""):
        haste[0] = PAR["haste"].get(step + str(h), 0.0)
        haste[1] = (step, h, haste[2])

    def either(e, on_v, on_s):
        (on_v if e == "v" else on_s)()

    def span(out, i, rate):
        if out[0] == "ind":
            return 0.05 + 16 * len(cols(out[2])[0]) * 3.8 * CY
        if i[0] == "ind":
            return 0.05 + 16 * len(cols(i[2])[0]) * PAR["gat"] * CY
        return PAR["nv"] + max(64, len(cols(i)[0]) * rate) * CY

    def half(*xs):
        return 0.5 if all(x[0] != "ind" and two(x) for x in xs) else 1.0

    def vt(out, i0, i1, o):
        rate = 1.0 if i0[0] == "ind" or psum(i0) or psum(i1) else 2.0
        op("v", lambda: v.tensor_tensor(ap(out), ap(i0), ap(i1), o), [i0, i1] + ([out[2]] if out[0] == "ind" else []),
           [out[1] if out[0] == "ind" else out], span(out, i0, rate))

    def vs(out, i0, s1, o1, s2=None, o2=None):
        def fn():
            a = [ap(x) if isinstance(x, tuple) else x for x in (s1, s2)]
            if o2 is None:
                return v.tensor_scalar(ap(out), ap(i0), a[0], None, o1)
            return v.tensor_scalar(ap(out), ap(i0), a[0], a[1], o1, o2)
        op("v", fn, [i0, s1, s2], [out], span(out, i0, half(out, i0)))

    def vc(out, i):
        op("v", lambda: v.tensor_copy(ap(out), ap(i)), [i], [out], span(out, i, half(out, i)))

    def ms(out, c):
        op("v", lambda: v.memset(ap(out), c), [], [out], span(out, out, half(out)))

    def scan(out, d0, d1, o0, o1):
        op("v", lambda: v.tensor_tensor_scan(ap(out), ap(d0), ap(d1), 0.0, o0, o1), [d0, d1], [out], span(out, d0, 1.0))

    def act(out, i, f=F.Identity, bias=0.0, scale=1.0):
        def fn():
            a = [ap(x) if isinstance(x, tuple) else x for x in (bias, scale)]
            return sc.activation(ap(out), ap(i), f, bias=a[0], scale=a[1])
        op("s", fn, [i, bias, scale], [out], (0.01 if i[0] == "ind" else PAR["ns"] - PAR["nv"]) + span(out, i, 1.0))

    todo = {}

    def mm(out, l, r, grp=None):
        grp = grp or ("one", len(ops))
        first = grp not in todo
        todo[grp] = todo.get(grp, 0) + 1

        def fn():
            todo[grp] -= 1
            return te.matmul(ap(out), ap(l), ap(r), first, todo[grp] == 0)
        cyc = max(min(64, len(cols(l)[0])), len(cols(r)[0])) * (1 if two(l) else 4)
        op("p", fn, [l, r], [out], cyc * CY / 2, PAR["pe"], grp=grp)

    def group():
        return ("grp", len(ops))

    def iota(out, pat, base, cm):
        kw = {} if SCRATCH[out[0]][2] == _i else {"allow_small_or_imprecise_dtypes": True}
        op("g", lambda: g.iota(ap(out), pat, base, cm, **kw), [], [out], 0.13 + 2 * len(cols(out)[0]) * CY)

    ndma = [0]

    def dma(out, i, lat, q="y"):
        s = "d%d" % ndma[0]
        ndma[0] += 1
        op(q, lambda: eng[q].dma_start(ap(out), ap(i)), [i], [out], 0.1, lat, s, 16)

    nls = [0]
    sent = []

    def send(src, items, lat):
        NE = 8 // len(items)

        def fn():
            tr, k = [], 0
            for d, dst, sem in items:
                to = T.cores[(rank - d) % N]
                rid, pid = topo.addr(to)[:2]
                es = topo.engines(core, to)[k:k + NE]
                k += NE
                tr.append(RemoteDMATransfer(dst_ids=[DstId(rid=rid, pnc=pid)], dma_engine_mask=sum(1 << e for e in es), remote_sem=T.sem[sem], src=ap(src), dst=T[dst][:], alu_op=0))
                nls[0] += NE
            g.remote_dma_fused(tr, local_sem=T.sem.ls)
        j = op("g", fn, [src], [], 0.4, sem="", after=tuple(sent[-1:]))
        sent.append(j)
        for d, dst, sem in items:
            op("", None, [], [b(dst)], lat, sem=sem, amt=NE, after=(j,))

    def gath(e, out, w, o):
        either(e, lambda: vc(out, ind(w, o)), lambda: act(out, ind(w, o)))

    def move(out, i, bias=0.0, floor=False, e=None):
        either(e or PAR["mv"], lambda: vs(out, i, bias, A.add, 0.0, A.max) if floor else vs(out, i, bias, A.add),
               lambda: act(out, i, F.Relu if floor else F.Identity, bias=bias))

    def under(out, i, bar):
        either(PAR["mv"], lambda: vs(out, i, bar, A.is_lt),
               lambda: act(out, i, F.Relu, bias=bar if isinstance(bar, tuple) else 2 * bar, scale=-1.0))

    def lanes(n, h):
        return b(n, S_[128 * h:128 * h + 128])

    full = S_[:]
    H = (0, 1)
    dma(b("raw"), ("ctl", full), 1.4)
    ops[-1]["after"] = ()
    dma(b("holI", S_[0:1024]), b("hol", S_[0:1024]), PAR["load"] - 1.5)
    ops[-1]["after"] = (0,)
    dma(b("X"), ("sha", full), PAR["load"])
    ops[-1]["after"] = (1,)
    dma(b("holI", S_[1024:2048]), b("hol", S_[1024:2048]), PAR["load"] + 1.5)
    ops[-1]["after"] = (2,)
    vc(b("rawf"), b("raw"))
    vc(b("rawh"), b("raw"))
    for j, ds in enumerate(PAR["first"]):
        at("snd", min(j, 1))
        send(b("rawf"), [(d, "la%d" % d, "a%d" % d) for d in ds], PAR["arr0"] + 1.5 * j)
    at("")
    iota(b("pi"), [[0, 1]], 0, 1)
    iota(b("IF"), [[1, 144]], 0, 0)
    iota(b("JG"), [[1, 8], [0, 16]], 0, 0)
    iota(b("JM"), [[0, 16], [1, 16]], 0, 0)
    iota(b("k15"), [[0, 8], [-1, 16]], 15, 0)
    iota(b("kc"), [[0, 16], [-1, 16]], 31, 0)
    iota(b("ID"), [[1, 2048]], 0, 0)
    for t in range(RO):
        iota(b("vG%d" % t), [[8, 256]], t, 0)
    col = {n: b("cols", S_[j:j + 1]) for j, n in enumerate(("p", "q", "g", "g15", "q0", "p15", "q8"))}
    vs(b("qi"), b("pi"), 15, A.bitwise_and)
    vc(col["p"], b("pi"))
    vc(col["q"], b("qi"))
    vt(col["g15"], b("pi"), b("qi"), A.subtract)
    vs(col["g"], col["g15"], 1.0 / 16, A.mult)
    vs(col["q0"], col["q"], 1.0, A.is_lt)
    vs(col["g15"], col["g15"], 15.0, A.add)
    vs(col["p15"], col["p"], 16.0, A.mult, 15.0, A.add)
    vs(col["q8"], col["q"], 8.0, A.mult)
    vs(b("Blk"), b("JG"), col["g"], A.is_equal)
    vs(b("km"), b("IF", S_[0:16]), col["q"], A.is_equal)
    vs(b("I"), b("IF", S_[0:128]), col["p"], A.is_equal)
    vs(b("KSa"), b("IF"), col["g15"], A.is_equal)
    vs(b("KS8"), b("IF"), col["p15"], A.is_equal)

    def times(out, i, c):
        either(PAR["cst"], lambda: vs(out, i, c, A.mult), lambda: act(out, i, F.Copy, scale=c))
    times(b("KS0"), b("KSa"), col["q0"])
    at("ek")
    for k in range(16):
        times(b("EK", S_[128 * k:128 * k + 128]), b("Blk"), b("km", S_[k:k + 1]))
    at("cst")
    for n, c in (("I16", 16.0), ("I256", 256.0), ("I5", 1.0 / 32), ("nIU", -U), ("nI", -1.0), ("I32", 1.0), ("nI32", -1.0)):
        times(b(n), b("I"), c)
    for h in H:
        at("paz")
        zs = [b("PA", S_[120 * h + 64 - 8 * PAR["prod"]:120 * h + (64 if PAR["round"][h] == "s" else 120)])] if PAR["prod"] or PAR["round"][h] != "s" else []
        if PAR["round"][h] == "s":
            zs.append(b("PW", S_[56 * h:56 * h + 56], S_[16:32]))
        for z in zs:
            if PAR["pz"] == "g":
                iota(z, [[0, len(cols(z)[0])]], 0, 0)
            else:
                ms(z, 0.0)
    at("cst")
    ms(b("cm", S_[0:16], S_[16:24]), 0.0)
    vs(b("twice0"), b("JG", S_[0:128:8]), col["g"], A.is_equal, col["q0"], A.mult)
    for n, c in (("Blk8", 1.0), ("B816", 16.0), ("B8n32", -32.0)):
        vs(b(n), b("IF", S_[0:8]), col["g"], A.is_equal, c, A.mult)
    vs(b("rst"), b("JM"), 0.0, A.is_gt)
    ms(b("zer"), 0.0)
    ms(b("one32"), 1.0)
    ms(b("thr", S_[0:1]), 1.0)
    ms(b("O", S_[2048:2304]), 0.0)
    vs(b("tri"), b("JM"), col["q"], A.is_gt)
    for h in H:
        times(lanes("BlkV", h), b("Blk"), 16.0)
        for j in range(4 - PAR["far"][h], 4):
            ms(b("BlkV", S_[128 * h + j:128 * h + 128:4]), 0.0)
    iota(b("run"), [[1, 256]], 2048, 0)
    vs(b("mxB"), b("JM"), col["q"], A.is_equal)
    vt(b("dumG"), b("run"), b("mxB"), A.mult)
    times(b("BlkU"), b("Blk"), U)
    vs(b("vW", S_[0:16]), b("IF", S_[0:16]), 128.0, A.mult, col["q8"], A.add)
    for t in (1, 2):
        vs(b("vW", S_[16 * t:16 * t + 16]), b("vW", S_[0:16]), float(t), A.add)
    for n, who in zip(("tabA", "tabB"), PAR["junk"]):
        at(n)
        for j in range(2):
            z = S_[1024 * j:1024 * j + 1024]
            if who[j] == "s":
                act(b(n, z), b("holI", S_[0:1024]))
            elif who[j] == "v":
                ms(b(n, z), 0.0)
            else:
                iota(b(n, z), [[0, 1024]], 0, 0)

    def table(d, t):
        at("")
        dma(bp(TAB[d], S_[0:128:16], full), b("la%d" % d), 2.0)
        for r in range(t):
            at("upd", 2 if r < t - 1 else HOPS[t].index(d))
            gath(PAR["small"], b(TAB[d], S_[r:2048:8]), b("ID", full), b("lb%d%d" % (r, d)))
    dma(bp("C8", S_[0:8], full), b("rawh"), PAR["late"])
    dma(bp("ycS", S_[0:128:16], full), b("rawf"), 2.0)
    gr = group()
    at("off")
    mm(b("k0", S_[0:4]), b("I"), lanes("zer", 0), gr)
    for q in range(16):
        for e in range(8):
            mm(b("k0", S_[e // 4:4:2], S_[8 * (e % 4):8 * (e % 4) + 8]), bp("KS8", S_[0:8], S_[15 - q:143 - q]), bp("C8", S_[0:8], full, 8 * q + e), gr)
    vc(b("off0"), b("k0", S_[0:4]))
    at("conv")
    for j in range(4):
        move(b("O", S_[512 * j:512 * j + 512]), b("holI", S_[512 * j:512 * j + 512]), e=PAR["conv"])

    def wrap(out, src, gr):
        for q in range(16):
            mm(out, b("KSa", S_[15 - q:143 - q]), b(src, S_[q:256:16]), gr)

    def chase(t):
        s, u = HOPS[t]
        if t == 1:
            at("upd", 0)
            gath(PAR["small"], b(TAB[s], S_[0:2048:8]), b("ID", full), b("lb0%d" % s))
        else:
            table(s, t)
        table(u, t)

        def pieces(who, out, tab, off, h):
            w = 128 // len(who)
            for j, e in enumerate(who):
                if j * w // 64 == h:
                    gath(e, b(out, S_[16 * w * j:16 * w * (j + 1)]), b(tab, full), b(off, S_[w * j:w * (j + 1)]))
        for h in H:
            at("c1", h)
            pieces(PAR["c1" if t else "c10"], "T1", TAB[s], "off0", h)
            bk, gr = b("k%d" % h, S_[0:2]), group()
            at("c2", h)
            for q in range(16):
                o = 1024 * h + 128 * (q % 8) + q // 8
                mm(bk, b("KS0", S_[15 - q:143 - q]), b("T1", S_[o:o + 127:2]), gr)
            move(b("off1", S_[64 * h:64 * h + 64]), bk, e=PAR["u16"][0])
            pieces(PAR["c2" if t else "c20"], "DT", TAB[u], "off1", h)
        at("")

    feed = [0]

    def sbank(among="01"):
        feed[0] += 1
        return "k" + among[feed[0] % len(among)]

    def block(n, h, j):
        return b(n, S_[2048 * h + j:2048 * h + 2048:4])

    def done(n, h, j):
        return b(n, S_[2048 * h + 512 * j:2048 * h + 512 * j + 512])

    def row(n, h, k):
        return b(n, S_[2048 * h + k:2048 * h + 2048:16])

    def drow(n, h, k):
        o = 2048 * h + 512 * (k % 4)
        return b(n, S_[o + k // 4:o + 512:4])

    def four(h, src):
        for u in range(4):
            mm(b("k%d" % (2 + h), full, S_[u::4]), b("I"), src)

    def top(h):
        K = "k%d" % (6 + h)
        back = slice(128 * h + 127, 128 * h - 1 if h else None, -1)
        scan(lanes("run", h), lanes("rst", 0), b(K, S_[0:128]), A.mult, A.max)
        scan(b("mxB", back), lanes("rst", 0), b("run", back), A.mult, A.max)
        vt(lanes("hotL", h), lanes("mxB", h), b(K, S_[0:128]), A.is_equal)
        mm(b(K, S_[128:256]), lanes("hotL", h), b("I"))
        return b(K, S_[128:256])

    chase(0)
    for t in range(RO):
        haste[2] = t + 1
        src = "O" if t else "holI"
        Ot = b("O", S_[t:2048:8])
        nk, VV = PAR["sk"], "VV%d" % (t % 2)
        at("vv", t)
        for j in range(4):
            iota(b(VV, S_[1024 * j:1024 * j + 1024]), [[8, 64], [0, 16]], t + 512 * j, 0)
            if t == 2:
                ops[-1]["after"] = (quiet,)
        for h in H:
            at("gx", h)
            vc(lanes("a16", h), b(src, S_[1024 * h + t:1024 * h + 1024:8]))
        for n, w, key in (("xk", "X", "gx"), ("dR", "DT", "gd")):
            who = PAR[key if t else key + "0"]
            c = 256 // len(who)
            for j, e in enumerate(who):
                at(key, j * c // 128)
                gath(e, b(n, S_[16 * c * j:16 * c * (j + 1)]), b(w, full), b("a16", S_[c * j:c * (j + 1)]))
        if t:
            sellers()
        for j in range(nk):
            w = 4096 // nk
            at("sk", 2 * j // nk)
            vt(b("sk", S_[w * j:w * j + w]), ind(b(src, S_[0:2048]), b("a16", S_[w // 16 * j:w // 16 * (j + 1)])), b(VV, S_[w * j:w * j + w]), A.is_equal)
        at("ad")
        move(b("aD"), Ot, -2048.0)
        for h in H:
            Ah, Kh = "k%d" % (4 + h), "k%d" % (6 + h)
            at("min", h)
            four(h, b("X", S_[1024 * h + t:1024 * h + 1024:8]))
            for j in range(4):
                vt(done("mR", h, j), block("xk", h, j), b("k%d" % (2 + h)), A.min)
            for k in range(16):
                at("c", h)
                mm(b(Ah, S_[0:8], S_[k::16]), row("dR", h, k), b("twice0"))
                at("m", h)
                mm(b(Ah, S_[8:16], k), drow("mR", h, k), b("Blk8"))
            nv = 4 - PAR["far"][h]
            at("sx", h)
            if nv:
                for k in range(16):
                    mm(b("k%d" % h, S_[0:4], S_[k::16]), row("xk", h, k), b("Blk8" if k % 4 < nv else "zer", S_[0:8]))
                move(lanes("sx", h), b("k%d" % h, S_[0:4]))
            zm = S_[8 * h:8 * h + 8]
            at("c", h)
            move(lanes("cS", h), b(Ah, S_[0:8], S_[0:16]))
            at("m", h)
            move(b("cm", zm, S_[0:16]), b(Ah, S_[8:16], S_[0:16]))
            at("ck", h)
            mm(b(Kh, S_[128:256]), lanes("cS", h), b("I"))
            move(lanes("cK", h), b(Kh, S_[128:256]))
            key, gr = b(Kh, S_[0:128]), group()
            mm(key, b("I"), b("k15"), gr)
            mm(key, b("I16"), b("cm", zm, S_[0:16]), gr)

            ns = 8 - PAR["prod"]
            for s in range(1, 9):
                z = S_[64 * h + 8 * s - 8:64 * h + 8 * s]
                at("eq", h)
                vt(b("EQ", z), lanes("cS", h), b(Ah, S_[0:8], S_[s:s + 16]), A.is_equal)
                at("pa", h)
                for far, lo, n in ((s, 0, 16 - s), (16 - s, 16 - s, s)) if s < 8 else ((s, 0, 8),):
                    if far <= ns or (far > 8 and PAR["round"][h] == "s"):
                        continue
                    y = S_[120 * h + 8 * far - 8:120 * h + 8 * far]
                    vt(b("PA", y, S_[0:n]), b("EQ", z, S_[lo:lo + n]), b(Ah, S_[8:16], S_[far:16]), A.mult)
                    mm(key, b("I16"), b("PA", y), gr)
            at("pb", h)
            for c in range(0, ns, 4):
                bank, part = sbank(PAR["fp"][h]), range(c + 1, min(c + 4, ns) + 1)
                for j, s in enumerate(part):
                    z, o, g2 = S_[8 * (j // 2):8 * (j // 2) + 8], 16 * (j % 2), group()
                    mm(b(bank, z, S_[o:o + 16]), b("I"), b("cm", zm, S_[s:s + 16]), g2)
                    mm(b(bank, z, S_[o:o + 16]), b("I256"), b("EQ", S_[64 * h + 8 * s - 8:64 * h + 8 * s]), g2)
                r0, m = 32 * h + 4 * c, len(part)
                if m == 3:
                    mm(b(bank, S_[8:16], S_[16:32]), b("I"), b("zer", S_[0:128]))
                nr, nc = (16 if m > 2 else 8), (32 if m > 1 else 16)
                move(b("PB", S_[r0:r0 + nr], S_[0:nc]), b(bank, S_[0:nr], S_[0:nc]), -256.0, True, PAR["pb"])
                for j, s in enumerate(part):
                    mm(key, b("I16"), b("PB", S_[r0 + 8 * (j // 2):r0 + 8 * (j // 2) + 8], S_[16 * (j % 2):16 * (j % 2) + 16]), gr)
            if PAR["round"][h] == "s":
                bank = sbank(PAR["fp"][h])
                at("pw", h)
                for s in range(1, 8):
                    g2 = group()
                    mm(b(bank, S_[2 * s - 2:2 * s]), b("I"), b("cm", zm, S_[8:16]), g2)
                    mm(b(bank, S_[2 * s - 2:2 * s]), b("I256"), b("EQ", S_[64 * h + 8 * s - 8:64 * h + 8 * s], S_[8:16]), g2)
                move(b("PW", S_[56 * h:56 * h + 56], S_[8:16]), b(bank, S_[0:14]), -256.0, True, PAR["pb"])
                for s in range(1, 8):
                    mm(key, b("I16"), b("PW", S_[56 * h + 8 * s - 8:56 * h + 8 * s], S_[16 - s:32 - s]), gr)
        for h in H:
            Kh = "k%d" % (6 + h)
            at("top", h)
            vt(lanes("ohc", h), lanes("cK", h), top(h), A.mult)
            mm(b(Kh, S_[256:384]), b("Blk"), lanes("ohc", h))
            vt(lanes("mine", h), lanes("cK", h), b(Kh, S_[256:384]), A.is_equal)
            if PAR["win"][h]:
                act(lanes("w1", h), lanes("mine", h), scale=2.0, bias=-1.0)
            bW, gr, z = b(Kh, S_[384:392]), group(), S_[8 * h:8 * h + 8]
            at("xb", h)
            for q in range(16):
                mm(bW, b("KSa", S_[15 - q:143 - q]), b("ohc", S_[128 * h + q:128 * h + 128:16]), gr)
            move(b("bo", z), bW, e=PAR["u16"][1])
            gath(PAR["small"], lanes("xb", h), b("X", full), b("bo", z))
            at("dbv")
            vt(b("dbv", z), bW, b("vW", S_[16 * t + 8 * h:16 * t + 8 * h + 8]), A.subtract)
        vW = b("vW", S_[16 * t:16 * t + 16])
        for h in H:
            Ah = "k%d" % (4 + h)
            at("st", h)
            for k in range(16):
                mm(b("k7", S_[256 * h + k:256 * h + 128:16]), row("sk", h, k), b("Blk8"))
            under(lanes("st", h), b("k7", S_[256 * h:256 * h + 128]), 0.5)
            at("win", h)
            for j in range(4):
                if j < PAR["win"][h]:
                    bank = "k%d" % (2 + j % 2)
                    for u in range(4):
                        k = j + 4 * u
                        mm(b(bank, full, S_[u::4]), b("EK", S_[128 * k:128 * k + 128]), lanes("w1", h))
                    vt(done("pR", h, j), block("xk", h, j), b(bank), A.mult)
                else:
                    bank, gr = sbank(PAR["fw"][h]), group()
                    mm(b(bank), b("I5"), block("xk", h, j), gr)
                    for u in range(4):
                        k = j + 4 * u
                        mm(b(bank, full, S_[u::4]), b("EK", S_[128 * k:128 * k + 128]), lanes("mine", h), gr)
                    act(done("pR", h, j), b(bank), F.Abs, scale=32.0, bias=-16.0)
            gr = group()
            at("sum", h)
            for k in range(16):
                kk = 4 * (k % 4) + k // 4
                mm(b(Ah, S_[0:4]), b("I"), drow("pR", h, kk), gr)
            act(lanes("gt", h), b(Ah, S_[0:4]), F.Sign, bias=-64.0 * (4 - PAR["win"][h]) - 0.5)
            at("wl", h)
            mm(b(Ah, S_[4:8]), lanes("gt", h), b("Blk"))
            under(lanes("wl", h), b(Ah, S_[4:8]), b("thr", S_[t:t + 1]))
        cW, nW = b("k4", 12, S_[0:16]), b("nW", S_[16 * t:16 * t + 16])
        at("new")
        wrap(cW, "gt", group())
        vs(b("winW"), cW, b("thr", S_[t:t + 1]), A.is_gt)
        vt(b("tw"), b("winW"), b("dbv"), A.mult)
        vt(b("nw"), b("tw"), vW, A.add)
        vc(nW, b("nw"))
        at("yc")
        gath(PAR["small"], b("ycS", S_[t:2048:8]), b("ID", full), nW)
        if t in NEXT:
            ds = NEXT[t]
            for j, part in enumerate((ds[0:1], ds[1:2], ds[2:4])):
                if part:
                    send(nW, [(d, "lb%d%d" % (t, d), "b%d%d" % (t, d)) for d in part], PAR["arr"] + j)
            if t == 0:
                quiet = sent[-1]
            at("own")
            for h in H:
                move(b("off0", S_[64 * h + 8 * t:64 * h + 8 * t + 8]), b("nw", S_[8 * h:8 * h + 8]), e=PAR["u16"][3])
            at("z")
            op("s", lambda: sc.activation(ap(b("cnj")), ap(b("winW")), F.Identity, bias=1.0 / 2048, scale=2.0, accum_out=ap(b("cnw"))),
               [b("winW")], [b("cnj"), b("cnw")], 0.14)
            odd = b("k5", 13, S_[0:1])
            mm(odd, b("one32"), b("cnw"))
            vs(b("cni"), odd, 0.25, A.mult, -0.5, A.add)
            vs(b("thr", S_[t + 1:t + 2]), b("cni"), -4.0, A.mult, odd, A.add)
        gr = group()
        at("key")
        mm(b("k6", S_[0:256]), b("I"), b("kc"), gr)
        for h in H:
            key, nv = lanes("k6", h), 4 - PAR["far"][h]
            if nv:
                at("xb", h)
                four(h, lanes("xb", h))
                at("key")
                mm(key, lanes("xb", h), lanes("BlkV", h), gr)
                mm(key, b("I16"), lanes("sx", h), gr)
            mm(key, lanes("mine", h), b("nIU"), gr)
            mm(key, b("nIU"), lanes("st", h), gr)
            for j in range(4):
                if j < nv:
                    at("far", h)
                    vt(done("mR", h, j), block("xk", h, j), b("k%d" % (2 + h)), A.min)
                else:
                    at("fars", h)
                    bank, g2 = sbank(), group()
                    mm(b(bank), b("I"), block("xk", h, j), g2)
                    for u in range(4):
                        mm(b(bank, full, S_[u::4]), b("nI"), lanes("xb", h), g2)
                    act(done("mR", h, j), b(bank), F.Abs)
            at("key")
            for k in range(16):
                o = b("k6", S_[128 * h + k:128 * h + 128:16])
                mm(o, drow("mR", h, k), b("B8n32" if k % 4 < nv else "B816"), gr)
            mm(key, b("nIU"), lanes("wl", h), gr)
        if t in NEXT:
            chase(t + 1)
        hot = b("k7", S_[0:256])
        at("sold")
        scan(b("run"), b("rst"), b("k6", S_[0:256]), A.mult, A.max)
        scan(b("mxB", S_[::-1]), b("rst"), b("run", S_[::-1]), A.mult, A.max)
        vt(b("hotL"), b("mxB"), b("k6", S_[0:256]), A.is_equal)
        for h in H:
            mm(lanes("k7", h), lanes("hotL", h), b("I"))
        vt(b("ga"), b("aD"), hot, A.mult)
        at("ca")
        vt(b("ca"), b("cK"), hot, A.mult)
        at("sell")
        rest = b("k7", S_[256:512])
        if t in NEXT:
            move(b("hotS"), hot)
        else:
            mm(rest, b("Blk"), b("ohc"))
            move(b("bS"), rest)
            vt(b("sb"), b("bS"), hot, A.mult)
            act(rest, hot, scale=-1.0, bias=1.0)
        gW, gG, cs, vP = b("k3", 0, S_[0:16]), b("k2", S_[0:8]), b("k4", S_[0:8]), b("k5", S_[0:8])
        at("goal")
        mm(gG, b("Blk"), b("ga"))
        wrap(gW, "ga", group())
        move(b("gS"), gG, 2048.0)
        move(b("gw"), gW, 2048.0, e=PAR["gw"])
        at("og")
        move(b("go"), gW, 2048.0, e=PAR["u16"][2])
        gath(PAR["small"], b("OG"), b("O", full), b("go"))
        triP = b("k3", S_[8:16])
        mm(vP, b("I32"), b("vG%d" % t))
        mm(triP, b("I"), b("tri"))
        gr = group()
        mm(cs, b("Blk"), b("ca"), gr)
        mm(cs, b("nI32"), b("OG"), gr)
        gr = group()
        at("dup")
        dup = b("k6", S_[256:512])
        mm(dup, b("I"), b("gS"), gr)
        for c in range(16):
            vs(b("E3", c, S_[0:256 - 16 * c]), b("gS", S_[16 * c:256]), b("gw", S_[c:c + 1]), A.is_equal)
            if c < 15:
                mm(b("k6", S_[16 * c + 272:512]), b("BlkU"), b("E3", c, S_[16:256 - 16 * c]), gr)
        vt(b("E3", full, S_[0:16]), b("E3", full, S_[0:16]), triP, A.mult)
        mm(dup, b("BlkU"), b("E3", full, S_[0:16]), gr)
        vt(b("eqv"), b("OG"), vP, A.is_equal)
        vt(b("tt"), b("eqv"), cs, A.mult)
        vt(b("run"), b("dumG"), dup, A.min)
        scan(b("mxB"), b("rst"), b("run"), A.mult, A.max)
        vc(b("so"), b("mxB", S_[15:256:16]))
        vt(ind(b("O", full), b("so")), b("OG"), b("tt"), A.add)

        def sellers(Ot=Ot):
            P, gr = b("k7", S_[256:512]), group()
            at("sell")
            mm(P, b("Blk"), b("ohc"), gr)
            mm(P, b("nI32"), Ot, gr)
            vt(P, b("hotS"), P, A.mult)
            vt(Ot, Ot, P, A.add)
    vt(rest, Ot, rest, A.mult)
    vt(Ot, b("sb"), rest, A.add)
    dma(("yo", full), b("O", S_[0:2048]), 5.0)
    dma(("yc", full), bp("ycS", S_[0:128:16], full), 2.0)

    if "order" not in _memo:
        _memo["order"] = order(ops)
    cnt, clk, hist, W, R = {}, {q: {} for q in eng}, {}, {}, {}

    def need(q, rd, wr):
        req = {}
        own = "q" + q

        def take(tab, x, skip):
            for s, arr in tab.get(x[0], {}).items():
                if s == own and skip and (q == "p" or skip == 2):
                    continue
                n = int(arr.max() if psum(x) and s != own else arr[cols(x)[0]].max())
                if s == own and skip and n <= cnt[own] - 4:
                    continue
                if n > req.get(s, 0):
                    req[s] = n
        for x in rd:
            take(W, x, False)
            if psum(x):
                take(R, x, 2)
        for x in wr:
            take(W, x, True)
            take(R, x, True)
        return req

    def note(tab, x, s, n):
        d = tab.setdefault(x[0], {})
        if s not in d:
            d[s] = np.zeros(int(np.prod(SCRATCH[x[0]][1][1:])), np.int64)
        d[s][cols(x)[0]] = n

    for i, q in _memo["order"]:
        o = ops[i]
        fn = o["fn"]
        if q:
            req = need(q, o["rd"], o["wr"])
            for s, n in sorted(req.items(), key=lambda z: -len(hist.get(z, ()))):
                if clk[q].get(s, 0) < n:
                    eng[q].wait_ge(T.sem[s], n)
                    clk[q][s] = n
                    for s2, n2 in hist.get((s, n), {}).items():
                        clk[q][s2] = max(clk[q].get(s2, 0), n2)
        if o["sem"] == "":
            fn()
            continue
        s = o["sem"] or "q" + q
        cnt[s] = n = cnt.get(s, 0) + o["amt"]
        if q:
            fn().then_inc(T.sem[s], o["amt"])
            hist[(s, n)] = dict(clk[q])
            if o["sem"] is None:
                hist[(s, n)][s] = n
        for x in o["rd"]:
            note(R, x, s, n)
        for x in o["wr"]:
            note(W, x, s, n)
    for s, n in cnt.items():
        g.wait_ge(T.sem[s], n)
    g.wait_ge(T.sem.ls, nls[0])
